import numpy as np
import ml_dtypes


def mxq(x, axis, fmt="e4m3"):
    dtype, down = {"e4m3": (ml_dtypes.float8_e4m3fn, 7), "e5m2": (ml_dtypes.float8_e5m2, 14)}[fmt]
    v = np.moveaxis(np.asarray(x, np.float32).astype(ml_dtypes.bfloat16).astype(np.float64), axis, -1)
    blocks = v.reshape(v.shape[:-1] + (-1, 32))
    amax = np.abs(blocks).max(-1, keepdims=True)
    byte = np.maximum(np.where(amax > 0, np.frexp(amax)[1] - 1 + 127, 0) - down, 1)
    scale = np.exp2(byte - 127.0)
    codes = (blocks / scale).astype(np.float32).astype(dtype).astype(np.float64)
    return np.moveaxis((codes * scale).reshape(v.shape), -1, axis)


WIDE = False


def mx_kscale(k):
    if not WIDE:
        return np.ones(k)
    levels = np.array([18, -18])
    if k % 512:
        return np.exp2(np.random.permutation(np.resize(levels, k // 32))).repeat(32)
    a = np.empty((k // 512, 16))
    for p in range(k // 512):
        a[p, :8] = np.random.permutation(np.resize(levels, 8))
        for g in range(8):
            far = levels[np.abs(levels - a[p, g]) >= 10]
            a[p, g + 8] = far[np.random.randint(len(far))]
    return np.exp2(a.ravel()).repeat(32)


def f64(x):
    return np.asarray(x).astype(np.float64)


def striped(idx):
    return np.tile(np.asarray(idx).reshape(-1, 16).T, (8, 1)).astype(np.uint16)


def unstriped(offs):
    return offs[:16].T.reshape(-1).astype(np.int64)


B, N, T, D, R = 2, 512, 2048, 512, 512


def setup_inputs():
    n = np.random.standard_normal
    idx = np.random.permutation(T)[:B * N]
    s = mx_kscale(D)[:, None]
    z = mx_kscale(R)[:, None]
    q = n((B, D, R))
    do = n((B, D, R))
    return {
        "qT": (q * s).astype(np.float32),
        "cT": (n((D, T)) * (1.00 / np.sqrt(D)) / s).astype(np.float32),
        "doT": (do * s).astype(np.float32),
        "rw": (np.random.uniform(0.5, 1.5, (B, R, 1)) * 1.0 / np.sqrt(R) * z).astype(np.float32),
        "qm": (q.transpose(0, 2, 1) / z).astype(np.float32),
        "dom": (do.transpose(0, 2, 1) / z).astype(np.float32),
        "offs": striped(idx),
    }


def reference(qT, cT, doT, rw, qm, dom, offs):
    idx = unstriped(offs)
    pick = lambda x: x[:, idx].reshape(x.shape[0], B, N).transpose(1, 0, 2)
    cq = mxq(pick(f64(cT)), 1, "e4m3")
    a = mxq(f64(qT), 1, "e4m3").transpose(0, 2, 1) @ cq
    p = 1.0 / (1.0 + np.exp(-a))
    dp = mxq(f64(doT), 1, "e5m2").transpose(0, 2, 1) @ cq
    ds = f64(rw) * dp * p * (1.0 - p)
    dk = mxq(f64(qm), 1, "e4m3").transpose(0, 2, 1) @ mxq(ds, 1, "e5m2")
    dv = mxq(f64(dom), 1, "e5m2").transpose(0, 2, 1) @ mxq(f64(rw) * p, 1, "e4m3")
    gc = np.zeros((D, T))
    gc[:, idx] = (dk + dv).transpose(1, 0, 2).reshape(D, B * N)
    return gc

@@ -1,0 +1,189 @@
+from contextlib import ExitStack
+
+import concourse.mybir as mybir
+
+B, N, T, D, R = 2, 512, 2048, 512, 512
+FLOPS = 4 * 2 * B * N * D * R
+
+F32 = mybir.dt.float32
+BF16 = mybir.dt.bfloat16
+U32 = mybir.dt.uint32
+U16 = mybir.dt.uint16
+U8 = mybir.dt.uint8
+E4M3 = mybir.dt.float8_e4m3fn_x4
+E5M2 = mybir.dt.float8_e5m2_x4
+ACT = mybir.ActivationFunctionType
+ALU = mybir.AluOpType
+
+P = 128
+PACK = 4
+LIST_COLS = N // 16
+
+
+def tile_attend_gat_sig_c_kernel(tc, qT, cT, doT, rw, qm, dom, offs, out):
+    nc = tc.nc
+
+    with ExitStack() as ctx:
+        keep = ctx.enter_context(tc.tile_pool(name="keep", bufs=1))
+        rawp = ctx.enter_context(tc.tile_pool(name="raw", bufs=6))
+        stage = ctx.enter_context(tc.tile_pool(name="stage", bufs=6))
+        work = ctx.enter_context(tc.tile_pool(name="work", bufs=1))
+        outp = ctx.enter_context(tc.tile_pool(name="outp", bufs=4))
+        psum = ctx.enter_context(tc.psum_pool(name="psum", bufs=8))
+
+        offsets = keep.tile([P, B * LIST_COLS], U16, name="offsets")
+        nc.sync.dma_start(offsets[:], offs)
+        gate = keep.tile([P, B, PACK], F32, name="gate")
+        nc.sync.dma_start(gate[:], rw.rearrange("b (p t) o -> p b (t o)", t=PACK))
+
+        planes = [keep.tile([P, T], F32, name="plane%d" % j) for j in range(PACK)]
+        pool_rows = cT.rearrange("(p j) c -> j p c", j=PACK)
+        for j in range(PACK):
+            nc.sync.dma_start(planes[j][:], pool_rows[j])
+
+        def load(src):
+            raw = rawp.tile([P, PACK, 512], F32, name="raw")
+            nc.sync.dma_start(raw[:], src.rearrange("(p j) c -> p j c", j=PACK))
+            return raw
+
+        windows = [keep.tile([P, T], F32, name="window%d" % k) for k in range(D // P)]
+        for window in windows:
+            nc.vector.memset(window[:], 0.0)
+
+        warm = keep.tile([P, 1], F32, name="warm")
+        nc.scalar.activation(warm[:], gate[:, 0, 0:1], ACT.Sigmoid)
+        neg_gate = keep.tile([P, B, PACK], F32, name="neg_gate")
+        nc.vector.tensor_scalar(neg_gate[:], gate[:], -1.0, None, ALU.mult)
+
+        def move(engine, dst, src):
+            if engine == "V":
+                nc.vector.tensor_copy(dst, src)
+            else:
+                nc.scalar.activation(dst, src, ACT.Copy)
+
+        def grouped_tile():
+            return stage.tile([P, 2048], BF16, name="grouped", align_bytes=64)
+
+        def pairs_out(grouped):
+            return grouped[:].rearrange("p (c e j) -> p c j e", e=2, j=PACK)
+
+        def pairs_in(planar):
+            return planar[:].rearrange("p j (c e) -> p c j e", e=2)
+
+        def operand(name):
+            codes = keep.tile([P, 512], U32, name=name + "_codes", align_bytes=64)
+            scales = keep.tile([P, 512], U8, name=name + "_scales", align_bytes=64)
+            return codes, scales
+
+        def quantize(op, fmt, grouped, lo=0, hi=512):
+            nc.vector.quantize_mx(
+                out=op[0][:, lo:hi].bitcast(fmt), scales=op[1][:, lo:hi], in_=grouped[:, PACK * lo : PACK * hi]
+            )
+
+        def group_plain(engine, planar):
+            grouped = grouped_tile()
+            move(engine, pairs_out(grouped), pairs_in(planar))
+            return grouped
+
+        def group_queries(engine, raw, name, fmt):
+            op = operand(name)
+            grouped = grouped_tile()
+            dst = grouped[:].rearrange("p (h e m j) -> p h m j e", h=2, e=2, j=PACK)
+            src = raw[:].rearrange("p j (m h e) -> p h m j e", h=2, e=2)
+            for h in range(2):
+                move(engine, dst[:, h], src[:, h])
+            for h in range(2):
+                quantize(op, fmt, grouped, 256 * h, 256 * (h + 1))
+            return op
+
+        def product(acc, lhs, lhs_fmt, block, rhs, rhs_fmt, start, stop):
+            cols = slice(P * block, P * (block + 1))
+            nc.tensor.matmul_mx(
+                out=acc[:],
+                lhsT=lhs[0][:, cols].bitcast(lhs_fmt),
+                lhsT_scale=lhs[1][:, cols],
+                rhs=rhs[0][:].bitcast(rhs_fmt),
+                rhs_scale=rhs[1][:],
+                start=start,
+                stop=stop,
+            )
+
+        picked = [keep.tile([P, PACK, N], F32, name="picked%d" % b) for b in range(B)]
+
+        def gather(b):
+            slots = offsets[:, b * LIST_COLS : (b + 1) * LIST_COLS]
+            for j in range(PACK):
+                nc.vector.tensor_copy(picked[b][:, j, :], planes[j][:].indirect(slots))
+
+        def scatter(b, k, dense):
+            slots = offsets[:, b * LIST_COLS : (b + 1) * LIST_COLS]
+            nc.vector.tensor_copy(windows[k][:].indirect(slots), dense[:])
+
+        waiting = []
+        for b in range(B):
+            first = b == 0
+            spare = "V" if first else "S"
+            raw_q = load(qT[b])
+            raw_do = load(doT[b])
+            raw_qm = load(qm[b])
+            raw_dom = load(dom[b])
+
+            if first:
+                gather(0)
+            latents = operand("latents%d" % b)
+            quantize(latents, E4M3, group_plain(spare, picked[b]))
+            if first:
+                gather(1)
+            q_op = group_queries("S", raw_q, "q%d" % b, E4M3)
+            do_op = group_queries(spare, raw_do, "do%d" % b, E5M2)
+
+            prob = work.tile([P, PACK, N], F32, name="prob", bufs=2)
+            neg_pw = work.tile([P, PACK, N], F32, name="neg_pw")
+            slope = work.tile([P, PACK, N], F32, name="slope")
+            for t in range(PACK):
+                score = psum.tile([P, N], F32, name="bank")
+                product(score, q_op, E4M3, t, latents, E4M3, True, True)
+                nc.scalar.activation(prob[:, t, :], score[:], ACT.Sigmoid)
+            for t in range(PACK):
+                dprob = psum.tile([P, N], F32, name="bank")
+                product(dprob, do_op, E5M2, t, latents, E4M3, True, True)
+                if first:
+                    nc.vector.tensor_scalar(neg_pw[:, t, :], prob[:, t, :], neg_gate[:, b, t : t + 1], None, ALU.mult)
+                else:
+                    nc.scalar.activation(neg_pw[:, t, :], prob[:, t, :], ACT.Copy, scale=neg_gate[:, b, t : t + 1])
+                nc.vector.scalar_tensor_tensor(
+                    slope[:, t, :], prob[:, t, :], 1.0, dprob[:], ALU.subtract, ALU.mult
+                )
+            qm_grouped = group_plain("S", raw_qm)
+            ds_grouped = grouped_tile()
+            nc.vector.tensor_tensor(pairs_out(ds_grouped), pairs_in(slope), pairs_in(neg_pw), ALU.mult)
+            pw_grouped = grouped_tile()
+            if first:
+                nc.vector.tensor_scalar(pairs_out(pw_grouped), pairs_in(neg_pw), -1.0, None, ALU.mult)
+            else:
+                nc.scalar.activation(pairs_out(pw_grouped), pairs_in(neg_pw), ACT.Copy, scale=-1.0)
+            dom_grouped = group_plain("S", raw_dom)
+
+            qm_op = operand("qm%d" % b)
+            ds_op = operand("ds%d" % b)
+            pw_op = operand("pw%d" % b)
+            dom_op = operand("dom%d" % b)
+            quantize(qm_op, E4M3, qm_grouped)
+            quantize(ds_op, E5M2, ds_grouped)
+            quantize(dom_op, E5M2, dom_grouped)
+            quantize(pw_op, E4M3, pw_grouped)
+
+            for k, dense in enumerate(waiting):
+                scatter(0, k, dense)
+
+            for k in range(D // P):
+                grad = psum.tile([P, N], F32, name="bank")
+                product(grad, qm_op, E4M3, k, ds_op, E5M2, True, False)
+                product(grad, dom_op, E5M2, k, pw_op, E4M3, False, True)
+                dense = outp.tile([P, N], F32, name="dense")
+                nc.scalar.activation(dense[:], grad[:], ACT.Copy)
+                if first:
+                    waiting.append(dense)
+                else:
+                    scatter(b, k, dense)
+                    nc.sync.dma_start(out[P * k : P * (k + 1), :], windows[k][:])

@@ -7,6 +7,7 @@ FLOPS = 4 * 2 * B * N * D * R
 
 F32 = mybir.dt.float32
 BF16 = mybir.dt.bfloat16
+I32 = mybir.dt.int32
 U32 = mybir.dt.uint32
 U16 = mybir.dt.uint16
 U8 = mybir.dt.uint8
@@ -17,7 +18,23 @@ ALU = mybir.AluOpType
 
 P = 128
 PACK = 4
-LIST_COLS = N // 16
+WIDTH = 512
+SLOTS_PER_COLUMN = 16
+CHUNK = T // 2
+
+WHOLE = slice(0, WIDTH)
+HALVES = (slice(0, WIDTH // 2), slice(WIDTH // 2, WIDTH))
+FORMAT = {"q": E4M3, "latent": E4M3, "do": E5M2, "qm": E4M3, "ds": E5M2, "dom": E5M2, "pw": E4M3}
+
+RAW_BUFFERS = 6
+
+GROUPED_BUFFER = {
+    ("latent", 0): 0, ("qm", 0): 0, ("qm", 1): 0,
+    ("q", 0): 1, ("dom", 0): 1, ("dom", 1): 1,
+    ("do", 0): 2, ("pw", 0): 2, ("pw", 1): 2,
+    ("latent", 1): 3,
+    ("ds", 0): 4, ("q", 1): 4, ("do", 1): 4, ("ds", 1): 4,
+}
 
 
 def tile_attend_gat_sig_c_kernel(tc, qT, cT, doT, rw, qm, dom, offs, out):
@@ -25,165 +42,195 @@ def tile_attend_gat_sig_c_kernel(tc, qT, cT, doT, rw, qm, dom, offs, out):
 
     with ExitStack() as ctx:
         keep = ctx.enter_context(tc.tile_pool(name="keep", bufs=1))
-        rawp = ctx.enter_context(tc.tile_pool(name="raw", bufs=6))
-        stage = ctx.enter_context(tc.tile_pool(name="stage", bufs=6))
-        work = ctx.enter_context(tc.tile_pool(name="work", bufs=1))
-        outp = ctx.enter_context(tc.tile_pool(name="outp", bufs=4))
-        psum = ctx.enter_context(tc.psum_pool(name="psum", bufs=8))
+        reuse = ctx.enter_context(tc.tile_pool(name="reuse", bufs=1))
+        psum = ctx.enter_context(tc.psum_pool(name="psum", bufs=1))
 
-        offsets = keep.tile([P, B * LIST_COLS], U16, name="offsets")
+        def on_scalar(dst, src):
+            nc.scalar.activation(dst, src, ACT.Copy)
+
+        on_vector = nc.vector.tensor_copy
+
+        offsets = keep.tile([P, B * N // SLOTS_PER_COLUMN], U16, name="offsets")
         nc.sync.dma_start(offsets[:], offs)
+
+        pool_rows = cT.rearrange("(p u e) c -> u p e c", u=2, e=2)
+        chunks = [[keep.tile([P, 2, CHUNK], F32, name="chunk%d%d" % (u, h)) for h in range(2)] for u in range(2)]
+        for u in range(2):
+            for h in range(2):
+                nc.sync.dma_start(chunks[u][h][:], pool_rows[u][:, :, CHUNK * h : CHUNK * (h + 1)])
+
         gate = keep.tile([P, B, PACK], F32, name="gate")
         nc.sync.dma_start(gate[:], rw.rearrange("b (p t) o -> p b (t o)", t=PACK))
 
-        planes = [keep.tile([P, T], F32, name="plane%d" % j) for j in range(PACK)]
-        pool_rows = cT.rearrange("(p j) c -> j p c", j=PACK)
-        for j in range(PACK):
-            nc.sync.dma_start(planes[j][:], pool_rows[j])
+        loads = [(name, b, src[b]) for b in range(B) for name, src in (("q", qT), ("do", doT), ("qm", qm), ("dom", dom))]
+        raw = {}
+        for index, (name, b, src) in enumerate(loads):
+            tile = reuse.tile([P, PACK, WIDTH], F32, name="raw%d" % (index % RAW_BUFFERS))
+            nc.sync.dma_start(tile[:], src.rearrange("(p j) c -> p j c", j=PACK))
+            raw[(name, b)] = tile
 
-        def load(src):
-            raw = rawp.tile([P, PACK, 512], F32, name="raw")
-            nc.sync.dma_start(raw[:], src.rearrange("(p j) c -> p j c", j=PACK))
-            return raw
+        warm_up = keep.tile([P, 1], F32, name="warm_up")
+        nc.scalar.activation(warm_up[:], chunks[0][0][:, 0, 0:1], ACT.Sigmoid)
+
+        pairs = [keep.tile([P, T, 2], BF16, name="pairs%d" % u) for u in range(2)]
+        picked = keep.tile([P, 2, B * N], U32, name="picked")
+
+        def pair_up(u):
+            for h in range(2):
+                for part, move in enumerate((on_scalar, on_vector)):
+                    first = CHUNK // 2 * part
+                    src = chunks[u][h][:, :, first : first + CHUNK // 2]
+                    dst = pairs[u][:, CHUNK * h + first : CHUNK * h + first + CHUNK // 2, :]
+                    move(dst.rearrange("p (c f) e -> p c e f", f=4), src.rearrange("p e (c f) -> p c e f", f=4))
+
+        def list_columns(first_slot, count):
+            return offsets[:, first_slot // SLOTS_PER_COLUMN : (first_slot + count) // SLOTS_PER_COLUMN]
+
+        def gather(u, first_slot, count):
+            words = pairs[u][:].rearrange("p c e -> p (c e)").bitcast(U32)
+            nc.vector.tensor_copy(
+                picked[:, u, first_slot : first_slot + count], words.indirect(list_columns(first_slot, count))
+            )
+
+        pair_up(0)
+        gather(0, 0, B * N)
+        pair_up(1)
+        for b in range(B):
+            gather(1, N * b, N)
 
         windows = [keep.tile([P, T], F32, name="window%d" % k) for k in range(D // P)]
         for window in windows:
-            nc.vector.memset(window[:], 0.0)
-
-        warm = keep.tile([P, 1], F32, name="warm")
-        nc.scalar.activation(warm[:], gate[:, 0, 0:1], ACT.Sigmoid)
+            nc.vector.memset(window[:].bitcast(I32), 0)
         neg_gate = keep.tile([P, B, PACK], F32, name="neg_gate")
         nc.vector.tensor_scalar(neg_gate[:], gate[:], -1.0, None, ALU.mult)
 
-        def move(engine, dst, src):
-            if engine == "V":
-                nc.vector.tensor_copy(dst, src)
-            else:
-                nc.scalar.activation(dst, src, ACT.Copy)
+        grouped = {}
+        codes = {}
+        scales = {}
 
-        def grouped_tile():
-            return stage.tile([P, 2048], BF16, name="grouped", align_bytes=64)
+        def new_operand(name, b):
+            buffer_name = "grouped%d" % GROUPED_BUFFER[(name, b)]
+            grouped[(name, b)] = reuse.tile([P, WIDTH * PACK], BF16, name=buffer_name, align_bytes=64)
+            codes[(name, b)] = keep.tile([P, WIDTH], U32, name="%s%d_codes" % (name, b), align_bytes=64)
+            scales[(name, b)] = keep.tile([P, WIDTH], U8, name="%s%d_scales" % (name, b), align_bytes=64)
 
-        def pairs_out(grouped):
-            return grouped[:].rearrange("p (c e j) -> p c j e", e=2, j=PACK)
+        def grouped_columns(name, b, cols):
+            return grouped[(name, b)][:, PACK * cols.start : PACK * cols.stop]
 
-        def pairs_in(planar):
-            return planar[:].rearrange("p j (c e) -> p c j e", e=2)
+        def as_grouped(name, b, cols):
+            return grouped_columns(name, b, cols).rearrange("p (c e j) -> p c j e", e=2, j=PACK)
 
-        def operand(name):
-            codes = keep.tile([P, 512], U32, name=name + "_codes", align_bytes=64)
-            scales = keep.tile([P, 512], U8, name=name + "_scales", align_bytes=64)
-            return codes, scales
+        def as_planar(tile, cols):
+            return tile[:, :, cols].rearrange("p j (c e) -> p c j e", e=2)
 
-        def quantize(op, fmt, grouped, lo=0, hi=512):
-            nc.vector.quantize_mx(
-                out=op[0][:, lo:hi].bitcast(fmt), scales=op[1][:, lo:hi], in_=grouped[:, PACK * lo : PACK * hi]
+        def group_latents(b, cols, move):
+            src = picked[:, :, N * b + cols.start : N * b + cols.stop].bitcast(BF16)
+            move(
+                grouped_columns("latent", b, cols).rearrange("p (c u e) -> p c u e", u=2, e=2),
+                src.rearrange("p u (c e) -> p c u e", e=2),
             )
 
-        def group_plain(engine, planar):
-            grouped = grouped_tile()
-            move(engine, pairs_out(grouped), pairs_in(planar))
-            return grouped
+        def group_queries(name, b, moves):
+            dst = grouped[(name, b)][:].rearrange("p (h e m j) -> p h m j e", h=2, e=2, j=PACK)
+            src = raw[(name, b)][:].rearrange("p j (m h e) -> p h m j e", h=2, e=2)
+            for h, move in enumerate(moves):
+                move(dst[:, h], src[:, h])
 
-        def group_queries(engine, raw, name, fmt):
-            op = operand(name)
-            grouped = grouped_tile()
-            dst = grouped[:].rearrange("p (h e m j) -> p h m j e", h=2, e=2, j=PACK)
-            src = raw[:].rearrange("p j (m h e) -> p h m j e", h=2, e=2)
-            for h in range(2):
-                move(engine, dst[:, h], src[:, h])
-            for h in range(2):
-                quantize(op, fmt, grouped, 256 * h, 256 * (h + 1))
-            return op
+        def quantize(name, b, cols):
+            nc.vector.quantize_mx(
+                out=codes[(name, b)][:, cols].bitcast(FORMAT[name]),
+                scales=scales[(name, b)][:, cols],
+                in_=grouped_columns(name, b, cols),
+            )
 
-        def product(acc, lhs, lhs_fmt, block, rhs, rhs_fmt, start, stop):
+        def product(bank, stationary, block, moving, b, start, stop):
             cols = slice(P * block, P * (block + 1))
             nc.tensor.matmul_mx(
-                out=acc[:],
-                lhsT=lhs[0][:, cols].bitcast(lhs_fmt),
-                lhsT_scale=lhs[1][:, cols],
-                rhs=rhs[0][:].bitcast(rhs_fmt),
-                rhs_scale=rhs[1][:],
+                out=bank[:],
+                lhsT=codes[(stationary, b)][:, cols].bitcast(FORMAT[stationary]),
+                lhsT_scale=scales[(stationary, b)][:, cols],
+                rhs=codes[(moving, b)][:].bitcast(FORMAT[moving]),
+                rhs_scale=scales[(moving, b)][:],
                 start=start,
                 stop=stop,
             )
 
-        picked = [keep.tile([P, PACK, N], F32, name="picked%d" % b) for b in range(B)]
-
-        def gather(b):
-            slots = offsets[:, b * LIST_COLS : (b + 1) * LIST_COLS]
-            for j in range(PACK):
-                nc.vector.tensor_copy(picked[b][:, j, :], planes[j][:].indirect(slots))
-
-        def scatter(b, k, dense):
-            slots = offsets[:, b * LIST_COLS : (b + 1) * LIST_COLS]
-            nc.vector.tensor_copy(windows[k][:].indirect(slots), dense[:])
-
-        waiting = []
-        for b in range(B):
-            first = b == 0
-            spare = "V" if first else "S"
-            raw_q = load(qT[b])
-            raw_do = load(doT[b])
-            raw_qm = load(qm[b])
-            raw_dom = load(dom[b])
-
-            if first:
-                gather(0)
-            latents = operand("latents%d" % b)
-            quantize(latents, E4M3, group_plain(spare, picked[b]))
-            if first:
-                gather(1)
-            q_op = group_queries("S", raw_q, "q%d" % b, E4M3)
-            do_op = group_queries(spare, raw_do, "do%d" % b, E5M2)
-
-            prob = work.tile([P, PACK, N], F32, name="prob", bufs=2)
-            neg_pw = work.tile([P, PACK, N], F32, name="neg_pw")
-            slope = work.tile([P, PACK, N], F32, name="slope")
+        def weights(b):
+            prob = reuse.tile([P, PACK, N], F32, name="prob")
+            neg_pw = reuse.tile([P, PACK, N], F32, name="neg_pw")
+            slope = reuse.tile([P, PACK, N], F32, name="slope")
             for t in range(PACK):
-                score = psum.tile([P, N], F32, name="bank")
-                product(score, q_op, E4M3, t, latents, E4M3, True, True)
+                score = psum.tile([P, N], F32, name="score_bank%d" % t)
+                product(score, "q", t, "latent", b, True, True)
                 nc.scalar.activation(prob[:, t, :], score[:], ACT.Sigmoid)
             for t in range(PACK):
-                dprob = psum.tile([P, N], F32, name="bank")
-                product(dprob, do_op, E5M2, t, latents, E4M3, True, True)
-                if first:
-                    nc.vector.tensor_scalar(neg_pw[:, t, :], prob[:, t, :], neg_gate[:, b, t : t + 1], None, ALU.mult)
-                else:
-                    nc.scalar.activation(neg_pw[:, t, :], prob[:, t, :], ACT.Copy, scale=neg_gate[:, b, t : t + 1])
-                nc.vector.scalar_tensor_tensor(
-                    slope[:, t, :], prob[:, t, :], 1.0, dprob[:], ALU.subtract, ALU.mult
+                dprob = psum.tile([P, N], F32, name="shared_bank%d" % t)
+                product(dprob, "do", t, "latent", b, True, True)
+                nc.scalar.activation(neg_pw[:, t, :], prob[:, t, :], ACT.Copy, scale=neg_gate[:, b, t : t + 1])
+                nc.vector.scalar_tensor_tensor(slope[:, t, :], prob[:, t, :], 1.0, dprob[:], ALU.subtract, ALU.mult)
+            return neg_pw, slope
+
+        def group_weights(b, neg_pw, slope, parts):
+            new_operand("ds", b)
+            new_operand("pw", b)
+            for cols in parts:
+                nc.vector.tensor_tensor(
+                    as_grouped("ds", b, cols), as_planar(slope, cols), as_planar(neg_pw, cols), ALU.mult
                 )
-            qm_grouped = group_plain("S", raw_qm)
-            ds_grouped = grouped_tile()
-            nc.vector.tensor_tensor(pairs_out(ds_grouped), pairs_in(slope), pairs_in(neg_pw), ALU.mult)
-            pw_grouped = grouped_tile()
-            if first:
-                nc.vector.tensor_scalar(pairs_out(pw_grouped), pairs_in(neg_pw), -1.0, None, ALU.mult)
-            else:
-                nc.scalar.activation(pairs_out(pw_grouped), pairs_in(neg_pw), ACT.Copy, scale=-1.0)
-            dom_grouped = group_plain("S", raw_dom)
+                nc.scalar.activation(as_grouped("pw", b, cols), as_planar(neg_pw, cols), ACT.Copy, scale=-1.0)
 
-            qm_op = operand("qm%d" % b)
-            ds_op = operand("ds%d" % b)
-            pw_op = operand("pw%d" % b)
-            dom_op = operand("dom%d" % b)
-            quantize(qm_op, E4M3, qm_grouped)
-            quantize(ds_op, E5M2, ds_grouped)
-            quantize(dom_op, E5M2, dom_grouped)
-            quantize(pw_op, E4M3, pw_grouped)
+        def gradient(b, k):
+            bank = psum.tile([P, N], F32, name="shared_bank%d" % k)
+            product(bank, "qm", k, "ds", b, True, False)
+            product(bank, "dom", k, "pw", b, False, True)
+            dense = reuse.tile([P, N], F32, name="dense%d" % k)
+            on_scalar(dense[:], bank[:])
+            nc.vector.tensor_copy(windows[k][:].indirect(list_columns(N * b, N)), dense[:])
 
-            for k, dense in enumerate(waiting):
-                scatter(0, k, dense)
+        for name in ("latent", "q", "do"):
+            new_operand(name, 0)
+        group_latents(0, HALVES[0], nc.scalar.copy)
+        group_latents(0, HALVES[1], on_vector)
+        group_queries("q", 0, (on_vector, on_scalar))
+        group_queries("do", 0, (on_scalar, on_vector))
+        quantize("latent", 0, WHOLE)
+        for name in ("q", "do"):
+            for cols in HALVES:
+                quantize(name, 0, cols)
+        neg_pw, slope = weights(0)
 
-            for k in range(D // P):
-                grad = psum.tile([P, N], F32, name="bank")
-                product(grad, qm_op, E4M3, k, ds_op, E5M2, True, False)
-                product(grad, dom_op, E5M2, k, pw_op, E4M3, False, True)
-                dense = outp.tile([P, N], F32, name="dense")
-                nc.scalar.activation(dense[:], grad[:], ACT.Copy)
-                if first:
-                    waiting.append(dense)
-                else:
-                    scatter(b, k, dense)
-                    nc.sync.dma_start(out[P * k : P * (k + 1), :], windows[k][:])
+        new_operand("latent", 1)
+        group_latents(1, WHOLE, nc.scalar.copy)
+        quantize("latent", 1, WHOLE)
+
+        group_weights(0, neg_pw, slope, HALVES)
+        for name in ("qm", "dom"):
+            new_operand(name, 0)
+            for cols, move in zip(HALVES, (on_vector, on_scalar)):
+                move(as_grouped(name, 0, cols), as_planar(raw[(name, 0)], cols))
+                quantize(name, 0, cols)
+        quantize("ds", 0, WHOLE)
+        quantize("pw", 0, WHOLE)
+
+        new_operand("q", 1)
+        group_queries("q", 1, (on_scalar, on_vector))
+        quantize("q", 1, WHOLE)
+        gradient(0, 0)
+        gradient(0, 1)
+        new_operand("do", 1)
+        group_queries("do", 1, (on_scalar, on_scalar))
+        quantize("do", 1, WHOLE)
+        gradient(0, 2)
+        neg_pw, slope = weights(1)
+        group_weights(1, neg_pw, slope, (WHOLE,))
+        for name in ("qm", "dom"):
+            new_operand(name, 1)
+            on_scalar(as_grouped(name, 1, WHOLE), as_planar(raw[(name, 1)], WHOLE))
+            quantize(name, 1, WHOLE)
+        quantize("ds", 1, WHOLE)
+        quantize("pw", 1, WHOLE)
+        gradient(0, 3)
+
+        for k in range(D // P):
+            gradient(1, k)
+            nc.sync.dma_start(out[P * k : P * (k + 1), :], windows[k][:])

@@ -26,15 +26,9 @@ WHOLE = slice(0, WIDTH)
 HALVES = (slice(0, WIDTH // 2), slice(WIDTH // 2, WIDTH))
 FORMAT = {"q": E4M3, "latent": E4M3, "do": E5M2, "qm": E4M3, "ds": E5M2, "dom": E5M2, "pw": E4M3}
 
-RAW_BUFFERS = 6
-
-GROUPED_BUFFER = {
-    ("latent", 0): 0, ("qm", 0): 0, ("qm", 1): 0,
-    ("q", 0): 1, ("dom", 0): 1, ("dom", 1): 1,
-    ("do", 0): 2, ("pw", 0): 2, ("pw", 1): 2,
-    ("latent", 1): 3,
-    ("ds", 0): 4, ("q", 1): 4, ("do", 1): 4, ("ds", 1): 4,
-}
+LAST_CHUNK_ON_VECTOR = 704
+GROUPED_BUFFERS = 8
+PSUM_BANKS = 8
 
 
 def tile_attend_gat_sig_c_kernel(tc, qT, cT, doT, rw, qm, dom, offs, out):
@@ -43,7 +37,8 @@ def tile_attend_gat_sig_c_kernel(tc, qT, cT, doT, rw, qm, dom, offs, out):
     with ExitStack() as ctx:
         keep = ctx.enter_context(tc.tile_pool(name="keep", bufs=1))
         reuse = ctx.enter_context(tc.tile_pool(name="reuse", bufs=1))
-        psum = ctx.enter_context(tc.psum_pool(name="psum", bufs=1))
+        ring = ctx.enter_context(tc.tile_pool(name="ring", bufs=GROUPED_BUFFERS))
+        psum = ctx.enter_context(tc.psum_pool(name="psum", bufs=PSUM_BANKS))
 
         def on_scalar(dst, src):
             nc.scalar.activation(dst, src, ACT.Copy)
@@ -54,34 +49,35 @@ def tile_attend_gat_sig_c_kernel(tc, qT, cT, doT, rw, qm, dom, offs, out):
         nc.sync.dma_start(offsets[:], offs)
 
         pool_rows = cT.rearrange("(p u e) c -> u p e c", u=2, e=2)
-        chunks = [[keep.tile([P, 2, CHUNK], F32, name="chunk%d%d" % (u, h)) for h in range(2)] for u in range(2)]
+        chunks = [[reuse.tile([P, 2, CHUNK], F32, name="raw%d" % (4 + 2 * u + h)) for h in range(2)] for u in range(2)]
         for u in range(2):
             for h in range(2):
-                nc.sync.dma_start(chunks[u][h][:], pool_rows[u][:, :, CHUNK * h : CHUNK * (h + 1)])
-
-        gate = keep.tile([P, B, PACK], F32, name="gate")
-        nc.sync.dma_start(gate[:], rw.rearrange("b (p t) o -> p b (t o)", t=PACK))
+                pieces = 2 if (u, h) == (1, 1) else 1
+                for piece in range(pieces):
+                    cols = slice(CHUNK // pieces * piece, CHUNK // pieces * (piece + 1))
+                    nc.sync.dma_start(chunks[u][h][:, :, cols], pool_rows[u][:, :, CHUNK * h + cols.start : CHUNK * h + cols.stop])
 
         loads = [(name, b, src[b]) for b in range(B) for name, src in (("q", qT), ("do", doT), ("qm", qm), ("dom", dom))]
         raw = {}
         for index, (name, b, src) in enumerate(loads):
-            tile = reuse.tile([P, PACK, WIDTH], F32, name="raw%d" % (index % RAW_BUFFERS))
+            tile = reuse.tile([P, PACK, WIDTH], F32, name="raw%d" % index)
             nc.sync.dma_start(tile[:], src.rearrange("(p j) c -> p j c", j=PACK))
             raw[(name, b)] = tile
+            if (name, b) == ("do", 0):
+                gate = keep.tile([P, B, PACK], F32, name="gate")
+                nc.sync.dma_start(gate[:], rw.rearrange("b (p t) o -> p b (t o)", t=PACK))
 
         warm_up = keep.tile([P, 1], F32, name="warm_up")
         nc.scalar.activation(warm_up[:], chunks[0][0][:, 0, 0:1], ACT.Sigmoid)
 
         pairs = [keep.tile([P, T, 2], BF16, name="pairs%d" % u) for u in range(2)]
-        picked = keep.tile([P, 2, B * N], U32, name="picked")
+        picked_row = keep.tile([P, 2 * B * N], U32, name="picked", align_bytes=64)
+        picked = picked_row[:].rearrange("p (u c) -> p u c", u=2)
 
-        def pair_up(u):
-            for h in range(2):
-                for part, move in enumerate((on_scalar, on_vector)):
-                    first = CHUNK // 2 * part
-                    src = chunks[u][h][:, :, first : first + CHUNK // 2]
-                    dst = pairs[u][:, CHUNK * h + first : CHUNK * h + first + CHUNK // 2, :]
-                    move(dst.rearrange("p (c f) e -> p c e f", f=4), src.rearrange("p e (c f) -> p c e f", f=4))
+        def pair_up(u, h, first, stop, move):
+            src = chunks[u][h][:, :, first:stop]
+            dst = pairs[u][:, CHUNK * h + first : CHUNK * h + stop, :]
+            move(dst.rearrange("p (c f) e -> p c e f", f=4), src.rearrange("p e (c f) -> p c e f", f=4))
 
         def list_columns(first_slot, count):
             return offsets[:, first_slot // SLOTS_PER_COLUMN : (first_slot + count) // SLOTS_PER_COLUMN]
@@ -92,11 +88,15 @@ def tile_attend_gat_sig_c_kernel(tc, qT, cT, doT, rw, qm, dom, offs, out):
                 picked[:, u, first_slot : first_slot + count], words.indirect(list_columns(first_slot, count))
             )
 
-        pair_up(0)
+        pair_up(0, 0, 0, CHUNK, on_scalar)
+        pair_up(0, 1, 0, 704, on_vector)
+        pair_up(0, 1, 704, CHUNK, on_scalar)
         gather(0, 0, B * N)
-        pair_up(1)
-        for b in range(B):
-            gather(1, N * b, N)
+        pair_up(1, 0, 0, CHUNK, on_scalar)
+        pair_up(1, 1, 0, CHUNK // 2, on_vector)
+        pair_up(1, 1, CHUNK // 2, 896, on_vector)
+        pair_up(1, 1, 896, CHUNK, on_scalar)
+        gather(1, 0, N)
 
         windows = [keep.tile([P, T], F32, name="window%d" % k) for k in range(D // P)]
         for window in windows:
@@ -109,12 +109,13 @@ def tile_attend_gat_sig_c_kernel(tc, qT, cT, doT, rw, qm, dom, offs, out):
         scales = {}
 
         def new_operand(name, b):
-            buffer_name = "grouped%d" % GROUPED_BUFFER[(name, b)]
-            grouped[(name, b)] = reuse.tile([P, WIDTH * PACK], BF16, name=buffer_name, align_bytes=64)
+            grouped[(name, b)] = ring.tile([P, WIDTH * PACK], BF16, name="grouped", align_bytes=64)
             codes[(name, b)] = keep.tile([P, WIDTH], U32, name="%s%d_codes" % (name, b), align_bytes=64)
             scales[(name, b)] = keep.tile([P, WIDTH], U8, name="%s%d_scales" % (name, b), align_bytes=64)
 
         def grouped_columns(name, b, cols):
+            if (name, b, cols) == ("dom", 0, HALVES[0]):
+                return picked_row[:, (2 * B - 1) * N :].bitcast(BF16)
             return grouped[(name, b)][:, PACK * cols.start : PACK * cols.stop]
 
         def as_grouped(name, b, cols):
@@ -124,11 +125,12 @@ def tile_attend_gat_sig_c_kernel(tc, qT, cT, doT, rw, qm, dom, offs, out):
             return tile[:, :, cols].rearrange("p j (c e) -> p c j e", e=2)
 
         def group_latents(b, cols, move):
-            src = picked[:, :, N * b + cols.start : N * b + cols.stop].bitcast(BF16)
-            move(
-                grouped_columns("latent", b, cols).rearrange("p (c u e) -> p c u e", u=2, e=2),
-                src.rearrange("p u (c e) -> p c u e", e=2),
-            )
+            src = picked[:, :, N * b + cols.start : N * b + cols.stop]
+            dst = grouped_columns("latent", b, cols).bitcast(U32).rearrange("p (c u) -> p c u", u=2)
+            move(dst, src.rearrange("p u c -> p c u"))
+
+        def words_on_vector(dst, src):
+            nc.vector.tensor_copy(dst.bitcast(I32), src.bitcast(I32))
 
         def group_queries(name, b, moves):
             dst = grouped[(name, b)][:].rearrange("p (h e m j) -> p h m j e", h=2, e=2, j=PACK)
@@ -155,81 +157,99 @@ def tile_attend_gat_sig_c_kernel(tc, qT, cT, doT, rw, qm, dom, offs, out):
                 stop=stop,
             )
 
-        def weights(b):
-            prob = reuse.tile([P, PACK, N], F32, name="prob")
-            neg_pw = reuse.tile([P, PACK, N], F32, name="neg_pw")
-            slope = reuse.tile([P, PACK, N], F32, name="slope")
-            for t in range(PACK):
-                score = psum.tile([P, N], F32, name="score_bank%d" % t)
-                product(score, "q", t, "latent", b, True, True)
-                nc.scalar.activation(prob[:, t, :], score[:], ACT.Sigmoid)
-            for t in range(PACK):
-                dprob = psum.tile([P, N], F32, name="shared_bank%d" % t)
-                product(dprob, "do", t, "latent", b, True, True)
-                nc.scalar.activation(neg_pw[:, t, :], prob[:, t, :], ACT.Copy, scale=neg_gate[:, b, t : t + 1])
-                nc.vector.scalar_tensor_tensor(slope[:, t, :], prob[:, t, :], 1.0, dprob[:], ALU.subtract, ALU.mult)
-            return neg_pw, slope
+        prob = {}
+        neg_pw = {}
+        slope = {}
 
-        def group_weights(b, neg_pw, slope, parts):
+        def scores(b):
+            prob[b] = reuse.tile([P, PACK, N], F32, name="prob")
+            for t in range(PACK):
+                bank = psum.tile([P, N], F32, name="bank")
+                product(bank, "q", t, "latent", b, True, True)
+                nc.scalar.activation(prob[b][:, t, :], bank[:], ACT.Sigmoid)
+
+        def gated_on_vector(b, t):
+            nc.vector.tensor_scalar(neg_pw[b][:, t, :], prob[b][:, t, :], neg_gate[:, b, t : t + 1], None, ALU.mult)
+
+        def gated_on_scalar(b, t):
+            nc.scalar.activation(neg_pw[b][:, t, :], prob[b][:, t, :], ACT.Copy, scale=neg_gate[:, b, t : t + 1])
+
+        def slopes(b, gated):
+            neg_pw[b] = reuse.tile([P, PACK, N], F32, name="neg_pw")
+            slope[b] = reuse.tile([P, PACK, N], F32, name="slope")
+            for t in range(PACK):
+                bank = psum.tile([P, N], F32, name="bank")
+                product(bank, "do", t, "latent", b, True, True)
+                gated(b, t)
+                nc.vector.scalar_tensor_tensor(slope[b][:, t, :], prob[b][:, t, :], 1.0, bank[:], ALU.subtract, ALU.mult)
+
+        def group_weights(b):
             new_operand("ds", b)
             new_operand("pw", b)
-            for cols in parts:
-                nc.vector.tensor_tensor(
-                    as_grouped("ds", b, cols), as_planar(slope, cols), as_planar(neg_pw, cols), ALU.mult
-                )
-                nc.scalar.activation(as_grouped("pw", b, cols), as_planar(neg_pw, cols), ACT.Copy, scale=-1.0)
+            nc.vector.tensor_tensor(
+                as_grouped("ds", b, WHOLE), as_planar(slope[b], WHOLE), as_planar(neg_pw[b], WHOLE), ALU.mult
+            )
+            nc.scalar.activation(as_grouped("pw", b, WHOLE), as_planar(neg_pw[b], WHOLE), ACT.Copy, scale=-1.0)
+
+        def rows_half(name, b, half):
+            cols = HALVES[half]
+            on_scalar(as_grouped(name, b, cols), as_planar(raw[(name, b)], cols))
+            quantize(name, b, cols)
 
         def gradient(b, k):
-            bank = psum.tile([P, N], F32, name="shared_bank%d" % k)
-            product(bank, "qm", k, "ds", b, True, False)
-            product(bank, "dom", k, "pw", b, False, True)
+            bank = psum.tile([P, N], F32, name="bank")
+            product(bank, "dom", k, "pw", b, True, False)
+            product(bank, "qm", k, "ds", b, False, True)
             dense = reuse.tile([P, N], F32, name="dense%d" % k)
             on_scalar(dense[:], bank[:])
             nc.vector.tensor_copy(windows[k][:].indirect(list_columns(N * b, N)), dense[:])
 
         for name in ("latent", "q", "do"):
             new_operand(name, 0)
-        group_latents(0, HALVES[0], nc.scalar.copy)
-        group_latents(0, HALVES[1], on_vector)
-        group_queries("q", 0, (on_vector, on_scalar))
-        group_queries("do", 0, (on_scalar, on_vector))
+        group_latents(0, WHOLE, words_on_vector)
         quantize("latent", 0, WHOLE)
-        for name in ("q", "do"):
-            for cols in HALVES:
-                quantize(name, 0, cols)
-        neg_pw, slope = weights(0)
-
+        group_queries("q", 0, (on_scalar, on_scalar))
+        for cols in HALVES:
+            quantize("q", 0, cols)
+        group_queries("do", 0, (on_vector, on_scalar))
+        for cols in HALVES:
+            quantize("do", 0, cols)
+        scores(0)
+        slopes(0, gated_on_vector)
+        for name in ("qm", "dom"):
+            new_operand(name, 0)
+        rows_half("qm", 0, 0)
+        group_weights(0)
+        rows_half("dom", 0, 0)
+        quantize("pw", 0, WHOLE)
+        quantize("ds", 0, WHOLE)
+        gather(1, N, N)
+        rows_half("qm", 0, 1)
+        gradient(0, 0)
         new_operand("latent", 1)
         group_latents(1, WHOLE, nc.scalar.copy)
         quantize("latent", 1, WHOLE)
-
-        group_weights(0, neg_pw, slope, HALVES)
-        for name in ("qm", "dom"):
-            new_operand(name, 0)
-            for cols, move in zip(HALVES, (on_vector, on_scalar)):
-                move(as_grouped(name, 0, cols), as_planar(raw[(name, 0)], cols))
-                quantize(name, 0, cols)
-        quantize("ds", 0, WHOLE)
-        quantize("pw", 0, WHOLE)
+        rows_half("dom", 0, 1)
 
         new_operand("q", 1)
-        group_queries("q", 1, (on_scalar, on_vector))
+        group_queries("q", 1, (on_scalar, on_scalar))
         quantize("q", 1, WHOLE)
-        gradient(0, 0)
         gradient(0, 1)
         new_operand("do", 1)
         group_queries("do", 1, (on_scalar, on_scalar))
         quantize("do", 1, WHOLE)
         gradient(0, 2)
-        neg_pw, slope = weights(1)
-        group_weights(1, neg_pw, slope, (WHOLE,))
+        scores(1)
+        slopes(1, gated_on_scalar)
+        group_weights(1)
         for name in ("qm", "dom"):
             new_operand(name, 1)
-            on_scalar(as_grouped(name, 1, WHOLE), as_planar(raw[(name, 1)], WHOLE))
-            quantize(name, 1, WHOLE)
-        quantize("ds", 1, WHOLE)
+            rows_half(name, 1, 0)
         quantize("pw", 1, WHOLE)
+        quantize("ds", 1, WHOLE)
         gradient(0, 3)
+        for name in ("qm", "dom"):
+            rows_half(name, 1, 1)
 
         for k in range(D // P):
             gradient(1, k)

@@ -26,9 +26,8 @@ WHOLE = slice(0, WIDTH)
 HALVES = (slice(0, WIDTH // 2), slice(WIDTH // 2, WIDTH))
 FORMAT = {"q": E4M3, "latent": E4M3, "do": E5M2, "qm": E4M3, "ds": E5M2, "dom": E5M2, "pw": E4M3}
 
-LAST_CHUNK_ON_VECTOR = 704
-GROUPED_BUFFERS = 8
-PSUM_BANKS = 8
+LAST_CHUNK_ON_VECTOR = 640
+GROUPED_BUFFERS = 7
 
 
 def tile_attend_gat_sig_c_kernel(tc, qT, cT, doT, rw, qm, dom, offs, out):
@@ -38,7 +37,7 @@ def tile_attend_gat_sig_c_kernel(tc, qT, cT, doT, rw, qm, dom, offs, out):
         keep = ctx.enter_context(tc.tile_pool(name="keep", bufs=1))
         reuse = ctx.enter_context(tc.tile_pool(name="reuse", bufs=1))
         ring = ctx.enter_context(tc.tile_pool(name="ring", bufs=GROUPED_BUFFERS))
-        psum = ctx.enter_context(tc.psum_pool(name="psum", bufs=PSUM_BANKS))
+        psum = ctx.enter_context(tc.psum_pool(name="psum", bufs=1))
 
         def on_scalar(dst, src):
             nc.scalar.activation(dst, src, ACT.Copy)
@@ -52,20 +51,25 @@ def tile_attend_gat_sig_c_kernel(tc, qT, cT, doT, rw, qm, dom, offs, out):
         chunks = [[reuse.tile([P, 2, CHUNK], F32, name="raw%d" % (4 + 2 * u + h)) for h in range(2)] for u in range(2)]
         for u in range(2):
             for h in range(2):
-                pieces = 2 if (u, h) == (1, 1) else 1
-                for piece in range(pieces):
-                    cols = slice(CHUNK // pieces * piece, CHUNK // pieces * (piece + 1))
-                    nc.sync.dma_start(chunks[u][h][:, :, cols], pool_rows[u][:, :, CHUNK * h + cols.start : CHUNK * h + cols.stop])
+                nc.sync.dma_start(chunks[u][h][:], pool_rows[u][:, :, CHUNK * h : CHUNK * (h + 1)])
 
-        loads = [(name, b, src[b]) for b in range(B) for name, src in (("q", qT), ("do", doT), ("qm", qm), ("dom", dom))]
         raw = {}
-        for index, (name, b, src) in enumerate(loads):
-            tile = reuse.tile([P, PACK, WIDTH], F32, name="raw%d" % index)
-            nc.sync.dma_start(tile[:], src.rearrange("(p j) c -> p j c", j=PACK))
-            raw[(name, b)] = tile
-            if (name, b) == ("do", 0):
-                gate = keep.tile([P, B, PACK], F32, name="gate")
-                nc.sync.dma_start(gate[:], rw.rearrange("b (p t) o -> p b (t o)", t=PACK))
+
+        def load(key, src, buffer_name):
+            raw[key] = reuse.tile([P, PACK, src.shape[1]], F32, name=buffer_name)
+            nc.sync.dma_start(raw[key][:], src.rearrange("(p j) c -> p j c", j=PACK))
+
+        load(("q", 0), qT[0], "raw0")
+        load(("do", 0), doT[0], "raw1")
+        gate = keep.tile([P, B, PACK], F32, name="gate")
+        nc.sync.dma_start(gate[:], rw.rearrange("b (p t) o -> p b (t o)", t=PACK))
+        for half, cols in enumerate(HALVES):
+            load(("qm", 0, half), qm[0][:, cols], "qm0%d" % half)
+            load(("dom", 0, half), dom[0][:, cols], "dom0%d" % half)
+        load(("q", 1), qT[1], "raw4")
+        load(("do", 1), doT[1], "raw5")
+        load(("qm", 1), qm[1], "raw6")
+        load(("dom", 1), dom[1], "raw7")
 
         warm_up = keep.tile([P, 1], F32, name="warm_up")
         nc.scalar.activation(warm_up[:], chunks[0][0][:, 0, 0:1], ACT.Sigmoid)
@@ -89,13 +93,11 @@ def tile_attend_gat_sig_c_kernel(tc, qT, cT, doT, rw, qm, dom, offs, out):
             )
 
         pair_up(0, 0, 0, CHUNK, on_scalar)
-        pair_up(0, 1, 0, 704, on_vector)
-        pair_up(0, 1, 704, CHUNK, on_scalar)
+        pair_up(0, 1, 0, CHUNK, on_scalar)
         gather(0, 0, B * N)
         pair_up(1, 0, 0, CHUNK, on_scalar)
-        pair_up(1, 1, 0, CHUNK // 2, on_vector)
-        pair_up(1, 1, CHUNK // 2, 896, on_vector)
-        pair_up(1, 1, 896, CHUNK, on_scalar)
+        pair_up(1, 1, 0, LAST_CHUNK_ON_VECTOR, on_vector)
+        pair_up(1, 1, LAST_CHUNK_ON_VECTOR, CHUNK, on_scalar)
         gather(1, 0, N)
 
         windows = [keep.tile([P, T], F32, name="window%d" % k) for k in range(D // P)]
@@ -105,17 +107,22 @@ def tile_attend_gat_sig_c_kernel(tc, qT, cT, doT, rw, qm, dom, offs, out):
         nc.vector.tensor_scalar(neg_gate[:], gate[:], -1.0, None, ALU.mult)
 
         grouped = {}
+        late = {}
         codes = {}
         scales = {}
 
-        def new_operand(name, b):
-            grouped[(name, b)] = ring.tile([P, WIDTH * PACK], BF16, name="grouped", align_bytes=64)
+        def new_operand(name, b, buffer=None):
+            if buffer is None:
+                buffer = ring.tile([P, WIDTH * PACK], BF16, name="grouped", align_bytes=64)[:]
+            grouped[(name, b)] = buffer
             codes[(name, b)] = keep.tile([P, WIDTH], U32, name="%s%d_codes" % (name, b), align_bytes=64)
             scales[(name, b)] = keep.tile([P, WIDTH], U8, name="%s%d_scales" % (name, b), align_bytes=64)
 
         def grouped_columns(name, b, cols):
             if (name, b, cols) == ("dom", 0, HALVES[0]):
                 return picked_row[:, (2 * B - 1) * N :].bitcast(BF16)
+            if (name, b, cols.start) in late:
+                return late[(name, b, cols.start)]
             return grouped[(name, b)][:, PACK * cols.start : PACK * cols.stop]
 
         def as_grouped(name, b, cols):
@@ -133,24 +140,33 @@ def tile_attend_gat_sig_c_kernel(tc, qT, cT, doT, rw, qm, dom, offs, out):
             nc.vector.tensor_copy(dst.bitcast(I32), src.bitcast(I32))
 
         def group_queries(name, b, moves):
-            dst = grouped[(name, b)][:].rearrange("p (h e m j) -> p h m j e", h=2, e=2, j=PACK)
+            dst = grouped[(name, b)].rearrange("p (h e m j) -> p h m j e", h=2, e=2, j=PACK)
             src = raw[(name, b)][:].rearrange("p j (m h e) -> p h m j e", h=2, e=2)
             for h, move in enumerate(moves):
                 move(dst[:, h], src[:, h])
 
+        early_codes = reuse.tile([P, WIDTH // 2], U32, name="early_codes", align_bytes=64)
+        early_scales = reuse.tile([P, WIDTH // 2], U8, name="early_scales", align_bytes=64)
+
+        def quantized(name, b, cols):
+            if (name, b) == ("qm", 0) and cols.stop <= WIDTH // 2:
+                return early_codes[:, cols].bitcast(FORMAT[name]), early_scales[:, cols]
+            return codes[(name, b)][:, cols].bitcast(FORMAT[name]), scales[(name, b)][:, cols]
+
         def quantize(name, b, cols):
+            out_codes, out_scales = quantized(name, b, cols)
             nc.vector.quantize_mx(
-                out=codes[(name, b)][:, cols].bitcast(FORMAT[name]),
-                scales=scales[(name, b)][:, cols],
+                out=out_codes,
+                scales=out_scales,
                 in_=grouped_columns(name, b, cols),
             )
 
         def product(bank, stationary, block, moving, b, start, stop):
-            cols = slice(P * block, P * (block + 1))
+            lhs_codes, lhs_scales = quantized(stationary, b, slice(P * block, P * (block + 1)))
             nc.tensor.matmul_mx(
                 out=bank[:],
-                lhsT=codes[(stationary, b)][:, cols].bitcast(FORMAT[stationary]),
-                lhsT_scale=scales[(stationary, b)][:, cols],
+                lhsT=lhs_codes,
+                lhsT_scale=lhs_scales,
                 rhs=codes[(moving, b)][:].bitcast(FORMAT[moving]),
                 rhs_scale=scales[(moving, b)][:],
                 start=start,
@@ -162,9 +178,9 @@ def tile_attend_gat_sig_c_kernel(tc, qT, cT, doT, rw, qm, dom, offs, out):
         slope = {}
 
         def scores(b):
-            prob[b] = reuse.tile([P, PACK, N], F32, name="prob")
+            prob[b] = reuse.tile([P, PACK, N], F32, name="prob", align_bytes=64)
             for t in range(PACK):
-                bank = psum.tile([P, N], F32, name="bank")
+                bank = psum.tile([P, N], F32, name="score_bank%d" % t)
                 product(bank, "q", t, "latent", b, True, True)
                 nc.scalar.activation(prob[b][:, t, :], bank[:], ACT.Sigmoid)
 
@@ -176,11 +192,11 @@ def tile_attend_gat_sig_c_kernel(tc, qT, cT, doT, rw, qm, dom, offs, out):
 
         def slopes(b, gated):
             neg_pw[b] = reuse.tile([P, PACK, N], F32, name="neg_pw")
-            slope[b] = reuse.tile([P, PACK, N], F32, name="slope")
+            slope[b] = reuse.tile([P, PACK, N], F32, name="slope", align_bytes=64)
             for t in range(PACK):
-                bank = psum.tile([P, N], F32, name="bank")
+                bank = psum.tile([P, N], F32, name="shared_bank%d" % t)
                 product(bank, "do", t, "latent", b, True, True)
-                gated(b, t)
+                gated[t](b, t)
                 nc.vector.scalar_tensor_tensor(slope[b][:, t, :], prob[b][:, t, :], 1.0, bank[:], ALU.subtract, ALU.mult)
 
         def group_weights(b):
@@ -193,14 +209,21 @@ def tile_attend_gat_sig_c_kernel(tc, qT, cT, doT, rw, qm, dom, offs, out):
 
         def rows_half(name, b, half):
             cols = HALVES[half]
-            on_scalar(as_grouped(name, b, cols), as_planar(raw[(name, b)], cols))
+            src = as_planar(raw[(name, b)], cols) if b == 1 else as_planar(raw[(name, b, half)], HALVES[0])
+            on_scalar(as_grouped(name, b, cols), src)
             quantize(name, b, cols)
 
-        def gradient(b, k):
-            bank = psum.tile([P, N], F32, name="bank")
+        def sums(b, k, bank_name):
+            bank = psum.tile([P, N], F32, name=bank_name)
             product(bank, "dom", k, "pw", b, True, False)
             product(bank, "qm", k, "ds", b, False, True)
-            dense = reuse.tile([P, N], F32, name="dense%d" % k)
+            return bank
+
+        def gradient(b, k, bank_name, buffer_name):
+            scatter(b, k, sums(b, k, bank_name), buffer_name)
+
+        def scatter(b, k, bank, buffer_name):
+            dense = reuse.tile([P, N], F32, name=buffer_name)
             on_scalar(dense[:], bank[:])
             nc.vector.tensor_copy(windows[k][:].indirect(list_columns(N * b, N)), dense[:])
 
@@ -211,11 +234,11 @@ def tile_attend_gat_sig_c_kernel(tc, qT, cT, doT, rw, qm, dom, offs, out):
         group_queries("q", 0, (on_scalar, on_scalar))
         for cols in HALVES:
             quantize("q", 0, cols)
-        group_queries("do", 0, (on_vector, on_scalar))
+        group_queries("do", 0, (on_vector, on_vector))
         for cols in HALVES:
             quantize("do", 0, cols)
         scores(0)
-        slopes(0, gated_on_vector)
+        slopes(0, [gated_on_vector] * 2 + [gated_on_scalar] * 2)
         for name in ("qm", "dom"):
             new_operand(name, 0)
         rows_half("qm", 0, 0)
@@ -225,32 +248,35 @@ def tile_attend_gat_sig_c_kernel(tc, qT, cT, doT, rw, qm, dom, offs, out):
         quantize("ds", 0, WHOLE)
         gather(1, N, N)
         rows_half("qm", 0, 1)
-        gradient(0, 0)
-        new_operand("latent", 1)
+        gradient(0, 0, "shared_bank0", "dense0")
+        second_sums = sums(0, 1, "shared_bank1")
+        new_operand("latent", 1, reuse.tile([P, WIDTH * PACK], BF16, name="early_codes", align_bytes=64)[:])
         group_latents(1, WHOLE, nc.scalar.copy)
         quantize("latent", 1, WHOLE)
         rows_half("dom", 0, 1)
 
-        new_operand("q", 1)
+        new_operand("q", 1, reuse.tile([P, WIDTH * PACK], BF16, name="early_scales", align_bytes=64)[:])
         group_queries("q", 1, (on_scalar, on_scalar))
         quantize("q", 1, WHOLE)
-        gradient(0, 1)
+        scatter(0, 1, second_sums, "raw4")
         new_operand("do", 1)
         group_queries("do", 1, (on_scalar, on_scalar))
         quantize("do", 1, WHOLE)
-        gradient(0, 2)
+        gradient(0, 2, "shared_bank2", "raw5")
         scores(1)
-        slopes(1, gated_on_scalar)
+        slopes(1, [gated_on_scalar] * 4)
         group_weights(1)
         for name in ("qm", "dom"):
             new_operand(name, 1)
             rows_half(name, 1, 0)
         quantize("pw", 1, WHOLE)
         quantize("ds", 1, WHOLE)
-        gradient(0, 3)
-        for name in ("qm", "dom"):
+        gradient(0, 3, "score_bank0", "neg_pw")
+        both = reuse.tile([P, 2, WIDTH // 2 * PACK], BF16, name="slope", align_bytes=64)
+        for index, name in enumerate(("qm", "dom")):
+            late[(name, 1, HALVES[1].start)] = both[:, index, :]
             rows_half(name, 1, 1)
 
         for k in range(D // P):
-            gradient(1, k)
+            gradient(1, k, "shared_bank%d" % k, "dense%d" % k)
             nc.sync.dma_start(out[P * k : P * (k + 1), :], windows[k][:])

@@ -45,18 +45,19 @@ def tile_attend_gat_sig_c_kernel(tc, qT, cT, doT, rw, qm, dom, offs, out):
         on_vector = nc.vector.tensor_copy
 
         offsets = keep.tile([P, B * N // SLOTS_PER_COLUMN], U16, name="offsets")
-        nc.sync.dma_start(offsets[:], offs)
 
         pool_rows = cT.rearrange("(p u e) c -> u p e c", u=2, e=2)
-        chunks = [[reuse.tile([P, 2, CHUNK], F32, name="raw%d" % (4 + 2 * u + h)) for h in range(2)] for u in range(2)]
+        chunks = [[reuse.tile([P, 2, CHUNK], F32, name="raw%d" % (4 + 2 * u + h), align_bytes=64) for h in range(2)] for u in range(2)]
         for u in range(2):
             for h in range(2):
                 nc.sync.dma_start(chunks[u][h][:], pool_rows[u][:, :, CHUNK * h : CHUNK * (h + 1)])
+            if u == 0:
+                nc.sync.dma_start(offsets[:], offs)
 
         raw = {}
 
         def load(key, src, buffer_name):
-            raw[key] = reuse.tile([P, PACK, src.shape[1]], F32, name=buffer_name)
+            raw[key] = reuse.tile([P, PACK, src.shape[1]], F32, name=buffer_name, align_bytes=64)
             nc.sync.dma_start(raw[key][:], src.rearrange("(p j) c -> p j c", j=PACK))
 
         load(("q", 0), qT[0], "raw0")
@@ -98,7 +99,8 @@ def tile_attend_gat_sig_c_kernel(tc, qT, cT, doT, rw, qm, dom, offs, out):
         pair_up(1, 0, 0, CHUNK, on_scalar)
         pair_up(1, 1, 0, LAST_CHUNK_ON_VECTOR, on_vector)
         pair_up(1, 1, LAST_CHUNK_ON_VECTOR, CHUNK, on_scalar)
-        gather(1, 0, N)
+        for cols in HALVES:
+            gather(1, cols.start, N // 2)
 
         windows = [keep.tile([P, T], F32, name="window%d" % k) for k in range(D // P)]
         for window in windows:
@@ -145,11 +147,11 @@ def tile_attend_gat_sig_c_kernel(tc, qT, cT, doT, rw, qm, dom, offs, out):
             for h, move in enumerate(moves):
                 move(dst[:, h], src[:, h])
 
-        early_codes = reuse.tile([P, WIDTH // 2], U32, name="early_codes", align_bytes=64)
-        early_scales = reuse.tile([P, WIDTH // 2], U8, name="early_scales", align_bytes=64)
+        early_codes = reuse.tile([P, P], U32, name="early_codes", align_bytes=64)
+        early_scales = reuse.tile([P, P], U8, name="early_scales", align_bytes=64)
 
         def quantized(name, b, cols):
-            if (name, b) == ("qm", 0) and cols.stop <= WIDTH // 2:
+            if (name, b) == ("qm", 0) and cols.stop <= P:
                 return early_codes[:, cols].bitcast(FORMAT[name]), early_scales[:, cols]
             return codes[(name, b)][:, cols].bitcast(FORMAT[name]), scales[(name, b)][:, cols]
 
@@ -191,7 +193,7 @@ def tile_attend_gat_sig_c_kernel(tc, qT, cT, doT, rw, qm, dom, offs, out):
             nc.scalar.activation(neg_pw[b][:, t, :], prob[b][:, t, :], ACT.Copy, scale=neg_gate[:, b, t : t + 1])
 
         def slopes(b, gated):
-            neg_pw[b] = reuse.tile([P, PACK, N], F32, name="neg_pw")
+            neg_pw[b] = reuse.tile([P, PACK, N], F32, name="neg_pw", align_bytes=64)
             slope[b] = reuse.tile([P, PACK, N], F32, name="slope", align_bytes=64)
             for t in range(PACK):
                 bank = psum.tile([P, N], F32, name="shared_bank%d" % t)
@@ -211,7 +213,11 @@ def tile_attend_gat_sig_c_kernel(tc, qT, cT, doT, rw, qm, dom, offs, out):
             cols = HALVES[half]
             src = as_planar(raw[(name, b)], cols) if b == 1 else as_planar(raw[(name, b, half)], HALVES[0])
             on_scalar(as_grouped(name, b, cols), src)
-            quantize(name, b, cols)
+            if (name, b, half) == ("qm", 0, 0):
+                quantize(name, b, slice(0, P))
+                quantize(name, b, slice(P, 2 * P))
+            else:
+                quantize(name, b, cols)
 
         def sums(b, k, bank_name):
             bank = psum.tile([P, N], F32, name=bank_name)
@@ -223,14 +229,16 @@ def tile_attend_gat_sig_c_kernel(tc, qT, cT, doT, rw, qm, dom, offs, out):
             scatter(b, k, sums(b, k, bank_name), buffer_name)
 
         def scatter(b, k, bank, buffer_name):
-            dense = reuse.tile([P, N], F32, name=buffer_name)
+            dense = reuse.tile([P, N], F32, name=buffer_name, align_bytes=64)
             on_scalar(dense[:], bank[:])
             nc.vector.tensor_copy(windows[k][:].indirect(list_columns(N * b, N)), dense[:])
 
         for name in ("latent", "q", "do"):
             new_operand(name, 0)
-        group_latents(0, WHOLE, words_on_vector)
-        quantize("latent", 0, WHOLE)
+        for cols in HALVES:
+            group_latents(0, cols, words_on_vector)
+        for cols in HALVES:
+            quantize("latent", 0, cols)
         group_queries("q", 0, (on_scalar, on_scalar))
         for cols in HALVES:
             quantize("q", 0, cols)
@@ -249,7 +257,7 @@ def tile_attend_gat_sig_c_kernel(tc, qT, cT, doT, rw, qm, dom, offs, out):
         gather(1, N, N)
         rows_half("qm", 0, 1)
         gradient(0, 0, "shared_bank0", "dense0")
-        second_sums = sums(0, 1, "shared_bank1")
+        second_sums = sums(0, 1, "shared_bank0")
         new_operand("latent", 1, reuse.tile([P, WIDTH * PACK], BF16, name="early_codes", align_bytes=64)[:])
         group_latents(1, WHOLE, nc.scalar.copy)
         quantize("latent", 1, WHOLE)
@@ -258,21 +266,22 @@ def tile_attend_gat_sig_c_kernel(tc, qT, cT, doT, rw, qm, dom, offs, out):
         new_operand("q", 1, reuse.tile([P, WIDTH * PACK], BF16, name="early_scales", align_bytes=64)[:])
         group_queries("q", 1, (on_scalar, on_scalar))
         quantize("q", 1, WHOLE)
-        scatter(0, 1, second_sums, "raw4")
+        scatter(0, 1, second_sums, "dom01")
         new_operand("do", 1)
         group_queries("do", 1, (on_scalar, on_scalar))
         quantize("do", 1, WHOLE)
         gradient(0, 2, "shared_bank2", "raw5")
         scores(1)
-        slopes(1, [gated_on_scalar] * 4)
-        group_weights(1)
         for name in ("qm", "dom"):
             new_operand(name, 1)
-            rows_half(name, 1, 0)
+        rows_half("qm", 1, 0)
+        slopes(1, [gated_on_scalar] * 4)
+        group_weights(1)
+        rows_half("dom", 1, 0)
         quantize("pw", 1, WHOLE)
         quantize("ds", 1, WHOLE)
-        gradient(0, 3, "score_bank0", "neg_pw")
-        both = reuse.tile([P, 2, WIDTH // 2 * PACK], BF16, name="slope", align_bytes=64)
+        gradient(0, 3, "score_bank0", "slope")
+        both = reuse.tile([P, 2, WIDTH // 2 * PACK], BF16, name="neg_pw", align_bytes=64)
         for index, name in enumerate(("qm", "dom")):
             late[(name, 1, HALVES[1].start)] = both[:, index, :]
             rows_half(name, 1, 1)

@@ -192,6 +192,9 @@ def tile_attend_gat_sig_c_kernel(tc, qT, cT, doT, rw, qm, dom, offs, out):
         def gated_on_scalar(b, t):
             nc.scalar.activation(neg_pw[b][:, t, :], prob[b][:, t, :], ACT.Copy, scale=neg_gate[:, b, t : t + 1])
 
+        def gated_on_gpsimd(b, t):
+            nc.gpsimd.tensor_scalar(neg_pw[b][:, t, :], prob[b][:, t, :], neg_gate[:, b, t : t + 1], 0.0, ALU.mult, ALU.add)
+
         def slopes(b, gated):
             neg_pw[b] = reuse.tile([P, PACK, N], F32, name="neg_pw", align_bytes=64)
             slope[b] = reuse.tile([P, PACK, N], F32, name="slope", align_bytes=64)
@@ -201,10 +204,10 @@ def tile_attend_gat_sig_c_kernel(tc, qT, cT, doT, rw, qm, dom, offs, out):
                 gated[t](b, t)
                 nc.vector.scalar_tensor_tensor(slope[b][:, t, :], prob[b][:, t, :], 1.0, bank[:], ALU.subtract, ALU.mult)
 
-        def group_weights(b):
+        def group_weights(b, engine):
             new_operand("ds", b)
             new_operand("pw", b)
-            nc.vector.tensor_tensor(
+            engine.tensor_tensor(
                 as_grouped("ds", b, WHOLE), as_planar(slope[b], WHOLE), as_planar(neg_pw[b], WHOLE), ALU.mult
             )
             nc.scalar.activation(as_grouped("pw", b, WHOLE), as_planar(neg_pw[b], WHOLE), ACT.Copy, scale=-1.0)
@@ -228,10 +231,11 @@ def tile_attend_gat_sig_c_kernel(tc, qT, cT, doT, rw, qm, dom, offs, out):
         def gradient(b, k, bank_name, buffer_name):
             scatter(b, k, sums(b, k, bank_name), buffer_name)
 
-        def scatter(b, k, bank, buffer_name):
-            dense = reuse.tile([P, N], F32, name=buffer_name, align_bytes=64)
-            on_scalar(dense[:], bank[:])
-            nc.vector.tensor_copy(windows[k][:].indirect(list_columns(N * b, N)), dense[:])
+        def scatter(b, k, bank, buffer_name, cols=WHOLE):
+            count = cols.stop - cols.start
+            dense = reuse.tile([P, count], F32, name=buffer_name, align_bytes=64)
+            on_scalar(dense[:], bank[:, cols])
+            nc.vector.tensor_copy(windows[k][:].indirect(list_columns(N * b + cols.start, count)), dense[:])
 
         for name in ("latent", "q", "do"):
             new_operand(name, 0)
@@ -250,7 +254,7 @@ def tile_attend_gat_sig_c_kernel(tc, qT, cT, doT, rw, qm, dom, offs, out):
         for name in ("qm", "dom"):
             new_operand(name, 0)
         rows_half("qm", 0, 0)
-        group_weights(0)
+        group_weights(0, nc.vector)
         rows_half("dom", 0, 0)
         quantize("pw", 0, WHOLE)
         quantize("ds", 0, WHOLE)
@@ -266,21 +270,36 @@ def tile_attend_gat_sig_c_kernel(tc, qT, cT, doT, rw, qm, dom, offs, out):
         new_operand("q", 1, reuse.tile([P, WIDTH * PACK], BF16, name="early_scales", align_bytes=64)[:])
         group_queries("q", 1, (on_scalar, on_scalar))
         quantize("q", 1, WHOLE)
-        scatter(0, 1, second_sums, "dom01")
+        scatter(0, 1, second_sums, "dom01", HALVES[0])
         new_operand("do", 1)
         group_queries("do", 1, (on_scalar, on_scalar))
         quantize("do", 1, WHOLE)
-        gradient(0, 2, "shared_bank2", "raw5")
+        scatter(0, 1, second_sums, "raw4", HALVES[1])
         scores(1)
+        third_sums = sums(0, 2, "score_bank0")
+        third = reuse.tile([P, N], F32, name="raw5", align_bytes=64)
+        on_scalar(third[:], third_sums[:])
+        slopes(1, [gated_on_gpsimd] * 4)
+        nc.vector.tensor_copy(windows[2][:].indirect(list_columns(0, N)), third[:])
+        new_operand("ds", 1)
+        new_operand("pw", 1)
+        nc.scalar.activation(as_grouped("pw", 1, WHOLE), as_planar(neg_pw[1], WHOLE), ACT.Copy, scale=-1.0)
+        planar_ds = reuse.tile([P, PACK, N], BF16, name="planar_ds")
+        for t in range(PACK):
+            nc.gpsimd.tensor_tensor(planar_ds[:, t, :], slope[1][:, t, :], neg_pw[1][:, t, :], ALU.mult)
+        quantize("pw", 1, WHOLE)
         for name in ("qm", "dom"):
             new_operand(name, 1)
         rows_half("qm", 1, 0)
-        slopes(1, [gated_on_scalar] * 4)
-        group_weights(1)
+        fourth_sums = sums(0, 3, "score_bank1")
+        scatter(0, 3, fourth_sums, "prob", HALVES[0])
         rows_half("dom", 1, 0)
-        quantize("pw", 1, WHOLE)
+        nc.scalar.copy(
+            grouped[("ds", 1)].rearrange("p (c e j) -> p c j e", e=4, j=PACK),
+            planar_ds[:].rearrange("p j (c e) -> p c j e", e=4),
+        )
         quantize("ds", 1, WHOLE)
-        gradient(0, 3, "score_bank0", "slope")
+        scatter(0, 3, fourth_sums, "slope", HALVES[1])
         both = reuse.tile([P, 2, WIDTH // 2 * PACK], BF16, name="neg_pw", align_bytes=64)
         for index, name in enumerate(("qm", "dom")):
             late[(name, 1, HALVES[1].start)] = both[:, index, :]

@@ -39,6 +39,9 @@ def tile_attend_gat_sig_c_kernel(tc, qT, cT, doT, rw, qm, dom, offs, out):
         ring = ctx.enter_context(tc.tile_pool(name="ring", bufs=GROUPED_BUFFERS))
         psum = ctx.enter_context(tc.psum_pool(name="psum", bufs=1))
 
+        def reused(shape, dtype, buffer_name):
+            return reuse.tile(shape, dtype, name=buffer_name, align_bytes=64)
+
         def on_scalar(dst, src):
             nc.scalar.activation(dst, src, ACT.Copy)
 
@@ -47,7 +50,7 @@ def tile_attend_gat_sig_c_kernel(tc, qT, cT, doT, rw, qm, dom, offs, out):
         offsets = keep.tile([P, B * N // SLOTS_PER_COLUMN], U16, name="offsets")
 
         pool_rows = cT.rearrange("(p u e) c -> u p e c", u=2, e=2)
-        chunks = [[reuse.tile([P, 2, CHUNK], F32, name="raw%d" % (4 + 2 * u + h), align_bytes=64) for h in range(2)] for u in range(2)]
+        chunks = [[reused([P, 2, CHUNK], F32, "chunk%d" % (2 * u + h)) for h in range(2)] for u in range(2)]
         for u in range(2):
             for h in range(2):
                 nc.sync.dma_start(chunks[u][h][:], pool_rows[u][:, :, CHUNK * h : CHUNK * (h + 1)])
@@ -57,20 +60,18 @@ def tile_attend_gat_sig_c_kernel(tc, qT, cT, doT, rw, qm, dom, offs, out):
         raw = {}
 
         def load(key, src, buffer_name):
-            raw[key] = reuse.tile([P, PACK, src.shape[1]], F32, name=buffer_name, align_bytes=64)
+            raw[key] = reused([P, PACK, src.shape[1]], F32, buffer_name)
             nc.sync.dma_start(raw[key][:], src.rearrange("(p j) c -> p j c", j=PACK))
 
-        load(("q", 0), qT[0], "raw0")
-        load(("do", 0), doT[0], "raw1")
+        load(("q", 0), qT[0], "q0")
+        load(("do", 0), doT[0], "do0")
         gate = keep.tile([P, B, PACK], F32, name="gate")
         nc.sync.dma_start(gate[:], rw.rearrange("b (p t) o -> p b (t o)", t=PACK))
         for half, cols in enumerate(HALVES):
-            load(("qm", 0, half), qm[0][:, cols], "qm0%d" % half)
-            load(("dom", 0, half), dom[0][:, cols], "dom0%d" % half)
-        load(("q", 1), qT[1], "raw4")
-        load(("do", 1), doT[1], "raw5")
-        load(("qm", 1), qm[1], "raw6")
-        load(("dom", 1), dom[1], "raw7")
+            load(("qm", 0, half), qm[0][:, cols], "qm0_half%d" % half)
+            load(("dom", 0, half), dom[0][:, cols], "dom0_half%d" % half)
+        for index, (name, src) in enumerate((("q", qT), ("do", doT), ("qm", qm), ("dom", dom))):
+            load((name, 1), src[1], "chunk%d" % index)
 
         warm_up = keep.tile([P, 1], F32, name="warm_up")
         nc.scalar.activation(warm_up[:], chunks[0][0][:, 0, 0:1], ACT.Sigmoid)
@@ -109,7 +110,7 @@ def tile_attend_gat_sig_c_kernel(tc, qT, cT, doT, rw, qm, dom, offs, out):
         nc.vector.tensor_scalar(neg_gate[:], gate[:], -1.0, None, ALU.mult)
 
         grouped = {}
-        late = {}
+        grouped_apart = {}
         codes = {}
         scales = {}
 
@@ -121,17 +122,15 @@ def tile_attend_gat_sig_c_kernel(tc, qT, cT, doT, rw, qm, dom, offs, out):
             scales[(name, b)] = keep.tile([P, WIDTH], U8, name="%s%d_scales" % (name, b), align_bytes=64)
 
         def grouped_columns(name, b, cols):
-            if (name, b, cols) == ("dom", 0, HALVES[0]):
-                return picked_row[:, (2 * B - 1) * N :].bitcast(BF16)
-            if (name, b, cols.start) in late:
-                return late[(name, b, cols.start)]
+            if (name, b, cols.start) in grouped_apart:
+                return grouped_apart[(name, b, cols.start)]
             return grouped[(name, b)][:, PACK * cols.start : PACK * cols.stop]
 
-        def as_grouped(name, b, cols):
-            return grouped_columns(name, b, cols).rearrange("p (c e j) -> p c j e", e=2, j=PACK)
+        def as_grouped(name, b, cols, run=2):
+            return grouped_columns(name, b, cols).rearrange("p (c e j) -> p c j e", e=run, j=PACK)
 
-        def as_planar(tile, cols):
-            return tile[:, :, cols].rearrange("p j (c e) -> p c j e", e=2)
+        def as_planar(tile, cols, run=2):
+            return tile[:, :, cols].rearrange("p j (c e) -> p c j e", e=run)
 
         def group_latents(b, cols, move):
             src = picked[:, :, N * b + cols.start : N * b + cols.stop]
@@ -141,36 +140,32 @@ def tile_attend_gat_sig_c_kernel(tc, qT, cT, doT, rw, qm, dom, offs, out):
         def words_on_vector(dst, src):
             nc.vector.tensor_copy(dst.bitcast(I32), src.bitcast(I32))
 
-        def group_queries(name, b, moves):
+        def query_views(name, b):
             dst = grouped[(name, b)].rearrange("p (h e m j) -> p h m j e", h=2, e=2, j=PACK)
             src = raw[(name, b)][:].rearrange("p j (m h e) -> p h m j e", h=2, e=2)
-            for h, move in enumerate(moves):
-                move(dst[:, h], src[:, h])
+            return dst, src
 
-        early_codes = reuse.tile([P, P], U32, name="early_codes", align_bytes=64)
-        early_scales = reuse.tile([P, P], U8, name="early_scales", align_bytes=64)
+        first_codes = reused([P, P], U32, "first_codes")
+        first_scales = reused([P, P], U8, "first_scales")
 
         def quantized(name, b, cols):
             if (name, b) == ("qm", 0) and cols.stop <= P:
-                return early_codes[:, cols].bitcast(FORMAT[name]), early_scales[:, cols]
+                return first_codes[:, cols].bitcast(FORMAT[name]), first_scales[:, cols]
             return codes[(name, b)][:, cols].bitcast(FORMAT[name]), scales[(name, b)][:, cols]
 
         def quantize(name, b, cols):
             out_codes, out_scales = quantized(name, b, cols)
-            nc.vector.quantize_mx(
-                out=out_codes,
-                scales=out_scales,
-                in_=grouped_columns(name, b, cols),
-            )
+            nc.vector.quantize_mx(out=out_codes, scales=out_scales, in_=grouped_columns(name, b, cols))
 
         def product(bank, stationary, block, moving, b, start, stop):
             lhs_codes, lhs_scales = quantized(stationary, b, slice(P * block, P * (block + 1)))
+            rhs_codes, rhs_scales = quantized(moving, b, WHOLE)
             nc.tensor.matmul_mx(
                 out=bank[:],
                 lhsT=lhs_codes,
                 lhsT_scale=lhs_scales,
-                rhs=codes[(moving, b)][:].bitcast(FORMAT[moving]),
-                rhs_scale=scales[(moving, b)][:],
+                rhs=rhs_codes,
+                rhs_scale=rhs_scales,
                 start=start,
                 stop=stop,
             )
@@ -180,47 +175,35 @@ def tile_attend_gat_sig_c_kernel(tc, qT, cT, doT, rw, qm, dom, offs, out):
         slope = {}
 
         def scores(b):
-            prob[b] = reuse.tile([P, PACK, N], F32, name="prob", align_bytes=64)
+            prob[b] = reused([P, PACK, N], F32, "prob")
             for t in range(PACK):
                 bank = psum.tile([P, N], F32, name="score_bank%d" % t)
                 product(bank, "q", t, "latent", b, True, True)
                 nc.scalar.activation(prob[b][:, t, :], bank[:], ACT.Sigmoid)
 
-        def gated_on_vector(b, t):
-            nc.vector.tensor_scalar(neg_pw[b][:, t, :], prob[b][:, t, :], neg_gate[:, b, t : t + 1], None, ALU.mult)
+        def gated_on_vector(dst, src, factor):
+            nc.vector.tensor_scalar(dst, src, factor, None, ALU.mult)
 
-        def gated_on_scalar(b, t):
-            nc.scalar.activation(neg_pw[b][:, t, :], prob[b][:, t, :], ACT.Copy, scale=neg_gate[:, b, t : t + 1])
+        def gated_on_scalar(dst, src, factor):
+            nc.scalar.activation(dst, src, ACT.Copy, scale=factor)
 
-        def gated_on_gpsimd(b, t):
-            nc.gpsimd.tensor_scalar(neg_pw[b][:, t, :], prob[b][:, t, :], neg_gate[:, b, t : t + 1], 0.0, ALU.mult, ALU.add)
+        def gated_on_gpsimd(dst, src, factor):
+            nc.gpsimd.tensor_scalar(dst, src, factor, 0.0, ALU.mult, ALU.add)
 
-        def slopes(b, gated):
-            neg_pw[b] = reuse.tile([P, PACK, N], F32, name="neg_pw", align_bytes=64)
-            slope[b] = reuse.tile([P, PACK, N], F32, name="slope", align_bytes=64)
+        def slopes(b, gated, bank_names):
+            neg_pw[b] = reused([P, PACK, N], F32, "neg_pw")
+            slope[b] = reused([P, PACK, N], F32, "slope")
             for t in range(PACK):
-                bank = psum.tile([P, N], F32, name="shared_bank%d" % t)
+                bank = psum.tile([P, N], F32, name=bank_names[t])
                 product(bank, "do", t, "latent", b, True, True)
-                gated[t](b, t)
+                gated[t](neg_pw[b][:, t, :], prob[b][:, t, :], neg_gate[:, b, t : t + 1])
                 nc.vector.scalar_tensor_tensor(slope[b][:, t, :], prob[b][:, t, :], 1.0, bank[:], ALU.subtract, ALU.mult)
 
-        def group_weights(b, engine):
-            new_operand("ds", b)
-            new_operand("pw", b)
-            engine.tensor_tensor(
-                as_grouped("ds", b, WHOLE), as_planar(slope[b], WHOLE), as_planar(neg_pw[b], WHOLE), ALU.mult
-            )
+        def group_pw(b):
             nc.scalar.activation(as_grouped("pw", b, WHOLE), as_planar(neg_pw[b], WHOLE), ACT.Copy, scale=-1.0)
 
-        def rows_half(name, b, half):
-            cols = HALVES[half]
-            src = as_planar(raw[(name, b)], cols) if b == 1 else as_planar(raw[(name, b, half)], HALVES[0])
-            on_scalar(as_grouped(name, b, cols), src)
-            if (name, b, half) == ("qm", 0, 0):
-                quantize(name, b, slice(0, P))
-                quantize(name, b, slice(P, 2 * P))
-            else:
-                quantize(name, b, cols)
+        def group_rows(name, b, cols, planar):
+            on_scalar(as_grouped(name, b, cols), planar)
 
         def sums(b, k, bank_name):
             bank = psum.tile([P, N], F32, name=bank_name)
@@ -228,14 +211,16 @@ def tile_attend_gat_sig_c_kernel(tc, qT, cT, doT, rw, qm, dom, offs, out):
             product(bank, "qm", k, "ds", b, False, True)
             return bank
 
-        def gradient(b, k, bank_name, buffer_name):
-            scatter(b, k, sums(b, k, bank_name), buffer_name)
-
-        def scatter(b, k, bank, buffer_name, cols=WHOLE):
-            count = cols.stop - cols.start
-            dense = reuse.tile([P, count], F32, name=buffer_name, align_bytes=64)
+        def copy_out(bank, cols, buffer_name):
+            dense = reused([P, cols.stop - cols.start], F32, buffer_name)
             on_scalar(dense[:], bank[:, cols])
-            nc.vector.tensor_copy(windows[k][:].indirect(list_columns(N * b + cols.start, count)), dense[:])
+            return dense
+
+        def scatter(b, k, cols, dense):
+            slots = list_columns(N * b + cols.start, cols.stop - cols.start)
+            nc.vector.tensor_copy(windows[k][:].indirect(slots), dense[:])
+
+        shared_banks = ["shared_bank%d" % t for t in range(PACK)]
 
         for name in ("latent", "q", "do"):
             new_operand(name, 0)
@@ -243,68 +228,89 @@ def tile_attend_gat_sig_c_kernel(tc, qT, cT, doT, rw, qm, dom, offs, out):
             group_latents(0, cols, words_on_vector)
         for cols in HALVES:
             quantize("latent", 0, cols)
-        group_queries("q", 0, (on_scalar, on_scalar))
-        for cols in HALVES:
-            quantize("q", 0, cols)
-        group_queries("do", 0, (on_vector, on_vector))
-        for cols in HALVES:
-            quantize("do", 0, cols)
+        for name, move in (("q", on_scalar), ("do", on_vector)):
+            dst, src = query_views(name, 0)
+            for h in range(2):
+                move(dst[:, h], src[:, h])
+            for cols in HALVES:
+                quantize(name, 0, cols)
         scores(0)
-        slopes(0, [gated_on_vector] * 2 + [gated_on_scalar] * 2)
+        slopes(0, [gated_on_vector] * 2 + [gated_on_scalar] * 2, shared_banks)
+
+        def rows_of_first(name, half, pieces):
+            group_rows(name, 0, HALVES[half], as_planar(raw[(name, 0, half)], HALVES[0]))
+            for cols in pieces:
+                quantize(name, 0, cols)
+
         for name in ("qm", "dom"):
             new_operand(name, 0)
-        rows_half("qm", 0, 0)
-        group_weights(0, nc.vector)
-        rows_half("dom", 0, 0)
+        rows_of_first("qm", 0, (slice(0, P), slice(P, 2 * P)))
+        new_operand("ds", 0)
+        new_operand("pw", 0)
+        nc.vector.tensor_tensor(
+            as_grouped("ds", 0, WHOLE), as_planar(slope[0], WHOLE), as_planar(neg_pw[0], WHOLE), ALU.mult
+        )
+        group_pw(0)
+        grouped_apart[("dom", 0, 0)] = picked_row[:, (2 * B - 1) * N :].bitcast(BF16)
+        rows_of_first("dom", 0, HALVES[:1])
         quantize("pw", 0, WHOLE)
         quantize("ds", 0, WHOLE)
         gather(1, N, N)
-        rows_half("qm", 0, 1)
-        gradient(0, 0, "shared_bank0", "dense0")
+        rows_of_first("qm", 1, HALVES[1:])
+        scatter(0, 0, WHOLE, copy_out(sums(0, 0, "shared_bank0"), WHOLE, "dense0"))
         second_sums = sums(0, 1, "shared_bank0")
-        new_operand("latent", 1, reuse.tile([P, WIDTH * PACK], BF16, name="early_codes", align_bytes=64)[:])
+
+        new_operand("latent", 1, reused([P, WIDTH * PACK], BF16, "first_codes")[:])
         group_latents(1, WHOLE, nc.scalar.copy)
         quantize("latent", 1, WHOLE)
-        rows_half("dom", 0, 1)
-
-        new_operand("q", 1, reuse.tile([P, WIDTH * PACK], BF16, name="early_scales", align_bytes=64)[:])
-        group_queries("q", 1, (on_scalar, on_scalar))
+        rows_of_first("dom", 1, HALVES[1:])
+        new_operand("q", 1, reused([P, WIDTH * PACK], BF16, "first_scales")[:])
+        nc.scalar.copy(*query_views("q", 1))
         quantize("q", 1, WHOLE)
-        scatter(0, 1, second_sums, "dom01", HALVES[0])
+        scatter(0, 1, HALVES[0], copy_out(second_sums, HALVES[0], "dom0_half1"))
         new_operand("do", 1)
-        group_queries("do", 1, (on_scalar, on_scalar))
+        nc.scalar.copy(*query_views("do", 1))
         quantize("do", 1, WHOLE)
-        scatter(0, 1, second_sums, "raw4", HALVES[1])
+        scatter(0, 1, HALVES[1], copy_out(second_sums, HALVES[1], "chunk0"))
+
+        third_sums = sums(0, 2, shared_banks[3])
         scores(1)
-        third_sums = sums(0, 2, "score_bank0")
-        third = reuse.tile([P, N], F32, name="raw5", align_bytes=64)
-        on_scalar(third[:], third_sums[:])
-        slopes(1, [gated_on_gpsimd] * 4)
-        nc.vector.tensor_copy(windows[2][:].indirect(list_columns(0, N)), third[:])
+        third_dense = copy_out(third_sums, WHOLE, "chunk1")
+        slopes(1, [gated_on_gpsimd] * PACK, shared_banks[:3] + ["score_bank0"])
+        scatter(0, 2, WHOLE, third_dense)
+
         new_operand("ds", 1)
         new_operand("pw", 1)
-        nc.scalar.activation(as_grouped("pw", 1, WHOLE), as_planar(neg_pw[1], WHOLE), ACT.Copy, scale=-1.0)
+        group_pw(1)
         planar_ds = reuse.tile([P, PACK, N], BF16, name="planar_ds")
-        for t in range(PACK):
-            nc.gpsimd.tensor_tensor(planar_ds[:, t, :], slope[1][:, t, :], neg_pw[1][:, t, :], ALU.mult)
+        for cols in HALVES:
+            for t in range(PACK):
+                nc.gpsimd.tensor_tensor(planar_ds[:, t, cols], slope[1][:, t, cols], neg_pw[1][:, t, cols], ALU.mult)
+
+        def group_ds(cols):
+            nc.scalar.copy(as_grouped("ds", 1, cols, run=4), as_planar(planar_ds, cols, run=4))
+            quantize("ds", 1, cols)
+
+        def rows_of_second(name, cols):
+            group_rows(name, 1, cols, as_planar(raw[(name, 1)], cols))
+            quantize(name, 1, cols)
+
         quantize("pw", 1, WHOLE)
         for name in ("qm", "dom"):
             new_operand(name, 1)
-        rows_half("qm", 1, 0)
+        rows_of_second("qm", HALVES[0])
         fourth_sums = sums(0, 3, "score_bank1")
-        scatter(0, 3, fourth_sums, "prob", HALVES[0])
-        rows_half("dom", 1, 0)
-        nc.scalar.copy(
-            grouped[("ds", 1)].rearrange("p (c e j) -> p c j e", e=4, j=PACK),
-            planar_ds[:].rearrange("p j (c e) -> p c j e", e=4),
-        )
-        quantize("ds", 1, WHOLE)
-        scatter(0, 3, fourth_sums, "slope", HALVES[1])
-        both = reuse.tile([P, 2, WIDTH // 2 * PACK], BF16, name="neg_pw", align_bytes=64)
-        for index, name in enumerate(("qm", "dom")):
-            late[(name, 1, HALVES[1].start)] = both[:, index, :]
-            rows_half(name, 1, 1)
+        scatter(0, 3, HALVES[0], copy_out(fourth_sums, HALVES[0], "prob"))
+        group_ds(HALVES[0])
+        rows_of_second("dom", HALVES[0])
+        group_ds(HALVES[1])
+        scatter(0, 3, HALVES[1], copy_out(fourth_sums, HALVES[1], "slope"))
 
+        last_halves = reused([P, 2, WIDTH // 2 * PACK], BF16, "neg_pw")
+        late_rows = ("qm", "dom")
         for k in range(D // P):
-            gradient(1, k, "shared_bank%d" % k, "dense%d" % k)
+            if k < len(late_rows):
+                grouped_apart[(late_rows[k], 1, HALVES[1].start)] = last_halves[:, k, :]
+                rows_of_second(late_rows[k], HALVES[1])
+            scatter(1, k, WHOLE, copy_out(sums(1, k, shared_banks[k]), WHOLE, "dense%d" % k))
             nc.sync.dma_start(out[P * k : P * (k + 1), :], windows[k][:])

@@ -114,11 +114,11 @@ def tile_attend_gat_sig_c_kernel(tc, qT, cT, doT, rw, qm, dom, offs, out):
         codes = {}
         scales = {}
 
-        def new_operand(name, b, buffer=None):
+        def new_operand(name, b, buffer=None, codes_buffer=None):
             if buffer is None:
                 buffer = ring.tile([P, WIDTH * PACK], BF16, name="grouped", align_bytes=64)[:]
             grouped[(name, b)] = buffer
-            codes[(name, b)] = keep.tile([P, WIDTH], U32, name="%s%d_codes" % (name, b), align_bytes=64)
+            codes[(name, b)] = reused([P, WIDTH], U32, codes_buffer or "%s%d_codes" % (name, b))
             scales[(name, b)] = keep.tile([P, WIDTH], U8, name="%s%d_scales" % (name, b), align_bytes=64)
 
         def grouped_columns(name, b, cols):
@@ -277,40 +277,37 @@ def tile_attend_gat_sig_c_kernel(tc, qT, cT, doT, rw, qm, dom, offs, out):
         scores(1)
         third_dense = copy_out(third_sums, WHOLE, "chunk1")
         slopes(1, [gated_on_gpsimd] * PACK, shared_banks[:3] + ["score_bank0"])
+
         scatter(0, 2, WHOLE, third_dense)
-
-        new_operand("ds", 1)
-        new_operand("pw", 1)
-        group_pw(1)
+        qm_grouped = ring.tile([P, WIDTH * PACK], BF16, name="grouped", align_bytes=64)
+        grouped[("qm", 1)] = qm_grouped[:]
+        group_rows("qm", 1, HALVES[0], as_planar(raw[("qm", 1)], HALVES[0]))
+        fourth_sums = sums(0, 3, "score_bank1")
+        scatter(0, 3, HALVES[0], copy_out(fourth_sums, HALVES[0], "fourth_half"))
+        new_operand("qm", 1, qm_grouped[:], "fourth_half")
         planar_ds = reuse.tile([P, PACK, N], BF16, name="planar_ds")
-        for cols in HALVES:
-            for t in range(PACK):
-                nc.gpsimd.tensor_tensor(planar_ds[:, t, cols], slope[1][:, t, cols], neg_pw[1][:, t, cols], ALU.mult)
-
-        def group_ds(cols):
-            nc.scalar.copy(as_grouped("ds", 1, cols, run=4), as_planar(planar_ds, cols, run=4))
-            quantize("ds", 1, cols)
+        for t in range(PACK):
+            nc.gpsimd.tensor_tensor(planar_ds[:, t, :], slope[1][:, t, :], neg_pw[1][:, t, :], ALU.mult)
 
         def rows_of_second(name, cols):
             group_rows(name, 1, cols, as_planar(raw[(name, 1)], cols))
             quantize(name, 1, cols)
 
-        quantize("pw", 1, WHOLE)
-        for name in ("qm", "dom"):
+        for name in ("ds", "pw", "dom"):
             new_operand(name, 1)
-        rows_of_second("qm", HALVES[0])
-        fourth_sums = sums(0, 3, "score_bank1")
-        scatter(0, 3, HALVES[0], copy_out(fourth_sums, HALVES[0], "prob"))
-        group_ds(HALVES[0])
+        quantize("qm", 1, HALVES[0])
+        group_pw(1)
+        quantize("pw", 1, WHOLE)
         rows_of_second("dom", HALVES[0])
-        group_ds(HALVES[1])
-        scatter(0, 3, HALVES[1], copy_out(fourth_sums, HALVES[1], "slope"))
+        rows_of_second("qm", HALVES[1])
+        for cols in HALVES:
+            nc.scalar.copy(as_grouped("ds", 1, cols, run=4), as_planar(planar_ds, cols, run=4))
+            quantize("ds", 1, cols)
 
-        last_halves = reused([P, 2, WIDTH // 2 * PACK], BF16, "neg_pw")
-        late_rows = ("qm", "dom")
+        scatter(0, 3, HALVES[1], copy_out(fourth_sums, HALVES[1], "slope"))
+        grouped_apart[("dom", 1, HALVES[1].start)] = reused([P, WIDTH // 2 * PACK], BF16, "neg_pw")[:]
+        rows_of_second("dom", HALVES[1])
+
         for k in range(D // P):
-            if k < len(late_rows):
-                grouped_apart[(late_rows[k], 1, HALVES[1].start)] = last_halves[:, k, :]
-                rows_of_second(late_rows[k], HALVES[1])
             scatter(1, k, WHOLE, copy_out(sums(1, k, shared_banks[k]), WHOLE, "dense%d" % k))
             nc.sync.dma_start(out[P * k : P * (k + 1), :], windows[k][:])

@@ -26,8 +26,9 @@ WHOLE = slice(0, WIDTH)
 HALVES = (slice(0, WIDTH // 2), slice(WIDTH // 2, WIDTH))
 FORMAT = {"q": E4M3, "latent": E4M3, "do": E5M2, "qm": E4M3, "ds": E5M2, "dom": E5M2, "pw": E4M3}
 
-LAST_CHUNK_ON_VECTOR = 640
-GROUPED_BUFFERS = 7
+POOL_LOADS = ((0, 0, CHUNK), (0, CHUNK, T), (1, 0, CHUNK), (1, CHUNK, T - T // 8), (1, T - T // 8, T))
+VECTOR_SHARE = (5, 8)
+BLOCKS = tuple(slice(P * k, P * (k + 1)) for k in range(WIDTH // P))
 
 
 def tile_attend_gat_sig_c_kernel(tc, qT, cT, doT, rw, qm, dom, offs, out):
@@ -36,7 +37,6 @@ def tile_attend_gat_sig_c_kernel(tc, qT, cT, doT, rw, qm, dom, offs, out):
     with ExitStack() as ctx:
         keep = ctx.enter_context(tc.tile_pool(name="keep", bufs=1))
         reuse = ctx.enter_context(tc.tile_pool(name="reuse", bufs=1))
-        ring = ctx.enter_context(tc.tile_pool(name="ring", bufs=GROUPED_BUFFERS))
         psum = ctx.enter_context(tc.psum_pool(name="psum", bufs=1))
 
         def reused(shape, dtype, buffer_name):
@@ -50,11 +50,11 @@ def tile_attend_gat_sig_c_kernel(tc, qT, cT, doT, rw, qm, dom, offs, out):
         offsets = keep.tile([P, B * N // SLOTS_PER_COLUMN], U16, name="offsets")
 
         pool_rows = cT.rearrange("(p u e) c -> u p e c", u=2, e=2)
-        chunks = [[reused([P, 2, CHUNK], F32, "chunk%d" % (2 * u + h)) for h in range(2)] for u in range(2)]
-        for u in range(2):
-            for h in range(2):
-                nc.sync.dma_start(chunks[u][h][:], pool_rows[u][:, :, CHUNK * h : CHUNK * (h + 1)])
-            if u == 0:
+        chunks = {}
+        for index, (u, first, stop) in enumerate(POOL_LOADS):
+            chunks[index] = reused([P, 2, stop - first], F32, "chunk%d" % index)
+            nc.sync.dma_start(chunks[index][:], pool_rows[u][:, :, first:stop])
+            if index == 1:
                 nc.sync.dma_start(offsets[:], offs)
 
         raw = {}
@@ -64,25 +64,25 @@ def tile_attend_gat_sig_c_kernel(tc, qT, cT, doT, rw, qm, dom, offs, out):
             nc.sync.dma_start(raw[key][:], src.rearrange("(p j) c -> p j c", j=PACK))
 
         load(("q", 0), qT[0], "q0")
-        load(("do", 0), doT[0], "do0")
-        gate = keep.tile([P, B, PACK], F32, name="gate")
+        load(("do", 0), doT[0], "prob")
+        gate = reused([P, B, PACK], F32, "gate")
         nc.sync.dma_start(gate[:], rw.rearrange("b (p t) o -> p b (t o)", t=PACK))
-        for half, cols in enumerate(HALVES):
-            load(("qm", 0, half), qm[0][:, cols], "qm0_half%d" % half)
-            load(("dom", 0, half), dom[0][:, cols], "dom0_half%d" % half)
+        load(("qm", 0), qm[0], "qm0")
+        load(("dom", 0), dom[0], "dom0")
         for index, (name, src) in enumerate((("q", qT), ("do", doT), ("qm", qm), ("dom", dom))):
             load((name, 1), src[1], "chunk%d" % index)
 
         warm_up = keep.tile([P, 1], F32, name="warm_up")
-        nc.scalar.activation(warm_up[:], chunks[0][0][:, 0, 0:1], ACT.Sigmoid)
+        nc.scalar.activation(warm_up[:], chunks[0][:, 0, 0:1], ACT.Sigmoid)
 
         pairs = [keep.tile([P, T, 2], BF16, name="pairs%d" % u) for u in range(2)]
         picked_row = keep.tile([P, 2 * B * N], U32, name="picked", align_bytes=64)
         picked = picked_row[:].rearrange("p (u c) -> p u c", u=2)
 
-        def pair_up(u, h, first, stop, move):
-            src = chunks[u][h][:, :, first:stop]
-            dst = pairs[u][:, CHUNK * h + first : CHUNK * h + stop, :]
+        def pair_up(index, first, stop, move):
+            u, base = POOL_LOADS[index][:2]
+            src = chunks[index][:, :, first:stop]
+            dst = pairs[u][:, base + first : base + stop, :]
             move(dst.rearrange("p (c f) e -> p c e f", f=4), src.rearrange("p e (c f) -> p c e f", f=4))
 
         def list_columns(first_slot, count):
@@ -94,12 +94,18 @@ def tile_attend_gat_sig_c_kernel(tc, qT, cT, doT, rw, qm, dom, offs, out):
                 picked[:, u, first_slot : first_slot + count], words.indirect(list_columns(first_slot, count))
             )
 
-        pair_up(0, 0, 0, CHUNK, on_scalar)
-        pair_up(0, 1, 0, CHUNK, on_scalar)
+        def pair_up_shared(index, tokens):
+            split = tokens * VECTOR_SHARE[0] // VECTOR_SHARE[1]
+            pair_up(index, 0, split, on_vector)
+            pair_up(index, split, tokens, on_scalar)
+
+        pair_up(0, 0, CHUNK, on_scalar)
+        pair_up_shared(1, CHUNK)
         gather(0, 0, B * N)
-        pair_up(1, 0, 0, CHUNK, on_scalar)
-        pair_up(1, 1, 0, LAST_CHUNK_ON_VECTOR, on_vector)
-        pair_up(1, 1, LAST_CHUNK_ON_VECTOR, CHUNK, on_scalar)
+        pair_up(2, 0, 640, on_scalar)
+        pair_up(2, 640, CHUNK, on_vector)
+        pair_up_shared(3, CHUNK - T // 8)
+        pair_up_shared(4, T // 8)
         for cols in HALVES:
             gather(1, cols.start, N // 2)
 
@@ -109,22 +115,27 @@ def tile_attend_gat_sig_c_kernel(tc, qT, cT, doT, rw, qm, dom, offs, out):
         neg_gate = keep.tile([P, B, PACK], F32, name="neg_gate")
         nc.vector.tensor_scalar(neg_gate[:], gate[:], -1.0, None, ALU.mult)
 
-        grouped = {}
-        grouped_apart = {}
+        pieces = {}
         codes = {}
         scales = {}
 
-        def new_operand(name, b, buffer=None, codes_buffer=None):
-            if buffer is None:
-                buffer = ring.tile([P, WIDTH * PACK], BF16, name="grouped", align_bytes=64)[:]
-            grouped[(name, b)] = buffer
+        def new_grouped(name, b, cols, buffer):
+            pieces.setdefault((name, b), []).append((cols, buffer))
+
+        def grouped_buffer(width, buffer_name):
+            return reused([P, width * PACK], BF16, buffer_name)[:]
+
+        def new_codes(name, b, codes_buffer=None):
             codes[(name, b)] = reused([P, WIDTH], U32, codes_buffer or "%s%d_codes" % (name, b))
             scales[(name, b)] = keep.tile([P, WIDTH], U8, name="%s%d_scales" % (name, b), align_bytes=64)
 
+        def new_operand(name, b, buffer_name, codes_buffer=None):
+            new_grouped(name, b, WHOLE, grouped_buffer(WIDTH, buffer_name))
+            new_codes(name, b, codes_buffer)
+
         def grouped_columns(name, b, cols):
-            if (name, b, cols.start) in grouped_apart:
-                return grouped_apart[(name, b, cols.start)]
-            return grouped[(name, b)][:, PACK * cols.start : PACK * cols.stop]
+            held, buffer = [x for x in pieces[(name, b)] if x[0].start <= cols.start and cols.stop <= x[0].stop][0]
+            return buffer[:, PACK * (cols.start - held.start) : PACK * (cols.stop - held.start)]
 
         def as_grouped(name, b, cols, run=2):
             return grouped_columns(name, b, cols).rearrange("p (c e j) -> p c j e", e=run, j=PACK)
@@ -141,16 +152,25 @@ def tile_attend_gat_sig_c_kernel(tc, qT, cT, doT, rw, qm, dom, offs, out):
             nc.vector.tensor_copy(dst.bitcast(I32), src.bitcast(I32))
 
         def query_views(name, b):
-            dst = grouped[(name, b)].rearrange("p (h e m j) -> p h m j e", h=2, e=2, j=PACK)
+            dst = grouped_columns(name, b, WHOLE).rearrange("p (h e m j) -> p h m j e", h=2, e=2, j=PACK)
             src = raw[(name, b)][:].rearrange("p j (m h e) -> p h m j e", h=2, e=2)
             return dst, src
+
+        def query_half(name, b, h, move):
+            dst = grouped_columns(name, b, HALVES[h]).rearrange("p (e m j) -> p m j e", e=2, j=PACK)
+            move(dst, raw[(name, b)][:].rearrange("p j (m h e) -> p h m j e", h=2, e=2)[:, h])
 
         first_codes = reused([P, P], U32, "first_codes")
         first_scales = reused([P, P], U8, "first_scales")
 
+        late_scales = {}
+
         def quantized(name, b, cols):
-            if (name, b) == ("qm", 0) and cols.stop <= P:
+            if (name, b) == ("dom", 0) and cols.stop <= P:
                 return first_codes[:, cols].bitcast(FORMAT[name]), first_scales[:, cols]
+            if name == "q" and cols.start >= WIDTH // 2:
+                late = slice(cols.start - WIDTH // 2, cols.stop - WIDTH // 2)
+                return codes[(name, b)][:, cols].bitcast(FORMAT[name]), late_scales[b][:, late]
             return codes[(name, b)][:, cols].bitcast(FORMAT[name]), scales[(name, b)][:, cols]
 
         def quantize(name, b, cols):
@@ -207,84 +227,120 @@ def tile_attend_gat_sig_c_kernel(tc, qT, cT, doT, rw, qm, dom, offs, out):
 
         def sums(b, k, bank_name):
             bank = psum.tile([P, N], F32, name=bank_name)
-            product(bank, "dom", k, "pw", b, True, False)
-            product(bank, "qm", k, "ds", b, False, True)
+            first, last = (("qm", "ds"), ("dom", "pw")) if b == 0 else (("dom", "pw"), ("qm", "ds"))
+            product(bank, first[0], k, first[1], b, True, False)
+            product(bank, last[0], k, last[1], b, False, True)
             return bank
 
         def copy_out(bank, cols, buffer_name):
             dense = reused([P, cols.stop - cols.start], F32, buffer_name)
             on_scalar(dense[:], bank[:, cols])
-            return dense
+            return dense[:]
 
         def scatter(b, k, cols, dense):
             slots = list_columns(N * b + cols.start, cols.stop - cols.start)
-            nc.vector.tensor_copy(windows[k][:].indirect(slots), dense[:])
+            nc.vector.tensor_copy(windows[k][:].indirect(slots), dense)
 
         shared_banks = ["shared_bank%d" % t for t in range(PACK)]
 
-        for name in ("latent", "q", "do"):
-            new_operand(name, 0)
+        def rows(name, b, cols):
+            group_rows(name, b, cols, as_planar(raw[(name, b)], cols))
+
+        new_operand("latent", 0, "grouped_a")
         for cols in HALVES:
             group_latents(0, cols, words_on_vector)
         for cols in HALVES:
             quantize("latent", 0, cols)
-        for name, move in (("q", on_scalar), ("do", on_vector)):
-            dst, src = query_views(name, 0)
-            for h in range(2):
-                move(dst[:, h], src[:, h])
-            for cols in HALVES:
-                quantize(name, 0, cols)
+        gather(1, N, N)
+        new_grouped("q", 0, HALVES[0], grouped_buffer(WIDTH // 2, "grouped_b"))
+        new_grouped("q", 0, HALVES[1], grouped_buffer(WIDTH // 2, "grouped_d"))
+        new_codes("q", 0)
+        late_scales[0] = reused([P, WIDTH // 2], U8, "gate")
+        for h in range(2):
+            query_half("q", 0, h, on_scalar)
+        quantize("q", 0, HALVES[0])
+        new_operand("do", 0, "grouped_c")
+        dst, src = query_views("do", 0)
+        split = P * VECTOR_SHARE[0] // VECTOR_SHARE[1]
+        on_vector(dst[:, :, :split], src[:, :, :split])
+        nc.scalar.copy(dst[:, :, split:], src[:, :, split:])
+        quantize("q", 0, HALVES[1])
+        for cols in HALVES:
+            quantize("do", 0, cols)
+        new_grouped("latent", 1, WHOLE, grouped_buffer(WIDTH, "grouped_d"))
+        group_latents(1, WHOLE, words_on_vector)
         scores(0)
-        slopes(0, [gated_on_vector] * 2 + [gated_on_scalar] * 2, shared_banks)
+        slopes(0, [gated_on_gpsimd] * 2 + [gated_on_scalar, gated_on_gpsimd], shared_banks)
 
-        def rows_of_first(name, half, pieces):
-            group_rows(name, 0, HALVES[half], as_planar(raw[(name, 0, half)], HALVES[0]))
-            for cols in pieces:
-                quantize(name, 0, cols)
-
-        for name in ("qm", "dom"):
-            new_operand(name, 0)
-        rows_of_first("qm", 0, (slice(0, P), slice(P, 2 * P)))
-        new_operand("ds", 0)
-        new_operand("pw", 0)
+        new_grouped("qm", 0, BLOCKS[0], grouped_buffer(P, "grouped_b"))
+        new_grouped("dom", 0, BLOCKS[0], grouped_buffer(P, "grouped_c"))
+        new_codes("qm", 0)
+        new_codes("dom", 0)
+        new_operand("ds", 0, "grouped_a")
+        new_operand("pw", 0, "grouped_e")
+        rows("qm", 0, BLOCKS[0])
         nc.vector.tensor_tensor(
             as_grouped("ds", 0, WHOLE), as_planar(slope[0], WHOLE), as_planar(neg_pw[0], WHOLE), ALU.mult
         )
+        rows("dom", 0, BLOCKS[0])
         group_pw(0)
-        grouped_apart[("dom", 0, 0)] = picked_row[:, (2 * B - 1) * N :].bitcast(BF16)
-        rows_of_first("dom", 0, HALVES[:1])
-        quantize("pw", 0, WHOLE)
+        quantize("qm", 0, BLOCKS[0])
+        quantize("dom", 0, BLOCKS[0])
         quantize("ds", 0, WHOLE)
-        gather(1, N, N)
-        rows_of_first("qm", 1, HALVES[1:])
-        scatter(0, 0, WHOLE, copy_out(sums(0, 0, "shared_bank0"), WHOLE, "dense0"))
-        second_sums = sums(0, 1, "shared_bank0")
-
-        new_operand("latent", 1, reused([P, WIDTH * PACK], BF16, "first_codes")[:])
-        group_latents(1, WHOLE, nc.scalar.copy)
+        quantize("pw", 0, WHOLE)
+        first_sums = sums(0, 0, "shared_bank0")
+        first_dense = copy_out(first_sums, WHOLE, "dense0")
+        new_codes("latent", 1, "grouped_e")
         quantize("latent", 1, WHOLE)
-        rows_of_first("dom", 1, HALVES[1:])
-        new_operand("q", 1, reused([P, WIDTH * PACK], BF16, "first_scales")[:])
-        nc.scalar.copy(*query_views("q", 1))
-        quantize("q", 1, WHOLE)
-        scatter(0, 1, HALVES[0], copy_out(second_sums, HALVES[0], "dom0_half1"))
-        new_operand("do", 1)
-        nc.scalar.copy(*query_views("do", 1))
-        quantize("do", 1, WHOLE)
-        scatter(0, 1, HALVES[1], copy_out(second_sums, HALVES[1], "chunk0"))
+        second_blocks = grouped_buffer(2 * P, "slope")
+        for index, name in enumerate(("qm", "dom")):
+            new_grouped(name, 0, BLOCKS[1], second_blocks[:, PACK * P * index : PACK * P * (index + 1)])
+            rows(name, 0, BLOCKS[1])
+            quantize(name, 0, BLOCKS[1])
 
-        third_sums = sums(0, 2, shared_banks[3])
+        new_codes("q", 1)
+        new_grouped("q", 1, HALVES[0], grouped_buffer(WIDTH // 2, "grouped_b"))
+        query_half("q", 1, 0, on_scalar)
+        quantize("q", 1, HALVES[0])
+        second_halves = grouped_buffer(WIDTH, "grouped_b")
+        for index, name in enumerate(("dom", "qm")):
+            new_grouped(name, 0, HALVES[1], second_halves[:, 2 * WIDTH * index : 2 * WIDTH * (index + 1)])
+            nc.gpsimd.tensor_scalar(
+                as_grouped(name, 0, HALVES[1]), as_planar(raw[(name, 0)], HALVES[1]), 1.0, 0.0, ALU.mult, ALU.add
+            )
+        scatter(0, 0, WHOLE, first_dense)
+        new_grouped("q", 1, HALVES[1], grouped_buffer(WIDTH // 2, "first_codes"))
+        query_half("q", 1, 1, on_scalar)
+        for name in ("dom", "qm"):
+            quantize(name, 0, HALVES[1])
+        after_casts = reused([P, WIDTH // 2 + WIDTH], U8, "qm0")
+        late_scales[1] = after_casts[:, : WIDTH // 2]
+        quantize("q", 1, HALVES[1])
+        second_sums = sums(0, 1, "shared_bank0")
+        new_grouped("do", 1, WHOLE, grouped_buffer(WIDTH, "neg_pw"))
+        codes[("do", 1)] = reused([P, WIDTH], U32, "do1_codes")
+        scales[("do", 1)] = after_casts[:, WIDTH // 2 :]
+        for h in range(2):
+            query_half("do", 1, h, on_scalar)
+        quantize("do", 1, WHOLE)
+        scatter(0, 1, HALVES[0], copy_out(second_sums, HALVES[0], "grouped_b"))
+
         scores(1)
-        third_dense = copy_out(third_sums, WHOLE, "chunk1")
-        slopes(1, [gated_on_gpsimd] * PACK, shared_banks[:3] + ["score_bank0"])
+        after_scores = reused([P, 4 * N + N // 2], F32, "qm0")
+        third_dense = after_scores[:, :N]
+        second_rest = after_scores[:, N : N + N // 2]
+        rows_of_qm = after_scores[:, N + N // 2 : 3 * N + N // 2].bitcast(BF16)
+        rows_of_dom = after_scores[:, 3 * N + N // 2 :].bitcast(BF16)
+        on_scalar(second_rest, second_sums[:, HALVES[1]])
+        slopes(1, [gated_on_gpsimd] * PACK, shared_banks[1:] + ["score_bank0"])
+        on_scalar(third_dense, sums(0, 2, "score_bank2")[:])
+        scatter(0, 1, HALVES[1], second_rest)
 
         scatter(0, 2, WHOLE, third_dense)
-        qm_grouped = ring.tile([P, WIDTH * PACK], BF16, name="grouped", align_bytes=64)
-        grouped[("qm", 1)] = qm_grouped[:]
+        new_grouped("qm", 1, WHOLE, rows_of_qm)
         group_rows("qm", 1, HALVES[0], as_planar(raw[("qm", 1)], HALVES[0]))
-        fourth_sums = sums(0, 3, "score_bank1")
+        fourth_sums = sums(0, 3, "score_bank3")
         scatter(0, 3, HALVES[0], copy_out(fourth_sums, HALVES[0], "fourth_half"))
-        new_operand("qm", 1, qm_grouped[:], "fourth_half")
         planar_ds = reuse.tile([P, PACK, N], BF16, name="planar_ds")
         for t in range(PACK):
             nc.gpsimd.tensor_tensor(planar_ds[:, t, :], slope[1][:, t, :], neg_pw[1][:, t, :], ALU.mult)
@@ -293,20 +349,26 @@ def tile_attend_gat_sig_c_kernel(tc, qT, cT, doT, rw, qm, dom, offs, out):
             group_rows(name, 1, cols, as_planar(raw[(name, 1)], cols))
             quantize(name, 1, cols)
 
-        for name in ("ds", "pw", "dom"):
-            new_operand(name, 1)
-        quantize("qm", 1, HALVES[0])
+        new_operand("ds", 1, "grouped_c")
+        new_operand("pw", 1, "grouped_d")
+        new_grouped("dom", 1, HALVES[0], rows_of_dom)
+        new_codes("dom", 1)
         group_pw(1)
         quantize("pw", 1, WHOLE)
         rows_of_second("dom", HALVES[0])
-        rows_of_second("qm", HALVES[1])
+        new_codes("qm", 1, "neg_pw")
+        quantize("qm", 1, HALVES[0])
         for cols in HALVES:
             nc.scalar.copy(as_grouped("ds", 1, cols, run=4), as_planar(planar_ds, cols, run=4))
             quantize("ds", 1, cols)
 
-        scatter(0, 3, HALVES[1], copy_out(fourth_sums, HALVES[1], "slope"))
-        grouped_apart[("dom", 1, HALVES[1].start)] = reused([P, WIDTH // 2 * PACK], BF16, "neg_pw")[:]
-        rows_of_second("dom", HALVES[1])
+        after_gpsimd = reused([P, N + N // 2], F32, "slope")
+        late_rows = after_gpsimd[:, N // 2 :].bitcast(BF16)
+        on_scalar(after_gpsimd[:, : N // 2], fourth_sums[:, HALVES[1]])
+        scatter(0, 3, HALVES[1], after_gpsimd[:, : N // 2])
+        new_grouped("dom", 1, HALVES[1], late_rows)
+        for name in ("dom", "qm"):
+            rows_of_second(name, HALVES[1])
 
         for k in range(D // P):
             scatter(1, k, WHOLE, copy_out(sums(1, k, shared_banks[k]), WHOLE, "dense%d" % k))

@@ -26,7 +26,7 @@ WHOLE = slice(0, WIDTH)
 HALVES = (slice(0, WIDTH // 2), slice(WIDTH // 2, WIDTH))
 FORMAT = {"q": E4M3, "latent": E4M3, "do": E5M2, "qm": E4M3, "ds": E5M2, "dom": E5M2, "pw": E4M3}
 
-POOL_LOADS = ((0, 0, CHUNK), (0, CHUNK, T), (1, 0, CHUNK), (1, CHUNK, T - T // 8), (1, T - T // 8, T))
+POOL_LOADS = ((0, 0, T), (1, 0, CHUNK), (1, CHUNK, T - T // 8), (1, T - T // 8, T))
 VECTOR_SHARE = (5, 8)
 BLOCKS = tuple(slice(P * k, P * (k + 1)) for k in range(WIDTH // P))
 
@@ -54,7 +54,7 @@ def tile_attend_gat_sig_c_kernel(tc, qT, cT, doT, rw, qm, dom, offs, out):
         for index, (u, first, stop) in enumerate(POOL_LOADS):
             chunks[index] = reused([P, 2, stop - first], F32, "chunk%d" % index)
             nc.sync.dma_start(chunks[index][:], pool_rows[u][:, :, first:stop])
-            if index == 1:
+            if index == 0:
                 nc.sync.dma_start(offsets[:], offs)
 
         raw = {}
@@ -65,10 +65,11 @@ def tile_attend_gat_sig_c_kernel(tc, qT, cT, doT, rw, qm, dom, offs, out):
 
         load(("q", 0), qT[0], "q0")
         load(("do", 0), doT[0], "prob")
-        gate = reused([P, B, PACK], F32, "gate")
+        gate = keep.tile([P, B, PACK], F32, name="gate")
         nc.sync.dma_start(gate[:], rw.rearrange("b (p t) o -> p b (t o)", t=PACK))
         load(("qm", 0), qm[0], "qm0")
-        load(("dom", 0), dom[0], "dom0")
+        for half, cols in enumerate(HALVES):
+            load(("dom", 0, half), dom[0][:, cols], "dom0_half%d" % half)
         for index, (name, src) in enumerate((("q", qT), ("do", doT), ("qm", qm), ("dom", dom))):
             load((name, 1), src[1], "chunk%d" % index)
 
@@ -76,8 +77,8 @@ def tile_attend_gat_sig_c_kernel(tc, qT, cT, doT, rw, qm, dom, offs, out):
         nc.scalar.activation(warm_up[:], chunks[0][:, 0, 0:1], ACT.Sigmoid)
 
         pairs = [keep.tile([P, T, 2], BF16, name="pairs%d" % u) for u in range(2)]
-        picked_row = keep.tile([P, 2 * B * N], U32, name="picked", align_bytes=64)
-        picked = picked_row[:].rearrange("p (u c) -> p u c", u=2)
+        picked_row = keep.tile([P, 2 * B * N + 3 * N // 2], U32, name="picked", align_bytes=64)
+        picked = picked_row[:, : 2 * B * N].rearrange("p (u c) -> p u c", u=2)
 
         def pair_up(index, first, stop, move):
             u, base = POOL_LOADS[index][:2]
@@ -99,13 +100,12 @@ def tile_attend_gat_sig_c_kernel(tc, qT, cT, doT, rw, qm, dom, offs, out):
             pair_up(index, 0, split, on_vector)
             pair_up(index, split, tokens, on_scalar)
 
-        pair_up(0, 0, CHUNK, on_scalar)
-        pair_up_shared(1, CHUNK)
+        pair_up(0, 0, 1376, on_vector)
+        pair_up(0, 1376, T, on_scalar)
         gather(0, 0, B * N)
-        pair_up(2, 0, 640, on_scalar)
-        pair_up(2, 640, CHUNK, on_vector)
-        pair_up_shared(3, CHUNK - T // 8)
-        pair_up_shared(4, T // 8)
+        pair_up(1, 0, CHUNK, on_scalar)
+        pair_up(2, 0, CHUNK - T // 8, on_vector)
+        pair_up_shared(3, T // 8)
         for cols in HALVES:
             gather(1, cols.start, N // 2)
 
@@ -161,14 +161,17 @@ def tile_attend_gat_sig_c_kernel(tc, qT, cT, doT, rw, qm, dom, offs, out):
             move(dst, raw[(name, b)][:].rearrange("p j (m h e) -> p h m j e", h=2, e=2)[:, h])
 
         first_codes = reused([P, P], U32, "first_codes")
-        first_scales = reused([P, P], U8, "first_scales")
+        first_scales = []
 
         late_scales = {}
+        last_codes = []
 
         def quantized(name, b, cols):
             if (name, b) == ("dom", 0) and cols.stop <= P:
-                return first_codes[:, cols].bitcast(FORMAT[name]), first_scales[:, cols]
-            if name == "q" and cols.start >= WIDTH // 2:
+                return first_codes[:, cols].bitcast(FORMAT[name]), first_scales[0][:, cols]
+            if (name, b) == ("qm", 1) and cols.stop <= P:
+                return last_codes[0][:, cols].bitcast(FORMAT[name]), scales[(name, b)][:, cols]
+            if (name, b) == ("q", 1) and cols.start >= WIDTH // 2:
                 late = slice(cols.start - WIDTH // 2, cols.stop - WIDTH // 2)
                 return codes[(name, b)][:, cols].bitcast(FORMAT[name]), late_scales[b][:, late]
             return codes[(name, b)][:, cols].bitcast(FORMAT[name]), scales[(name, b)][:, cols]
@@ -243,70 +246,77 @@ def tile_attend_gat_sig_c_kernel(tc, qT, cT, doT, rw, qm, dom, offs, out):
 
         shared_banks = ["shared_bank%d" % t for t in range(PACK)]
 
+        def planar_rows(name, b, cols):
+            if (name, b) == ("dom", 0):
+                half, first = divmod(cols.start, WIDTH // 2)
+                return as_planar(raw[(name, b, half)], slice(first, first + cols.stop - cols.start))
+            return as_planar(raw[(name, b)], cols)
+
         def rows(name, b, cols):
-            group_rows(name, b, cols, as_planar(raw[(name, b)], cols))
+            group_rows(name, b, cols, planar_rows(name, b, cols))
 
         new_operand("latent", 0, "grouped_a")
         for cols in HALVES:
             group_latents(0, cols, words_on_vector)
         for cols in HALVES:
             quantize("latent", 0, cols)
-        gather(1, N, N)
-        new_grouped("q", 0, HALVES[0], grouped_buffer(WIDTH // 2, "grouped_b"))
-        new_grouped("q", 0, HALVES[1], grouped_buffer(WIDTH // 2, "grouped_d"))
-        new_codes("q", 0)
-        late_scales[0] = reused([P, WIDTH // 2], U8, "gate")
-        for h in range(2):
-            query_half("q", 0, h, on_scalar)
-        quantize("q", 0, HALVES[0])
-        new_operand("do", 0, "grouped_c")
+        gather(1, N, N // 2)
+        new_operand("q", 0, "grouped_b")
+        query_half("q", 0, 0, on_vector)
+        query_half("q", 0, 1, on_scalar)
+        for cols in HALVES:
+            quantize("q", 0, cols)
+        new_grouped("do", 0, WHOLE, picked_row[:, 2 * B * N - N // 2 :].bitcast(BF16))
+        new_codes("do", 0)
         dst, src = query_views("do", 0)
         split = P * VECTOR_SHARE[0] // VECTOR_SHARE[1]
         on_vector(dst[:, :, :split], src[:, :, :split])
         nc.scalar.copy(dst[:, :, split:], src[:, :, split:])
-        quantize("q", 0, HALVES[1])
         for cols in HALVES:
             quantize("do", 0, cols)
-        new_grouped("latent", 1, WHOLE, grouped_buffer(WIDTH, "grouped_d"))
-        group_latents(1, WHOLE, words_on_vector)
+        gather(1, N + N // 2, N // 2)
         scores(0)
-        slopes(0, [gated_on_gpsimd] * 2 + [gated_on_scalar, gated_on_gpsimd], shared_banks)
-
         new_grouped("qm", 0, BLOCKS[0], grouped_buffer(P, "grouped_b"))
+        rows("qm", 0, BLOCKS[0])
+        slopes(0, [gated_on_gpsimd] * 3 + [gated_on_scalar], shared_banks)
+
         new_grouped("dom", 0, BLOCKS[0], grouped_buffer(P, "grouped_c"))
+        first_scales.append(reused([P, P], U8, "prob"))
         new_codes("qm", 0)
         new_codes("dom", 0)
         new_operand("ds", 0, "grouped_a")
         new_operand("pw", 0, "grouped_e")
-        rows("qm", 0, BLOCKS[0])
+        quantize("qm", 0, BLOCKS[0])
         nc.vector.tensor_tensor(
             as_grouped("ds", 0, WHOLE), as_planar(slope[0], WHOLE), as_planar(neg_pw[0], WHOLE), ALU.mult
         )
         rows("dom", 0, BLOCKS[0])
         group_pw(0)
-        quantize("qm", 0, BLOCKS[0])
         quantize("dom", 0, BLOCKS[0])
         quantize("ds", 0, WHOLE)
         quantize("pw", 0, WHOLE)
         first_sums = sums(0, 0, "shared_bank0")
         first_dense = copy_out(first_sums, WHOLE, "dense0")
-        new_codes("latent", 1, "grouped_e")
-        quantize("latent", 1, WHOLE)
+        after_ds = grouped_buffer(WIDTH + WIDTH // 2, "grouped_a")
+        new_grouped("latent", 1, WHOLE, after_ds[:, : PACK * WIDTH])
+        new_codes("latent", 1)
+        group_latents(1, WHOLE, words_on_vector)
         second_blocks = grouped_buffer(2 * P, "slope")
         for index, name in enumerate(("qm", "dom")):
             new_grouped(name, 0, BLOCKS[1], second_blocks[:, PACK * P * index : PACK * P * (index + 1)])
             rows(name, 0, BLOCKS[1])
             quantize(name, 0, BLOCKS[1])
 
+        quantize("latent", 1, WHOLE)
         new_codes("q", 1)
-        new_grouped("q", 1, HALVES[0], grouped_buffer(WIDTH // 2, "grouped_b"))
+        new_grouped("q", 1, HALVES[0], after_ds[:, PACK * WIDTH :])
         query_half("q", 1, 0, on_scalar)
         quantize("q", 1, HALVES[0])
-        second_halves = grouped_buffer(WIDTH, "grouped_b")
+        second_halves = grouped_buffer(WIDTH, "grouped_a")
         for index, name in enumerate(("dom", "qm")):
             new_grouped(name, 0, HALVES[1], second_halves[:, 2 * WIDTH * index : 2 * WIDTH * (index + 1)])
             nc.gpsimd.tensor_scalar(
-                as_grouped(name, 0, HALVES[1]), as_planar(raw[(name, 0)], HALVES[1]), 1.0, 0.0, ALU.mult, ALU.add
+                as_grouped(name, 0, HALVES[1]), planar_rows(name, 0, HALVES[1]), 1.0, 0.0, ALU.mult, ALU.add
             )
         scatter(0, 0, WHOLE, first_dense)
         new_grouped("q", 1, HALVES[1], grouped_buffer(WIDTH // 2, "first_codes"))
@@ -323,27 +333,43 @@ def tile_attend_gat_sig_c_kernel(tc, qT, cT, doT, rw, qm, dom, offs, out):
         for h in range(2):
             query_half("do", 1, h, on_scalar)
         quantize("do", 1, WHOLE)
-        scatter(0, 1, HALVES[0], copy_out(second_sums, HALVES[0], "grouped_b"))
+        after_quantising = reused([P, N // 2 + N], F32, "grouped_a")
+        second_first, less_one = after_quantising[:, : N // 2], after_quantising[:, N // 2 :]
+        on_scalar(second_first, second_sums[:, HALVES[0]])
+        scatter(0, 1, HALVES[0], second_first)
 
         scores(1)
-        after_scores = reused([P, 4 * N + N // 2], F32, "qm0")
+        after_scores = reused([P, 3 * N + N // 2], F32, "qm0")
         third_dense = after_scores[:, :N]
         second_rest = after_scores[:, N : N + N // 2]
-        rows_of_qm = after_scores[:, N + N // 2 : 3 * N + N // 2].bitcast(BF16)
-        rows_of_dom = after_scores[:, 3 * N + N // 2 :].bitcast(BF16)
+        rows_of_qm = after_scores[:, N + N // 2 : 2 * N + N // 2].bitcast(BF16)
+        rows_of_dom = after_scores[:, 2 * N + N // 2 :].bitcast(BF16)
+        neg_pw[1] = reused([P, PACK, N], F32, "neg_pw")
+        slope[1] = reused([P, PACK, N], F32, "slope")
+        dp_banks = {}
+        for t, bank_name in ((1, shared_banks[2]), (0, shared_banks[1]), (2, shared_banks[3]), (3, "score_bank0")):
+            dp_banks[t] = psum.tile([P, N], F32, name=bank_name)
+            product(dp_banks[t], "do", t, "latent", 1, True, True)
+        gated_on_gpsimd(neg_pw[1][:, 0, :], prob[1][:, 0, :], neg_gate[:, 1, 0:1])
+        nc.scalar.activation(less_one, prob[1][:, 0, :], ACT.Copy, bias=-1.0)
+        nc.gpsimd.tensor_tensor(slope[1][:, 0, :], less_one, neg_pw[1][:, 0, :], ALU.mult)
+        first_dp = copy_out(dp_banks[0], WHOLE, "first_dp")
         on_scalar(second_rest, second_sums[:, HALVES[1]])
-        slopes(1, [gated_on_gpsimd] * PACK, shared_banks[1:] + ["score_bank0"])
+        for t in range(1, PACK):
+            bank = dp_banks[t]
+            (gated_on_gpsimd if t < 3 else gated_on_scalar)(neg_pw[1][:, t, :], prob[1][:, t, :], neg_gate[:, 1, t : t + 1])
+            nc.vector.scalar_tensor_tensor(slope[1][:, t, :], prob[1][:, t, :], 1.0, bank[:], ALU.subtract, ALU.mult)
         on_scalar(third_dense, sums(0, 2, "score_bank2")[:])
         scatter(0, 1, HALVES[1], second_rest)
 
         scatter(0, 2, WHOLE, third_dense)
-        new_grouped("qm", 1, WHOLE, rows_of_qm)
+        new_grouped("qm", 1, HALVES[0], rows_of_qm)
         group_rows("qm", 1, HALVES[0], as_planar(raw[("qm", 1)], HALVES[0]))
         fourth_sums = sums(0, 3, "score_bank3")
         scatter(0, 3, HALVES[0], copy_out(fourth_sums, HALVES[0], "fourth_half"))
         planar_ds = reuse.tile([P, PACK, N], BF16, name="planar_ds")
-        for t in range(PACK):
-            nc.gpsimd.tensor_tensor(planar_ds[:, t, :], slope[1][:, t, :], neg_pw[1][:, t, :], ALU.mult)
+        nc.gpsimd.tensor_tensor(planar_ds[:, 0, :], slope[1][:, 0, :], first_dp, ALU.mult)
+        nc.gpsimd.tensor_tensor(planar_ds[:, 1:, :], slope[1][:, 1:, :], neg_pw[1][:, 1:, :], ALU.mult)
 
         def rows_of_second(name, cols):
             group_rows(name, 1, cols, as_planar(raw[(name, 1)], cols))
@@ -356,20 +382,24 @@ def tile_attend_gat_sig_c_kernel(tc, qT, cT, doT, rw, qm, dom, offs, out):
         group_pw(1)
         quantize("pw", 1, WHOLE)
         rows_of_second("dom", HALVES[0])
-        new_codes("qm", 1, "neg_pw")
-        quantize("qm", 1, HALVES[0])
+        new_codes("qm", 1, "first_dp")
+        last_codes.append(reused([P, P], U32, "neg_pw"))
+        quantize("qm", 1, BLOCKS[1])
+        quantize("qm", 1, BLOCKS[0])
+        after_gpsimd = reused([P, N + N // 2], F32, "slope")
+        late_rows = after_gpsimd[:, N // 2 :].bitcast(BF16)
         for cols in HALVES:
             nc.scalar.copy(as_grouped("ds", 1, cols, run=4), as_planar(planar_ds, cols, run=4))
             quantize("ds", 1, cols)
 
-        after_gpsimd = reused([P, N + N // 2], F32, "slope")
-        late_rows = after_gpsimd[:, N // 2 :].bitcast(BF16)
         on_scalar(after_gpsimd[:, : N // 2], fourth_sums[:, HALVES[1]])
         scatter(0, 3, HALVES[1], after_gpsimd[:, : N // 2])
         new_grouped("dom", 1, HALVES[1], late_rows)
-        for name in ("dom", "qm"):
-            rows_of_second(name, HALVES[1])
+        rows_of_second("dom", HALVES[1])
 
         for k in range(D // P):
             scatter(1, k, WHOLE, copy_out(sums(1, k, shared_banks[k]), WHOLE, "dense%d" % k))
             nc.sync.dma_start(out[P * k : P * (k + 1), :], windows[k][:])
+            if k == 0:
+                new_grouped("qm", 1, HALVES[1], grouped_buffer(WIDTH // 2, "neg_pw"))
+                rows_of_second("qm", HALVES[1])

@@ -28,6 +28,7 @@ FORMAT = {"q": E4M3, "latent": E4M3, "do": E5M2, "qm": E4M3, "ds": E5M2, "dom": 
 
 POOL_LOADS = ((0, 0, T), (1, 0, CHUNK), (1, CHUNK, T - T // 8), (1, T - T // 8, T))
 VECTOR_SHARE = (5, 8)
+DO_COLUMNS_ON_VECTOR = 84
 BLOCKS = tuple(slice(P * k, P * (k + 1)) for k in range(WIDTH // P))
 
 
@@ -164,13 +165,10 @@ def tile_attend_gat_sig_c_kernel(tc, qT, cT, doT, rw, qm, dom, offs, out):
         first_scales = []
 
         late_scales = {}
-        last_codes = []
 
         def quantized(name, b, cols):
             if (name, b) == ("dom", 0) and cols.stop <= P:
                 return first_codes[:, cols].bitcast(FORMAT[name]), first_scales[0][:, cols]
-            if (name, b) == ("qm", 1) and cols.stop <= P:
-                return last_codes[0][:, cols].bitcast(FORMAT[name]), scales[(name, b)][:, cols]
             if (name, b) == ("q", 1) and cols.start >= WIDTH // 2:
                 late = slice(cols.start - WIDTH // 2, cols.stop - WIDTH // 2)
                 return codes[(name, b)][:, cols].bitcast(FORMAT[name]), late_scales[b][:, late]
@@ -256,20 +254,22 @@ def tile_attend_gat_sig_c_kernel(tc, qT, cT, doT, rw, qm, dom, offs, out):
             group_rows(name, b, cols, planar_rows(name, b, cols))
 
         new_operand("latent", 0, "grouped_a")
-        for cols in HALVES:
-            group_latents(0, cols, words_on_vector)
+        gather(1, N, N // 2)
+        group_latents(0, HALVES[0], nc.scalar.copy)
+        group_latents(0, HALVES[1], words_on_vector)
         for cols in HALVES:
             quantize("latent", 0, cols)
-        gather(1, N, N // 2)
         new_operand("q", 0, "grouped_b")
-        query_half("q", 0, 0, on_vector)
-        query_half("q", 0, 1, on_scalar)
+        dst, src = query_views("q", 0)
+        on_vector(dst[:, 0, : P // 2], src[:, 0, : P // 2])
+        on_scalar(dst[:, 0, P // 2 :], src[:, 0, P // 2 :])
+        on_scalar(dst[:, 1], src[:, 1])
         for cols in HALVES:
             quantize("q", 0, cols)
         new_grouped("do", 0, WHOLE, picked_row[:, 2 * B * N - N // 2 :].bitcast(BF16))
         new_codes("do", 0)
         dst, src = query_views("do", 0)
-        split = P * VECTOR_SHARE[0] // VECTOR_SHARE[1]
+        split = DO_COLUMNS_ON_VECTOR
         on_vector(dst[:, :, :split], src[:, :, :split])
         nc.scalar.copy(dst[:, :, split:], src[:, :, split:])
         for cols in HALVES:
@@ -333,43 +333,27 @@ def tile_attend_gat_sig_c_kernel(tc, qT, cT, doT, rw, qm, dom, offs, out):
         for h in range(2):
             query_half("do", 1, h, on_scalar)
         quantize("do", 1, WHOLE)
-        after_quantising = reused([P, N // 2 + N], F32, "grouped_a")
-        second_first, less_one = after_quantising[:, : N // 2], after_quantising[:, N // 2 :]
-        on_scalar(second_first, second_sums[:, HALVES[0]])
-        scatter(0, 1, HALVES[0], second_first)
+        scatter(0, 1, HALVES[0], copy_out(second_sums, HALVES[0], "grouped_a"))
 
         scores(1)
-        after_scores = reused([P, 3 * N + N // 2], F32, "qm0")
+        after_scores = reused([P, 4 * N + N // 2], F32, "qm0")
         third_dense = after_scores[:, :N]
         second_rest = after_scores[:, N : N + N // 2]
-        rows_of_qm = after_scores[:, N + N // 2 : 2 * N + N // 2].bitcast(BF16)
-        rows_of_dom = after_scores[:, 2 * N + N // 2 :].bitcast(BF16)
-        neg_pw[1] = reused([P, PACK, N], F32, "neg_pw")
-        slope[1] = reused([P, PACK, N], F32, "slope")
-        dp_banks = {}
-        for t, bank_name in ((1, shared_banks[2]), (0, shared_banks[1]), (2, shared_banks[3]), (3, "score_bank0")):
-            dp_banks[t] = psum.tile([P, N], F32, name=bank_name)
-            product(dp_banks[t], "do", t, "latent", 1, True, True)
-        gated_on_gpsimd(neg_pw[1][:, 0, :], prob[1][:, 0, :], neg_gate[:, 1, 0:1])
-        nc.scalar.activation(less_one, prob[1][:, 0, :], ACT.Copy, bias=-1.0)
-        nc.gpsimd.tensor_tensor(slope[1][:, 0, :], less_one, neg_pw[1][:, 0, :], ALU.mult)
-        first_dp = copy_out(dp_banks[0], WHOLE, "first_dp")
+        rows_of_qm = after_scores[:, N + N // 2 : 3 * N + N // 2].bitcast(BF16)
+        rows_of_dom = after_scores[:, 3 * N + N // 2 :].bitcast(BF16)
         on_scalar(second_rest, second_sums[:, HALVES[1]])
-        for t in range(1, PACK):
-            bank = dp_banks[t]
-            (gated_on_gpsimd if t < 3 else gated_on_scalar)(neg_pw[1][:, t, :], prob[1][:, t, :], neg_gate[:, 1, t : t + 1])
-            nc.vector.scalar_tensor_tensor(slope[1][:, t, :], prob[1][:, t, :], 1.0, bank[:], ALU.subtract, ALU.mult)
+        slopes(1, [gated_on_gpsimd] * PACK, shared_banks[1:] + ["score_bank0"])
         on_scalar(third_dense, sums(0, 2, "score_bank2")[:])
         scatter(0, 1, HALVES[1], second_rest)
 
         scatter(0, 2, WHOLE, third_dense)
-        new_grouped("qm", 1, HALVES[0], rows_of_qm)
+        new_grouped("qm", 1, WHOLE, rows_of_qm)
         group_rows("qm", 1, HALVES[0], as_planar(raw[("qm", 1)], HALVES[0]))
         fourth_sums = sums(0, 3, "score_bank3")
         scatter(0, 3, HALVES[0], copy_out(fourth_sums, HALVES[0], "fourth_half"))
         planar_ds = reuse.tile([P, PACK, N], BF16, name="planar_ds")
-        nc.gpsimd.tensor_tensor(planar_ds[:, 0, :], slope[1][:, 0, :], first_dp, ALU.mult)
-        nc.gpsimd.tensor_tensor(planar_ds[:, 1:, :], slope[1][:, 1:, :], neg_pw[1][:, 1:, :], ALU.mult)
+        for t in range(PACK):
+            nc.gpsimd.tensor_tensor(planar_ds[:, t, :], slope[1][:, t, :], neg_pw[1][:, t, :], ALU.mult)
 
         def rows_of_second(name, cols):
             group_rows(name, 1, cols, as_planar(raw[(name, 1)], cols))
@@ -382,24 +366,20 @@ def tile_attend_gat_sig_c_kernel(tc, qT, cT, doT, rw, qm, dom, offs, out):
         group_pw(1)
         quantize("pw", 1, WHOLE)
         rows_of_second("dom", HALVES[0])
-        new_codes("qm", 1, "first_dp")
-        last_codes.append(reused([P, P], U32, "neg_pw"))
-        quantize("qm", 1, BLOCKS[1])
-        quantize("qm", 1, BLOCKS[0])
-        after_gpsimd = reused([P, N + N // 2], F32, "slope")
-        late_rows = after_gpsimd[:, N // 2 :].bitcast(BF16)
+        new_codes("qm", 1, "neg_pw")
+        quantize("qm", 1, HALVES[0])
         for cols in HALVES:
             nc.scalar.copy(as_grouped("ds", 1, cols, run=4), as_planar(planar_ds, cols, run=4))
             quantize("ds", 1, cols)
 
+        after_gpsimd = reused([P, N + N // 2], F32, "slope")
+        late_rows = after_gpsimd[:, N // 2 :].bitcast(BF16)
         on_scalar(after_gpsimd[:, : N // 2], fourth_sums[:, HALVES[1]])
         scatter(0, 3, HALVES[1], after_gpsimd[:, : N // 2])
         new_grouped("dom", 1, HALVES[1], late_rows)
-        rows_of_second("dom", HALVES[1])
+        for name in ("dom", "qm"):
+            rows_of_second(name, HALVES[1])
 
         for k in range(D // P):
             scatter(1, k, WHOLE, copy_out(sums(1, k, shared_banks[k]), WHOLE, "dense%d" % k))
             nc.sync.dma_start(out[P * k : P * (k + 1), :], windows[k][:])
-            if k == 0:
-                new_grouped("qm", 1, HALVES[1], grouped_buffer(WIDTH // 2, "neg_pw"))
-                rows_of_second("qm", HALVES[1])

@@ -259,6 +259,8 @@ def tile_attend_gat_sig_c_kernel(tc, qT, cT, doT, rw, qm, dom, offs, out):
         group_latents(0, HALVES[1], words_on_vector)
         for cols in HALVES:
             quantize("latent", 0, cols)
+        for index in range(2):
+            product(psum.tile([P, N], F32, name=shared_banks[index]), "latent", index, "latent", 0, True, True)
         new_operand("q", 0, "grouped_b")
         dst, src = query_views("q", 0)
         on_vector(dst[:, 0, : P // 2], src[:, 0, : P // 2])

@@ -68,11 +68,19 @@ def tile_attend_gat_sig_c_kernel(tc, qT, cT, doT, rw, qm, dom, offs, out):
         load(("do", 0), doT[0], "prob")
         gate = keep.tile([P, B, PACK], F32, name="gate")
         nc.sync.dma_start(gate[:], rw.rearrange("b (p t) o -> p b (t o)", t=PACK))
-        load(("qm", 0), qm[0], "qm0")
-        for half, cols in enumerate(HALVES):
-            load(("dom", 0, half), dom[0][:, cols], "dom0_half%d" % half)
-        for index, (name, src) in enumerate((("q", qT), ("do", doT), ("qm", qm), ("dom", dom))):
-            load((name, 1), src[1], "chunk%d" % index)
+        def load_halves(half, buffer_name):
+            raw[("rows", half)] = reused([P, PACK, WIDTH], F32, buffer_name)
+            for index, src in enumerate((qm, dom)):
+                nc.sync.dma_start(
+                    raw[("rows", half)][:, :, HALVES[index]],
+                    src[0][:, HALVES[half]].rearrange("(p j) c -> p j c", j=PACK),
+                )
+
+        load_halves(0, "rows_first")
+        load(("q", 1), qT[1], "chunk0")
+        load_halves(1, "qm0")
+        for index, (name, src) in enumerate((("do", doT), ("qm", qm), ("dom", dom))):
+            load((name, 1), src[1], "chunk%d" % (index + 1))
 
         warm_up = keep.tile([P, 1], F32, name="warm_up")
         nc.scalar.activation(warm_up[:], chunks[0][:, 0, 0:1], ACT.Sigmoid)
@@ -113,8 +121,9 @@ def tile_attend_gat_sig_c_kernel(tc, qT, cT, doT, rw, qm, dom, offs, out):
         windows = [keep.tile([P, T], F32, name="window%d" % k) for k in range(D // P)]
         for window in windows:
             nc.vector.memset(window[:].bitcast(I32), 0)
-        neg_gate = keep.tile([P, B, PACK], F32, name="neg_gate")
-        nc.vector.tensor_scalar(neg_gate[:], gate[:], -1.0, None, ALU.mult)
+        neg_gate = [reused([P, PACK], F32, "neg_gate%d" % b) for b in range(B)]
+        nc.vector.tensor_scalar(neg_gate[0][:], gate[:, 0, :], -1.0, None, ALU.mult)
+        nc.scalar.activation(neg_gate[1][:], gate[:, 1, :], ACT.Copy, scale=-1.0)
 
         pieces = {}
         codes = {}
@@ -169,9 +178,9 @@ def tile_attend_gat_sig_c_kernel(tc, qT, cT, doT, rw, qm, dom, offs, out):
         def quantized(name, b, cols):
             if (name, b) == ("dom", 0) and cols.stop <= P:
                 return first_codes[:, cols].bitcast(FORMAT[name]), first_scales[0][:, cols]
-            if (name, b) == ("q", 1) and cols.start >= WIDTH // 2:
+            if b == 1 and name in late_scales and cols.start >= WIDTH // 2:
                 late = slice(cols.start - WIDTH // 2, cols.stop - WIDTH // 2)
-                return codes[(name, b)][:, cols].bitcast(FORMAT[name]), late_scales[b][:, late]
+                return codes[(name, b)][:, cols].bitcast(FORMAT[name]), late_scales[name][:, late]
             return codes[(name, b)][:, cols].bitcast(FORMAT[name]), scales[(name, b)][:, cols]
 
         def quantize(name, b, cols):
@@ -217,7 +226,7 @@ def tile_attend_gat_sig_c_kernel(tc, qT, cT, doT, rw, qm, dom, offs, out):
             for t in range(PACK):
                 bank = psum.tile([P, N], F32, name=bank_names[t])
                 product(bank, "do", t, "latent", b, True, True)
-                gated[t](neg_pw[b][:, t, :], prob[b][:, t, :], neg_gate[:, b, t : t + 1])
+                gated[t](neg_pw[b][:, t, :], prob[b][:, t, :], neg_gate[b][:, t : t + 1])
                 nc.vector.scalar_tensor_tensor(slope[b][:, t, :], prob[b][:, t, :], 1.0, bank[:], ALU.subtract, ALU.mult)
 
         def group_pw(b):
@@ -245,9 +254,10 @@ def tile_attend_gat_sig_c_kernel(tc, qT, cT, doT, rw, qm, dom, offs, out):
         shared_banks = ["shared_bank%d" % t for t in range(PACK)]
 
         def planar_rows(name, b, cols):
-            if (name, b) == ("dom", 0):
+            if b == 0:
                 half, first = divmod(cols.start, WIDTH // 2)
-                return as_planar(raw[(name, b, half)], slice(first, first + cols.stop - cols.start))
+                first = first + HALVES[("qm", "dom").index(name)].start
+                return as_planar(raw[("rows", half)], slice(first, first + cols.stop - cols.start))
             return as_planar(raw[(name, b)], cols)
 
         def rows(name, b, cols):
@@ -283,27 +293,29 @@ def tile_attend_gat_sig_c_kernel(tc, qT, cT, doT, rw, qm, dom, offs, out):
         slopes(0, [gated_on_gpsimd] * 3 + [gated_on_scalar], shared_banks)
 
         new_grouped("dom", 0, BLOCKS[0], grouped_buffer(P, "grouped_c"))
-        first_scales.append(reused([P, P], U8, "prob"))
+        first_scales.append(reused([P, P], U8, "neg_gate0"))
         new_codes("qm", 0)
         new_codes("dom", 0)
         new_operand("ds", 0, "grouped_a")
         new_operand("pw", 0, "grouped_e")
         quantize("qm", 0, BLOCKS[0])
-        nc.vector.tensor_tensor(
-            as_grouped("ds", 0, WHOLE), as_planar(slope[0], WHOLE), as_planar(neg_pw[0], WHOLE), ALU.mult
-        )
+        for cols in HALVES:
+            nc.vector.tensor_tensor(
+                as_grouped("ds", 0, cols), as_planar(slope[0], cols), as_planar(neg_pw[0], cols), ALU.mult
+            )
         rows("dom", 0, BLOCKS[0])
         group_pw(0)
+        quantize("ds", 0, HALVES[0])
         quantize("dom", 0, BLOCKS[0])
-        quantize("ds", 0, WHOLE)
+        quantize("ds", 0, HALVES[1])
         quantize("pw", 0, WHOLE)
         first_sums = sums(0, 0, "shared_bank0")
-        first_dense = copy_out(first_sums, WHOLE, "dense0")
+        first_dense = copy_out(first_sums, HALVES[0], "dense0")
         after_ds = grouped_buffer(WIDTH + WIDTH // 2, "grouped_a")
         new_grouped("latent", 1, WHOLE, after_ds[:, : PACK * WIDTH])
         new_codes("latent", 1)
         group_latents(1, WHOLE, words_on_vector)
-        second_blocks = grouped_buffer(2 * P, "slope")
+        second_blocks = grouped_buffer(2 * P, "prob")
         for index, name in enumerate(("qm", "dom")):
             new_grouped(name, 0, BLOCKS[1], second_blocks[:, PACK * P * index : PACK * P * (index + 1)])
             rows(name, 0, BLOCKS[1])
@@ -314,28 +326,42 @@ def tile_attend_gat_sig_c_kernel(tc, qT, cT, doT, rw, qm, dom, offs, out):
         new_grouped("q", 1, HALVES[0], after_ds[:, PACK * WIDTH :])
         query_half("q", 1, 0, on_scalar)
         quantize("q", 1, HALVES[0])
-        second_halves = grouped_buffer(WIDTH, "grouped_a")
-        for index, name in enumerate(("dom", "qm")):
+        late = 16
+        after_first = reused([P, N // 2 - late + 2 * N], F32, "grouped_a")
+        first_rest = after_first[:, : N // 2]
+        second_halves = after_first[:, N // 2 - late :].bitcast(BF16)
+        for index, name in enumerate(("qm", "dom")):
             new_grouped(name, 0, HALVES[1], second_halves[:, 2 * WIDTH * index : 2 * WIDTH * (index + 1)])
-            nc.gpsimd.tensor_scalar(
-                as_grouped(name, 0, HALVES[1]), planar_rows(name, 0, HALVES[1]), 1.0, 0.0, ALU.mult, ALU.add
-            )
-        scatter(0, 0, WHOLE, first_dense)
-        new_grouped("q", 1, HALVES[1], grouped_buffer(WIDTH // 2, "first_codes"))
-        query_half("q", 1, 1, on_scalar)
-        for name in ("dom", "qm"):
+        nc.gpsimd.tensor_scalar(
+            second_halves.rearrange("p (c e j) -> p c j e", e=2, j=PACK),
+            as_planar(raw[("rows", 1)], WHOLE),
+            1.0,
+            0.0,
+            ALU.mult,
+            ALU.add,
+        )
+        scatter(0, 0, HALVES[0], first_dense)
+        second_sums = sums(0, 1, "shared_bank1")
+        new_grouped("q", 1, HALVES[1], grouped_buffer(WIDTH // 2, "slope"))
+        dst, src = grouped_columns("q", 1, HALVES[1]).rearrange("p (e m j) -> p m j e", e=2, j=PACK), raw[("q", 1)][:].rearrange("p j (m h e) -> p h m j e", h=2, e=2)[:, 1]
+        for part in (slice(0, P // 2), slice(P // 2, P)):
+            on_scalar(dst[:, part], src[:, part])
+        scatter(0, 1, HALVES[0], copy_out(second_sums, HALVES[0], "first_codes"))
+        on_scalar(first_rest[:, : N // 2 - late], first_sums[:, N // 2 : N - late])
+        for name in ("qm", "dom"):
             quantize(name, 0, HALVES[1])
-        after_casts = reused([P, WIDTH // 2 + WIDTH], U8, "qm0")
-        late_scales[1] = after_casts[:, : WIDTH // 2]
+        after_casts = reused([P, WIDTH], U8, "qm0")
+        late_scales["q"] = after_casts[:, HALVES[0]]
+        late_scales["do"] = after_casts[:, HALVES[1]]
         quantize("q", 1, HALVES[1])
-        second_sums = sums(0, 1, "shared_bank0")
         new_grouped("do", 1, WHOLE, grouped_buffer(WIDTH, "neg_pw"))
-        codes[("do", 1)] = reused([P, WIDTH], U32, "do1_codes")
-        scales[("do", 1)] = after_casts[:, WIDTH // 2 :]
+        new_codes("do", 1)
         for h in range(2):
             query_half("do", 1, h, on_scalar)
-        quantize("do", 1, WHOLE)
-        scatter(0, 1, HALVES[0], copy_out(second_sums, HALVES[0], "grouped_a"))
+        quantize("do", 1, HALVES[0])
+        on_vector(first_rest[:, N // 2 - late :], first_sums[:, N - late :])
+        quantize("do", 1, HALVES[1])
+        scatter(0, 0, HALVES[1], first_rest)
 
         scores(1)
         after_scores = reused([P, 4 * N + N // 2], F32, "qm0")
@@ -344,7 +370,7 @@ def tile_attend_gat_sig_c_kernel(tc, qT, cT, doT, rw, qm, dom, offs, out):
         rows_of_qm = after_scores[:, N + N // 2 : 3 * N + N // 2].bitcast(BF16)
         rows_of_dom = after_scores[:, 3 * N + N // 2 :].bitcast(BF16)
         on_scalar(second_rest, second_sums[:, HALVES[1]])
-        slopes(1, [gated_on_gpsimd] * PACK, shared_banks[1:] + ["score_bank0"])
+        slopes(1, [gated_on_gpsimd] * PACK, shared_banks[2:] + ["shared_bank0", "score_bank0"])
         on_scalar(third_dense, sums(0, 2, "score_bank2")[:])
         scatter(0, 1, HALVES[1], second_rest)
 
@@ -353,9 +379,9 @@ def tile_attend_gat_sig_c_kernel(tc, qT, cT, doT, rw, qm, dom, offs, out):
         group_rows("qm", 1, HALVES[0], as_planar(raw[("qm", 1)], HALVES[0]))
         fourth_sums = sums(0, 3, "score_bank3")
         scatter(0, 3, HALVES[0], copy_out(fourth_sums, HALVES[0], "fourth_half"))
-        planar_ds = reuse.tile([P, PACK, N], BF16, name="planar_ds")
-        for t in range(PACK):
-            nc.gpsimd.tensor_tensor(planar_ds[:, t, :], slope[1][:, t, :], neg_pw[1][:, t, :], ALU.mult)
+        planar_ds = reused([P, PACK, N], BF16, "planar_ds")
+        for pair in (slice(0, 2), slice(2, PACK)):
+            nc.gpsimd.tensor_tensor(planar_ds[:, pair, :], slope[1][:, pair, :], neg_pw[1][:, pair, :], ALU.mult)
 
         def rows_of_second(name, cols):
             group_rows(name, 1, cols, as_planar(raw[(name, 1)], cols))
@@ -368,6 +394,7 @@ def tile_attend_gat_sig_c_kernel(tc, qT, cT, doT, rw, qm, dom, offs, out):
         group_pw(1)
         quantize("pw", 1, WHOLE)
         rows_of_second("dom", HALVES[0])
+        rows("qm", 1, HALVES[1])
         new_codes("qm", 1, "neg_pw")
         quantize("qm", 1, HALVES[0])
         for cols in HALVES:
@@ -378,9 +405,10 @@ def tile_attend_gat_sig_c_kernel(tc, qT, cT, doT, rw, qm, dom, offs, out):
         late_rows = after_gpsimd[:, N // 2 :].bitcast(BF16)
         on_scalar(after_gpsimd[:, : N // 2], fourth_sums[:, HALVES[1]])
         scatter(0, 3, HALVES[1], after_gpsimd[:, : N // 2])
+        late_scales["qm"] = reused([P, WIDTH // 2], U8, "planar_ds")
+        quantize("qm", 1, HALVES[1])
         new_grouped("dom", 1, HALVES[1], late_rows)
-        for name in ("dom", "qm"):
-            rows_of_second(name, HALVES[1])
+        rows_of_second("dom", HALVES[1])
 
         for k in range(D // P):
             scatter(1, k, WHOLE, copy_out(sums(1, k, shared_banks[k]), WHOLE, "dense%d" % k))

@@ -20,16 +20,20 @@ P = 128
 PACK = 4
 WIDTH = 512
 SLOTS_PER_COLUMN = 16
-CHUNK = T // 2
 
 WHOLE = slice(0, WIDTH)
 HALVES = (slice(0, WIDTH // 2), slice(WIDTH // 2, WIDTH))
+BLOCKS = tuple(slice(P * k, P * (k + 1)) for k in range(WIDTH // P))
 FORMAT = {"q": E4M3, "latent": E4M3, "do": E5M2, "qm": E4M3, "ds": E5M2, "dom": E5M2, "pw": E4M3}
 
-POOL_LOADS = ((0, 0, T), (1, 0, CHUNK), (1, CHUNK, T - T // 8), (1, T - T // 8, T))
-VECTOR_SHARE = (5, 8)
-DO_COLUMNS_ON_VECTOR = 84
-BLOCKS = tuple(slice(P * k, P * (k + 1)) for k in range(WIDTH // P))
+POOL_LOADS = (
+    (0, 0, T, 1376),
+    (1, 0, T // 2, 0),
+    (1, T // 2, T - T // 8, T // 2 - T // 8),
+    (1, T - T // 8, T, 160),
+)
+DO_GROUPS_ON_VECTOR = 84
+LAST_COLUMNS = 16
 
 
 def tile_attend_gat_sig_c_kernel(tc, qT, cT, doT, rw, qm, dom, offs, out):
@@ -51,9 +55,9 @@ def tile_attend_gat_sig_c_kernel(tc, qT, cT, doT, rw, qm, dom, offs, out):
         offsets = keep.tile([P, B * N // SLOTS_PER_COLUMN], U16, name="offsets")
 
         pool_rows = cT.rearrange("(p u e) c -> u p e c", u=2, e=2)
-        chunks = {}
-        for index, (u, first, stop) in enumerate(POOL_LOADS):
-            chunks[index] = reused([P, 2, stop - first], F32, "chunk%d" % index)
+        chunks = []
+        for index, (u, first, stop, on_vector_tokens) in enumerate(POOL_LOADS):
+            chunks.append(reused([P, 2, stop - first], F32, "chunk%d" % index))
             nc.sync.dma_start(chunks[index][:], pool_rows[u][:, :, first:stop])
             if index == 0:
                 nc.sync.dma_start(offsets[:], offs)
@@ -64,21 +68,21 @@ def tile_attend_gat_sig_c_kernel(tc, qT, cT, doT, rw, qm, dom, offs, out):
             raw[key] = reused([P, PACK, src.shape[1]], F32, buffer_name)
             nc.sync.dma_start(raw[key][:], src.rearrange("(p j) c -> p j c", j=PACK))
 
-        load(("q", 0), qT[0], "q0")
-        load(("do", 0), doT[0], "prob")
-        gate = keep.tile([P, B, PACK], F32, name="gate")
-        nc.sync.dma_start(gate[:], rw.rearrange("b (p t) o -> p b (t o)", t=PACK))
-        def load_halves(half, buffer_name):
-            raw[("rows", half)] = reused([P, PACK, WIDTH], F32, buffer_name)
+        def load_halves(half):
+            raw[("rows", half)] = reused([P, PACK, WIDTH], F32, "rows%d" % half)
             for index, src in enumerate((qm, dom)):
                 nc.sync.dma_start(
                     raw[("rows", half)][:, :, HALVES[index]],
                     src[0][:, HALVES[half]].rearrange("(p j) c -> p j c", j=PACK),
                 )
 
-        load_halves(0, "rows_first")
+        load(("q", 0), qT[0], "q0")
+        load(("do", 0), doT[0], "do0")
+        gate = keep.tile([P, B, PACK], F32, name="gate")
+        nc.sync.dma_start(gate[:], rw.rearrange("b (p t) o -> p b (t o)", t=PACK))
+        load_halves(0)
         load(("q", 1), qT[1], "chunk0")
-        load_halves(1, "qm0")
+        load_halves(1)
         for index, (name, src) in enumerate((("do", doT), ("qm", qm), ("dom", dom))):
             load((name, 1), src[1], "chunk%d" % (index + 1))
 
@@ -89,11 +93,13 @@ def tile_attend_gat_sig_c_kernel(tc, qT, cT, doT, rw, qm, dom, offs, out):
         picked_row = keep.tile([P, 2 * B * N + 3 * N // 2], U32, name="picked", align_bytes=64)
         picked = picked_row[:, : 2 * B * N].rearrange("p (u c) -> p u c", u=2)
 
-        def pair_up(index, first, stop, move):
-            u, base = POOL_LOADS[index][:2]
-            src = chunks[index][:, :, first:stop]
-            dst = pairs[u][:, base + first : base + stop, :]
-            move(dst.rearrange("p (c f) e -> p c e f", f=4), src.rearrange("p e (c f) -> p c e f", f=4))
+        def pair_up(index):
+            u, first, stop, split = POOL_LOADS[index]
+            for move, lo, hi in ((on_vector, 0, split), (on_scalar, split, stop - first)):
+                if lo < hi:
+                    src = chunks[index][:, :, lo:hi]
+                    dst = pairs[u][:, first + lo : first + hi, :]
+                    move(dst.rearrange("p (c f) e -> p c e f", f=4), src.rearrange("p e (c f) -> p c e f", f=4))
 
         def list_columns(first_slot, count):
             return offsets[:, first_slot // SLOTS_PER_COLUMN : (first_slot + count) // SLOTS_PER_COLUMN]
@@ -104,17 +110,10 @@ def tile_attend_gat_sig_c_kernel(tc, qT, cT, doT, rw, qm, dom, offs, out):
                 picked[:, u, first_slot : first_slot + count], words.indirect(list_columns(first_slot, count))
             )
 
-        def pair_up_shared(index, tokens):
-            split = tokens * VECTOR_SHARE[0] // VECTOR_SHARE[1]
-            pair_up(index, 0, split, on_vector)
-            pair_up(index, split, tokens, on_scalar)
-
-        pair_up(0, 0, 1376, on_vector)
-        pair_up(0, 1376, T, on_scalar)
+        pair_up(0)
         gather(0, 0, B * N)
-        pair_up(1, 0, CHUNK, on_scalar)
-        pair_up(2, 0, CHUNK - T // 8, on_vector)
-        pair_up_shared(3, T // 8)
+        for index in range(1, len(POOL_LOADS)):
+            pair_up(index)
         for cols in HALVES:
             gather(1, cols.start, N // 2)
 
@@ -166,22 +165,20 @@ def tile_attend_gat_sig_c_kernel(tc, qT, cT, doT, rw, qm, dom, offs, out):
             src = raw[(name, b)][:].rearrange("p j (m h e) -> p h m j e", h=2, e=2)
             return dst, src
 
-        def query_half(name, b, h, move):
+        def query_half(name, b, h, move, groups=slice(0, P)):
             dst = grouped_columns(name, b, HALVES[h]).rearrange("p (e m j) -> p m j e", e=2, j=PACK)
-            move(dst, raw[(name, b)][:].rearrange("p j (m h e) -> p h m j e", h=2, e=2)[:, h])
+            src = raw[(name, b)][:].rearrange("p j (m h e) -> p h m j e", h=2, e=2)[:, h]
+            move(dst[:, groups], src[:, groups])
 
         first_codes = reused([P, P], U32, "first_codes")
-        first_scales = []
-
-        late_scales = {}
+        scales_apart = {}
 
         def quantized(name, b, cols):
-            if (name, b) == ("dom", 0) and cols.stop <= P:
-                return first_codes[:, cols].bitcast(FORMAT[name]), first_scales[0][:, cols]
-            if b == 1 and name in late_scales and cols.start >= WIDTH // 2:
-                late = slice(cols.start - WIDTH // 2, cols.stop - WIDTH // 2)
-                return codes[(name, b)][:, cols].bitcast(FORMAT[name]), late_scales[name][:, late]
-            return codes[(name, b)][:, cols].bitcast(FORMAT[name]), scales[(name, b)][:, cols]
+            words = first_codes if (name, b, cols.start) == ("dom", 0, 0) else codes[(name, b)]
+            held, plane = scales_apart.get((name, b), (slice(0, 0), None))
+            if held.start <= cols.start < held.stop:
+                return words[:, cols].bitcast(FORMAT[name]), plane[:, cols.start - held.start : cols.stop - held.start]
+            return words[:, cols].bitcast(FORMAT[name]), scales[(name, b)][:, cols]
 
         def quantize(name, b, cols):
             out_codes, out_scales = quantized(name, b, cols)
@@ -205,22 +202,20 @@ def tile_attend_gat_sig_c_kernel(tc, qT, cT, doT, rw, qm, dom, offs, out):
         slope = {}
 
         def scores(b):
-            prob[b] = reused([P, PACK, N], F32, "prob")
+            prob[b] = reused([P, PACK, N], F32, "do0")
             for t in range(PACK):
                 bank = psum.tile([P, N], F32, name="score_bank%d" % t)
                 product(bank, "q", t, "latent", b, True, True)
                 nc.scalar.activation(prob[b][:, t, :], bank[:], ACT.Sigmoid)
 
-        def gated_on_vector(dst, src, factor):
-            nc.vector.tensor_scalar(dst, src, factor, None, ALU.mult)
-
-        def gated_on_scalar(dst, src, factor):
+        def scaled_on_scalar(dst, src, factor):
             nc.scalar.activation(dst, src, ACT.Copy, scale=factor)
 
-        def gated_on_gpsimd(dst, src, factor):
+        def scaled_on_gpsimd(dst, src, factor):
             nc.gpsimd.tensor_scalar(dst, src, factor, 0.0, ALU.mult, ALU.add)
 
-        def slopes(b, gated, bank_names):
+        def slopes(b, bank_names):
+            gated = [scaled_on_gpsimd] * (PACK - 1) + [scaled_on_scalar]
             neg_pw[b] = reused([P, PACK, N], F32, "neg_pw")
             slope[b] = reused([P, PACK, N], F32, "slope")
             for t in range(PACK):
@@ -232,8 +227,15 @@ def tile_attend_gat_sig_c_kernel(tc, qT, cT, doT, rw, qm, dom, offs, out):
         def group_pw(b):
             nc.scalar.activation(as_grouped("pw", b, WHOLE), as_planar(neg_pw[b], WHOLE), ACT.Copy, scale=-1.0)
 
-        def group_rows(name, b, cols, planar):
-            on_scalar(as_grouped(name, b, cols), planar)
+        def planar_rows(name, b, cols):
+            if b == 0:
+                half, first = divmod(cols.start, WIDTH // 2)
+                first = first + HALVES[("qm", "dom").index(name)].start
+                return as_planar(raw[("rows", half)], slice(first, first + cols.stop - cols.start))
+            return as_planar(raw[(name, b)], cols)
+
+        def group_rows(name, b, cols):
+            on_scalar(as_grouped(name, b, cols), planar_rows(name, b, cols))
 
         def sums(b, k, bank_name):
             bank = psum.tile([P, N], F32, name=bank_name)
@@ -253,16 +255,6 @@ def tile_attend_gat_sig_c_kernel(tc, qT, cT, doT, rw, qm, dom, offs, out):
 
         shared_banks = ["shared_bank%d" % t for t in range(PACK)]
 
-        def planar_rows(name, b, cols):
-            if b == 0:
-                half, first = divmod(cols.start, WIDTH // 2)
-                first = first + HALVES[("qm", "dom").index(name)].start
-                return as_planar(raw[("rows", half)], slice(first, first + cols.stop - cols.start))
-            return as_planar(raw[(name, b)], cols)
-
-        def rows(name, b, cols):
-            group_rows(name, b, cols, planar_rows(name, b, cols))
-
         new_operand("latent", 0, "grouped_a")
         gather(1, N, N // 2)
         group_latents(0, HALVES[0], nc.scalar.copy)
@@ -271,6 +263,7 @@ def tile_attend_gat_sig_c_kernel(tc, qT, cT, doT, rw, qm, dom, offs, out):
             quantize("latent", 0, cols)
         for index in range(2):
             product(psum.tile([P, N], F32, name=shared_banks[index]), "latent", index, "latent", 0, True, True)
+
         new_operand("q", 0, "grouped_b")
         dst, src = query_views("q", 0)
         on_vector(dst[:, 0, : P // 2], src[:, 0, : P // 2])
@@ -278,22 +271,22 @@ def tile_attend_gat_sig_c_kernel(tc, qT, cT, doT, rw, qm, dom, offs, out):
         on_scalar(dst[:, 1], src[:, 1])
         for cols in HALVES:
             quantize("q", 0, cols)
+
         new_grouped("do", 0, WHOLE, picked_row[:, 2 * B * N - N // 2 :].bitcast(BF16))
         new_codes("do", 0)
         dst, src = query_views("do", 0)
-        split = DO_COLUMNS_ON_VECTOR
-        on_vector(dst[:, :, :split], src[:, :, :split])
-        nc.scalar.copy(dst[:, :, split:], src[:, :, split:])
+        on_vector(dst[:, :, :DO_GROUPS_ON_VECTOR], src[:, :, :DO_GROUPS_ON_VECTOR])
+        nc.scalar.copy(dst[:, :, DO_GROUPS_ON_VECTOR:], src[:, :, DO_GROUPS_ON_VECTOR:])
         for cols in HALVES:
             quantize("do", 0, cols)
         gather(1, N + N // 2, N // 2)
         scores(0)
         new_grouped("qm", 0, BLOCKS[0], grouped_buffer(P, "grouped_b"))
-        rows("qm", 0, BLOCKS[0])
-        slopes(0, [gated_on_gpsimd] * 3 + [gated_on_scalar], shared_banks)
+        group_rows("qm", 0, BLOCKS[0])
+        slopes(0, shared_banks)
 
         new_grouped("dom", 0, BLOCKS[0], grouped_buffer(P, "grouped_c"))
-        first_scales.append(reused([P, P], U8, "neg_gate0"))
+        scales_apart[("dom", 0)] = (BLOCKS[0], reused([P, P], U8, "neg_gate0"))
         new_codes("qm", 0)
         new_codes("dom", 0)
         new_operand("ds", 0, "grouped_a")
@@ -303,7 +296,7 @@ def tile_attend_gat_sig_c_kernel(tc, qT, cT, doT, rw, qm, dom, offs, out):
             nc.vector.tensor_tensor(
                 as_grouped("ds", 0, cols), as_planar(slope[0], cols), as_planar(neg_pw[0], cols), ALU.mult
             )
-        rows("dom", 0, BLOCKS[0])
+        group_rows("dom", 0, BLOCKS[0])
         group_pw(0)
         quantize("ds", 0, HALVES[0])
         quantize("dom", 0, BLOCKS[0])
@@ -311,104 +304,94 @@ def tile_attend_gat_sig_c_kernel(tc, qT, cT, doT, rw, qm, dom, offs, out):
         quantize("pw", 0, WHOLE)
         first_sums = sums(0, 0, "shared_bank0")
         first_dense = copy_out(first_sums, HALVES[0], "dense0")
+
         after_ds = grouped_buffer(WIDTH + WIDTH // 2, "grouped_a")
         new_grouped("latent", 1, WHOLE, after_ds[:, : PACK * WIDTH])
         new_codes("latent", 1)
         group_latents(1, WHOLE, words_on_vector)
-        second_blocks = grouped_buffer(2 * P, "prob")
+        second_blocks = grouped_buffer(2 * P, "do0")
         for index, name in enumerate(("qm", "dom")):
             new_grouped(name, 0, BLOCKS[1], second_blocks[:, PACK * P * index : PACK * P * (index + 1)])
-            rows(name, 0, BLOCKS[1])
+            group_rows(name, 0, BLOCKS[1])
             quantize(name, 0, BLOCKS[1])
-
         quantize("latent", 1, WHOLE)
         new_codes("q", 1)
         new_grouped("q", 1, HALVES[0], after_ds[:, PACK * WIDTH :])
         query_half("q", 1, 0, on_scalar)
         quantize("q", 1, HALVES[0])
-        late = 16
-        after_first = reused([P, N // 2 - late + 2 * N], F32, "grouped_a")
+
+        after_first = reused([P, N // 2 - LAST_COLUMNS + 2 * N], F32, "grouped_a")
         first_rest = after_first[:, : N // 2]
-        second_halves = after_first[:, N // 2 - late :].bitcast(BF16)
+        second_halves = after_first[:, N // 2 - LAST_COLUMNS :].bitcast(BF16)
         for index, name in enumerate(("qm", "dom")):
             new_grouped(name, 0, HALVES[1], second_halves[:, 2 * WIDTH * index : 2 * WIDTH * (index + 1)])
-        nc.gpsimd.tensor_scalar(
-            second_halves.rearrange("p (c e j) -> p c j e", e=2, j=PACK),
-            as_planar(raw[("rows", 1)], WHOLE),
-            1.0,
-            0.0,
-            ALU.mult,
-            ALU.add,
+        scaled_on_gpsimd(
+            second_halves.rearrange("p (c e j) -> p c j e", e=2, j=PACK), as_planar(raw[("rows", 1)], WHOLE), 1.0
         )
         scatter(0, 0, HALVES[0], first_dense)
         second_sums = sums(0, 1, "shared_bank1")
         new_grouped("q", 1, HALVES[1], grouped_buffer(WIDTH // 2, "slope"))
-        dst, src = grouped_columns("q", 1, HALVES[1]).rearrange("p (e m j) -> p m j e", e=2, j=PACK), raw[("q", 1)][:].rearrange("p j (m h e) -> p h m j e", h=2, e=2)[:, 1]
-        for part in (slice(0, P // 2), slice(P // 2, P)):
-            on_scalar(dst[:, part], src[:, part])
+        for groups in (slice(0, P // 2), slice(P // 2, P)):
+            query_half("q", 1, 1, on_scalar, groups)
         scatter(0, 1, HALVES[0], copy_out(second_sums, HALVES[0], "first_codes"))
-        on_scalar(first_rest[:, : N // 2 - late], first_sums[:, N // 2 : N - late])
+        on_scalar(first_rest[:, : N // 2 - LAST_COLUMNS], first_sums[:, N // 2 : N - LAST_COLUMNS])
+
         for name in ("qm", "dom"):
             quantize(name, 0, HALVES[1])
-        after_casts = reused([P, WIDTH], U8, "qm0")
-        late_scales["q"] = after_casts[:, HALVES[0]]
-        late_scales["do"] = after_casts[:, HALVES[1]]
+        after_cast = reused([P, WIDTH], U8, "rows1")
+        for index, name in enumerate(("q", "do")):
+            scales_apart[(name, 1)] = (HALVES[1], after_cast[:, HALVES[index]])
         quantize("q", 1, HALVES[1])
-        new_grouped("do", 1, WHOLE, grouped_buffer(WIDTH, "neg_pw"))
-        new_codes("do", 1)
+        new_operand("do", 1, "neg_pw")
         for h in range(2):
             query_half("do", 1, h, on_scalar)
         quantize("do", 1, HALVES[0])
-        on_vector(first_rest[:, N // 2 - late :], first_sums[:, N - late :])
+        on_vector(first_rest[:, N // 2 - LAST_COLUMNS :], first_sums[:, N - LAST_COLUMNS :])
         quantize("do", 1, HALVES[1])
         scatter(0, 0, HALVES[1], first_rest)
 
         scores(1)
-        after_scores = reused([P, 4 * N + N // 2], F32, "qm0")
+        after_scores = reused([P, 3 * N + N // 2], F32, "rows1")
         third_dense = after_scores[:, :N]
         second_rest = after_scores[:, N : N + N // 2]
-        rows_of_qm = after_scores[:, N + N // 2 : 3 * N + N // 2].bitcast(BF16)
-        rows_of_dom = after_scores[:, 3 * N + N // 2 :].bitcast(BF16)
+        new_grouped("qm", 1, HALVES[0], after_scores[:, N + N // 2 : 2 * N + N // 2].bitcast(BF16))
+        new_grouped("dom", 1, HALVES[0], after_scores[:, 2 * N + N // 2 :].bitcast(BF16))
         on_scalar(second_rest, second_sums[:, HALVES[1]])
-        slopes(1, [gated_on_gpsimd] * PACK, shared_banks[2:] + ["shared_bank0", "score_bank0"])
+        slopes(1, shared_banks[2:] + ["shared_bank0", "score_bank0"])
         on_scalar(third_dense, sums(0, 2, "score_bank2")[:])
-        scatter(0, 1, HALVES[1], second_rest)
 
+        scatter(0, 1, HALVES[1], second_rest)
         scatter(0, 2, WHOLE, third_dense)
-        new_grouped("qm", 1, WHOLE, rows_of_qm)
-        group_rows("qm", 1, HALVES[0], as_planar(raw[("qm", 1)], HALVES[0]))
+        group_rows("qm", 1, HALVES[0])
         fourth_sums = sums(0, 3, "score_bank3")
         scatter(0, 3, HALVES[0], copy_out(fourth_sums, HALVES[0], "fourth_half"))
         planar_ds = reused([P, PACK, N], BF16, "planar_ds")
         for pair in (slice(0, 2), slice(2, PACK)):
             nc.gpsimd.tensor_tensor(planar_ds[:, pair, :], slope[1][:, pair, :], neg_pw[1][:, pair, :], ALU.mult)
-
-        def rows_of_second(name, cols):
-            group_rows(name, 1, cols, as_planar(raw[(name, 1)], cols))
-            quantize(name, 1, cols)
+        new_grouped("qm", 1, HALVES[1], grouped_buffer(WIDTH // 2, "do0"))
+        scaled_on_gpsimd(as_grouped("qm", 1, HALVES[1]), planar_rows("qm", 1, HALVES[1]), 1.0)
 
         new_operand("ds", 1, "grouped_c")
         new_operand("pw", 1, "grouped_d")
-        new_grouped("dom", 1, HALVES[0], rows_of_dom)
         new_codes("dom", 1)
         group_pw(1)
         quantize("pw", 1, WHOLE)
-        rows_of_second("dom", HALVES[0])
-        rows("qm", 1, HALVES[1])
+        group_rows("dom", 1, HALVES[0])
+        quantize("dom", 1, HALVES[0])
         new_codes("qm", 1, "neg_pw")
         quantize("qm", 1, HALVES[0])
         for cols in HALVES:
             nc.scalar.copy(as_grouped("ds", 1, cols, run=4), as_planar(planar_ds, cols, run=4))
             quantize("ds", 1, cols)
 
-        after_gpsimd = reused([P, N + N // 2], F32, "slope")
-        late_rows = after_gpsimd[:, N // 2 :].bitcast(BF16)
-        on_scalar(after_gpsimd[:, : N // 2], fourth_sums[:, HALVES[1]])
-        scatter(0, 3, HALVES[1], after_gpsimd[:, : N // 2])
-        late_scales["qm"] = reused([P, WIDTH // 2], U8, "planar_ds")
+        after_products = reused([P, N + N // 2], F32, "slope")
+        on_scalar(after_products[:, : N // 2], fourth_sums[:, HALVES[1]])
+        scatter(0, 3, HALVES[1], after_products[:, : N // 2])
+        scales_apart[("qm", 1)] = (HALVES[1], reused([P, WIDTH // 2], U8, "planar_ds"))
         quantize("qm", 1, HALVES[1])
-        new_grouped("dom", 1, HALVES[1], late_rows)
-        rows_of_second("dom", HALVES[1])
+        new_grouped("dom", 1, HALVES[1], after_products[:, N // 2 :].bitcast(BF16))
+        group_rows("dom", 1, HALVES[1])
+        quantize("dom", 1, HALVES[1])
 
         for k in range(D // P):
             scatter(1, k, WHOLE, copy_out(sums(1, k, shared_banks[k]), WHOLE, "dense%d" % k))

@@ -32,8 +32,9 @@ POOL_LOADS = (
     (1, T // 2, T - T // 8, T // 2 - T // 8),
     (1, T - T // 8, T, 160),
 )
-DO_GROUPS_ON_VECTOR = 84
-LAST_COLUMNS = 16
+Q0_GROUPS_ON_VECTOR = 104
+DO0_GROUPS_ON_VECTOR = 168
+DS_FILLER = 64
 
 
 def tile_attend_gat_sig_c_kernel(tc, qT, cT, doT, rw, qm, dom, offs, out):
@@ -68,29 +69,20 @@ def tile_attend_gat_sig_c_kernel(tc, qT, cT, doT, rw, qm, dom, offs, out):
             raw[key] = reused([P, PACK, src.shape[1]], F32, buffer_name)
             nc.sync.dma_start(raw[key][:], src.rearrange("(p j) c -> p j c", j=PACK))
 
-        def load_halves(half):
-            raw[("rows", half)] = reused([P, PACK, WIDTH], F32, "rows%d" % half)
-            for index, src in enumerate((qm, dom)):
-                nc.sync.dma_start(
-                    raw[("rows", half)][:, :, HALVES[index]],
-                    src[0][:, HALVES[half]].rearrange("(p j) c -> p j c", j=PACK),
-                )
-
         load(("q", 0), qT[0], "q0")
         load(("do", 0), doT[0], "do0")
         gate = keep.tile([P, B, PACK], F32, name="gate")
         nc.sync.dma_start(gate[:], rw.rearrange("b (p t) o -> p b (t o)", t=PACK))
-        load_halves(0)
-        load(("q", 1), qT[1], "chunk0")
-        load_halves(1)
-        for index, (name, src) in enumerate((("do", doT), ("qm", qm), ("dom", dom))):
-            load((name, 1), src[1], "chunk%d" % (index + 1))
+        load(("q", 1), qT[1], "q1")
+        for index, (name, b, src) in enumerate((("do", 1, doT), ("qm", 0, qm), ("dom", 0, dom), ("dom", 1, dom))):
+            load((name, b), src[b], "chunk%d" % index)
+        load(("qm", 1), qm[1], "q1")
 
         warm_up = keep.tile([P, 1], F32, name="warm_up")
         nc.scalar.activation(warm_up[:], chunks[0][:, 0, 0:1], ACT.Sigmoid)
 
         pairs = [keep.tile([P, T, 2], BF16, name="pairs%d" % u) for u in range(2)]
-        picked_row = keep.tile([P, 2 * B * N + 3 * N // 2], U32, name="picked", align_bytes=64)
+        picked_row = keep.tile([P, 2 * B * N + N // 2], U32, name="picked", align_bytes=64)
         picked = picked_row[:, : 2 * B * N].rearrange("p (u c) -> p u c", u=2)
 
         def pair_up(index):
@@ -120,37 +112,44 @@ def tile_attend_gat_sig_c_kernel(tc, qT, cT, doT, rw, qm, dom, offs, out):
         windows = [keep.tile([P, T], F32, name="window%d" % k) for k in range(D // P)]
         for window in windows:
             nc.vector.memset(window[:].bitcast(I32), 0)
-        neg_gate = [reused([P, PACK], F32, "neg_gate%d" % b) for b in range(B)]
-        nc.vector.tensor_scalar(neg_gate[0][:], gate[:, 0, :], -1.0, None, ALU.mult)
-        nc.scalar.activation(neg_gate[1][:], gate[:, 1, :], ACT.Copy, scale=-1.0)
+        neg_gate = keep.tile([P, B, PACK], F32, name="neg_gate")
+        nc.scalar.activation(neg_gate[:], gate[:], ACT.Copy, scale=-1.0)
 
         pieces = {}
         codes = {}
         scales = {}
+        for name in FORMAT:
+            for b in range(B):
+                if (name, b) not in (("dom", 0), ("ds", 1)):
+                    codes[(name, b)] = keep.tile([P, WIDTH], U32, name="%s%d_codes" % (name, b), align_bytes=64)
+                if (name, b) not in (("dom", 0), ("ds", 1), ("pw", 0)):
+                    scales[(name, b)] = keep.tile([P, WIDTH], U8, name="%s%d_scales" % (name, b), align_bytes=64)
+        joint_codes = keep.tile([P, 2 * WIDTH], U32, name="joint_codes", align_bytes=64)
+        joint_scales = keep.tile([P, 2 * WIDTH], U8, name="joint_scales", align_bytes=64)
 
-        def new_grouped(name, b, cols, buffer):
+        def joint_columns(name, cols):
+            first = cols.start + (WIDTH // 2 if name == "ds" else WIDTH * (cols.start // (WIDTH // 2)))
+            return slice(first, first + cols.stop - cols.start)
+
+        def quantized(name, b, cols):
+            if (name, b) in (("dom", 0), ("ds", 1)):
+                place = joint_columns(name, cols)
+                return joint_codes[:, place].bitcast(E5M2), joint_scales[:, place]
+            return codes[(name, b)][:, cols].bitcast(FORMAT[name]), scales[(name, b)][:, cols]
+
+        def new_grouped(name, b, cols, buffer_name):
+            buffer = reused([P, (cols.stop - cols.start) * PACK], BF16, buffer_name)
             pieces.setdefault((name, b), []).append((cols, buffer))
-
-        def grouped_buffer(width, buffer_name):
-            return reused([P, width * PACK], BF16, buffer_name)[:]
-
-        def new_codes(name, b, codes_buffer=None):
-            codes[(name, b)] = reused([P, WIDTH], U32, codes_buffer or "%s%d_codes" % (name, b))
-            scales[(name, b)] = keep.tile([P, WIDTH], U8, name="%s%d_scales" % (name, b), align_bytes=64)
-
-        def new_operand(name, b, buffer_name, codes_buffer=None):
-            new_grouped(name, b, WHOLE, grouped_buffer(WIDTH, buffer_name))
-            new_codes(name, b, codes_buffer)
 
         def grouped_columns(name, b, cols):
             held, buffer = [x for x in pieces[(name, b)] if x[0].start <= cols.start and cols.stop <= x[0].stop][0]
             return buffer[:, PACK * (cols.start - held.start) : PACK * (cols.stop - held.start)]
 
-        def as_grouped(name, b, cols, run=2):
-            return grouped_columns(name, b, cols).rearrange("p (c e j) -> p c j e", e=run, j=PACK)
+        def as_grouped(name, b, cols):
+            return grouped_columns(name, b, cols).rearrange("p (c e j) -> p c j e", e=2, j=PACK)
 
-        def as_planar(tile, cols, run=2):
-            return tile[:, :, cols].rearrange("p j (c e) -> p c j e", e=run)
+        def as_planar(view):
+            return view.rearrange("p j (c e) -> p c j e", e=2)
 
         def group_latents(b, cols, move):
             src = picked[:, :, N * b + cols.start : N * b + cols.stop]
@@ -160,35 +159,15 @@ def tile_attend_gat_sig_c_kernel(tc, qT, cT, doT, rw, qm, dom, offs, out):
         def words_on_vector(dst, src):
             nc.vector.tensor_copy(dst.bitcast(I32), src.bitcast(I32))
 
-        def query_views(name, b):
-            dst = grouped_columns(name, b, WHOLE).rearrange("p (h e m j) -> p h m j e", h=2, e=2, j=PACK)
-            src = raw[(name, b)][:].rearrange("p j (m h e) -> p h m j e", h=2, e=2)
-            return dst, src
-
-        def query_half(name, b, h, move, groups=slice(0, P)):
-            dst = grouped_columns(name, b, HALVES[h]).rearrange("p (e m j) -> p m j e", e=2, j=PACK)
-            src = raw[(name, b)][:].rearrange("p j (m h e) -> p h m j e", h=2, e=2)[:, h]
-            move(dst[:, groups], src[:, groups])
-
-        first_codes = reused([P, P], U32, "first_codes")
-        scales_apart = {}
-
-        def quantized(name, b, cols):
-            words = first_codes if (name, b, cols.start) == ("dom", 0, 0) else codes[(name, b)]
-            held, plane = scales_apart.get((name, b), (slice(0, 0), None))
-            if held.start <= cols.start < held.stop:
-                return words[:, cols].bitcast(FORMAT[name]), plane[:, cols.start - held.start : cols.stop - held.start]
-            return words[:, cols].bitcast(FORMAT[name]), scales[(name, b)][:, cols]
-
         def quantize(name, b, cols):
             out_codes, out_scales = quantized(name, b, cols)
             nc.vector.quantize_mx(out=out_codes, scales=out_scales, in_=grouped_columns(name, b, cols))
 
-        def product(bank, stationary, block, moving, b, start, stop):
-            lhs_codes, lhs_scales = quantized(stationary, b, slice(P * block, P * (block + 1)))
-            rhs_codes, rhs_scales = quantized(moving, b, WHOLE)
+        def product(sums, stationary, block, moving, b, cols, start, stop):
+            lhs_codes, lhs_scales = quantized(stationary, b, BLOCKS[block])
+            rhs_codes, rhs_scales = quantized(moving, b, cols)
             nc.tensor.matmul_mx(
-                out=bank[:],
+                out=sums,
                 lhsT=lhs_codes,
                 lhsT_scale=lhs_scales,
                 rhs=rhs_codes,
@@ -201,11 +180,11 @@ def tile_attend_gat_sig_c_kernel(tc, qT, cT, doT, rw, qm, dom, offs, out):
         neg_pw = {}
         slope = {}
 
-        def scores(b):
-            prob[b] = reused([P, PACK, N], F32, "do0")
+        def scores(b, buffer_name):
+            prob[b] = reused([P, PACK, N], F32, buffer_name)
             for t in range(PACK):
                 bank = psum.tile([P, N], F32, name="score_bank%d" % t)
-                product(bank, "q", t, "latent", b, True, True)
+                product(bank[:], "q", t, "latent", b, WHOLE, True, True)
                 nc.scalar.activation(prob[b][:, t, :], bank[:], ACT.Sigmoid)
 
         def scaled_on_scalar(dst, src, factor):
@@ -214,185 +193,180 @@ def tile_attend_gat_sig_c_kernel(tc, qT, cT, doT, rw, qm, dom, offs, out):
         def scaled_on_gpsimd(dst, src, factor):
             nc.gpsimd.tensor_scalar(dst, src, factor, 0.0, ALU.mult, ALU.add)
 
-        def slopes(b, bank_names):
+        def on_gpsimd(dst, src):
+            scaled_on_gpsimd(dst, src, 1.0)
+
+        def slopes(b, buffer_name):
             gated = [scaled_on_gpsimd] * (PACK - 1) + [scaled_on_scalar]
-            neg_pw[b] = reused([P, PACK, N], F32, "neg_pw")
+            neg_pw[b] = reused([P, PACK, N], F32, buffer_name)
             slope[b] = reused([P, PACK, N], F32, "slope")
             for t in range(PACK):
-                bank = psum.tile([P, N], F32, name=bank_names[t])
-                product(bank, "do", t, "latent", b, True, True)
-                gated[t](neg_pw[b][:, t, :], prob[b][:, t, :], neg_gate[b][:, t : t + 1])
+                bank = psum.tile([P, N], F32, name="slope_bank%d" % t)
+                product(bank[:], "do", t, "latent", b, WHOLE, True, True)
+                gated[t](neg_pw[b][:, t, :], prob[b][:, t, :], neg_gate[:, b, t : t + 1])
                 nc.vector.scalar_tensor_tensor(slope[b][:, t, :], prob[b][:, t, :], 1.0, bank[:], ALU.subtract, ALU.mult)
 
-        def group_pw(b):
-            nc.scalar.activation(as_grouped("pw", b, WHOLE), as_planar(neg_pw[b], WHOLE), ACT.Copy, scale=-1.0)
+        def group_ds(b, cols):
+            nc.vector.tensor_tensor(
+                as_grouped("ds", b, cols), as_planar(slope[b][:, :, cols]), as_planar(neg_pw[b][:, :, cols]), ALU.mult
+            )
 
-        def planar_rows(name, b, cols):
-            if b == 0:
-                half, first = divmod(cols.start, WIDTH // 2)
-                first = first + HALVES[("qm", "dom").index(name)].start
-                return as_planar(raw[("rows", half)], slice(first, first + cols.stop - cols.start))
-            return as_planar(raw[(name, b)], cols)
+        def group_pw(b, scaled):
+            scaled(as_grouped("pw", b, WHOLE), as_planar(neg_pw[b][:]), -1.0)
 
-        def group_rows(name, b, cols):
-            on_scalar(as_grouped(name, b, cols), planar_rows(name, b, cols))
+        def group_rows(name, b, cols, move):
+            move(as_grouped(name, b, cols), as_planar(raw[(name, b)][:, :, cols]))
 
-        def sums(b, k, bank_name):
+        def sums(b, parts, bank_name):
             bank = psum.tile([P, N], F32, name=bank_name)
-            first, last = (("qm", "ds"), ("dom", "pw")) if b == 0 else (("dom", "pw"), ("qm", "ds"))
-            product(bank, first[0], k, first[1], b, True, False)
-            product(bank, last[0], k, last[1], b, False, True)
+            first = 0
+            for k, cols in parts:
+                stop = first + cols.stop - cols.start
+                product(bank[:, first:stop], "qm", k, "ds", b, cols, True, False)
+                product(bank[:, first:stop], "dom", k, "pw", b, cols, False, True)
+                first = stop
             return bank
 
-        def copy_out(bank, cols, buffer_name):
-            dense = reused([P, cols.stop - cols.start], F32, buffer_name)
-            on_scalar(dense[:], bank[:, cols])
-            return dense[:]
+        def copy_out(bank, cols, move, dense):
+            move(dense, bank[:, cols])
+            return dense
 
-        def scatter(b, k, cols, dense):
-            slots = list_columns(N * b + cols.start, cols.stop - cols.start)
-            nc.vector.tensor_copy(windows[k][:].indirect(slots), dense)
+        def dense_buffer(width, buffer_name):
+            return reused([P, width], F32, buffer_name)[:]
 
-        shared_banks = ["shared_bank%d" % t for t in range(PACK)]
+        def scatter(b, k, cols, move, dense):
+            move(windows[k][:].indirect(list_columns(N * b + cols.start, cols.stop - cols.start)), dense)
 
-        new_operand("latent", 0, "grouped_a")
-        gather(1, N, N // 2)
+        def store(k):
+            nc.sync.dma_start(out[P * k : P * (k + 1), :], windows[k][:])
+
+        def cast_queries(name, b, on_vector_groups):
+            src = raw[(name, b)][:].rearrange("p j (m h e) -> p h m j e", h=2, e=2)
+            dst = [grouped_columns(name, b, cols).rearrange("p (e m j) -> p m j e", e=2, j=PACK) for cols in HALVES]
+            first, second = min(on_vector_groups, P), max(on_vector_groups - P, 0)
+            for h, split in enumerate((first, second)):
+                if split > 0:
+                    on_vector(dst[h][:, :split], src[:, h, :split])
+            for h, split in enumerate((first, second)):
+                if split < P:
+                    on_scalar(dst[h][:, split:], src[:, h, split:])
+
+        new_grouped("latent", 0, WHOLE, "grouped_a")
         group_latents(0, HALVES[0], nc.scalar.copy)
+        gather(1, N, N // 2)
         group_latents(0, HALVES[1], words_on_vector)
         for cols in HALVES:
             quantize("latent", 0, cols)
-        for index in range(2):
-            product(psum.tile([P, N], F32, name=shared_banks[index]), "latent", index, "latent", 0, True, True)
-
-        new_operand("q", 0, "grouped_b")
-        dst, src = query_views("q", 0)
-        on_vector(dst[:, 0, : P // 2], src[:, 0, : P // 2])
-        on_scalar(dst[:, 0, P // 2 :], src[:, 0, P // 2 :])
-        on_scalar(dst[:, 1], src[:, 1])
+        new_grouped("q", 0, WHOLE, "grouped_b")
+        cast_queries("q", 0, Q0_GROUPS_ON_VECTOR)
         for cols in HALVES:
             quantize("q", 0, cols)
-
-        new_grouped("do", 0, WHOLE, picked_row[:, 2 * B * N - N // 2 :].bitcast(BF16))
-        new_codes("do", 0)
-        dst, src = query_views("do", 0)
-        on_vector(dst[:, :, :DO_GROUPS_ON_VECTOR], src[:, :, :DO_GROUPS_ON_VECTOR])
-        nc.scalar.copy(dst[:, :, DO_GROUPS_ON_VECTOR:], src[:, :, DO_GROUPS_ON_VECTOR:])
+        new_grouped("latent", 1, WHOLE, "q0")
+        group_latents(1, HALVES[0], nc.scalar.copy)
+        pieces[("do", 0)] = [(HALVES[0], picked_row[:, 2 * B * N - N // 2 :].bitcast(BF16))]
+        new_grouped("do", 0, HALVES[1], "grouped_c")
+        cast_queries("do", 0, DO0_GROUPS_ON_VECTOR)
+        scores(0, "do0")
         for cols in HALVES:
             quantize("do", 0, cols)
         gather(1, N + N // 2, N // 2)
-        scores(0)
-        new_grouped("qm", 0, BLOCKS[0], grouped_buffer(P, "grouped_b"))
-        group_rows("qm", 0, BLOCKS[0])
-        slopes(0, shared_banks)
-
-        new_grouped("dom", 0, BLOCKS[0], grouped_buffer(P, "grouped_c"))
-        scales_apart[("dom", 0)] = (BLOCKS[0], reused([P, P], U8, "neg_gate0"))
-        new_codes("qm", 0)
-        new_codes("dom", 0)
-        new_operand("ds", 0, "grouped_a")
-        new_operand("pw", 0, "grouped_e")
-        quantize("qm", 0, BLOCKS[0])
-        for cols in HALVES:
-            nc.vector.tensor_tensor(
-                as_grouped("ds", 0, cols), as_planar(slope[0], cols), as_planar(neg_pw[0], cols), ALU.mult
-            )
-        group_rows("dom", 0, BLOCKS[0])
-        group_pw(0)
-        quantize("ds", 0, HALVES[0])
-        quantize("dom", 0, BLOCKS[0])
-        quantize("ds", 0, HALVES[1])
-        quantize("pw", 0, WHOLE)
-        first_sums = sums(0, 0, "shared_bank0")
-        first_dense = copy_out(first_sums, HALVES[0], "dense0")
-
-        after_ds = grouped_buffer(WIDTH + WIDTH // 2, "grouped_a")
-        new_grouped("latent", 1, WHOLE, after_ds[:, : PACK * WIDTH])
-        new_codes("latent", 1)
-        group_latents(1, WHOLE, words_on_vector)
-        second_blocks = grouped_buffer(2 * P, "do0")
-        for index, name in enumerate(("qm", "dom")):
-            new_grouped(name, 0, BLOCKS[1], second_blocks[:, PACK * P * index : PACK * P * (index + 1)])
-            group_rows(name, 0, BLOCKS[1])
-            quantize(name, 0, BLOCKS[1])
+        slopes(0, "grouped_c")
+        group_latents(1, HALVES[1], nc.scalar.copy)
         quantize("latent", 1, WHOLE)
-        new_codes("q", 1)
-        new_grouped("q", 1, HALVES[0], after_ds[:, PACK * WIDTH :])
-        query_half("q", 1, 0, on_scalar)
-        quantize("q", 1, HALVES[0])
+        new_grouped("q", 1, WHOLE, "grouped_b")
+        cast_queries("q", 1, 0)
+        new_grouped("ds", 0, WHOLE, "grouped_ds")
+        group_ds(0, HALVES[0])
+        quantize("q", 1, WHOLE)
+        group_ds(0, HALVES[1])
+        new_grouped("pw", 0, WHOLE, "grouped_pw")
+        group_pw(0, scaled_on_scalar)
 
-        after_first = reused([P, N // 2 - LAST_COLUMNS + 2 * N], F32, "grouped_a")
-        first_rest = after_first[:, : N // 2]
-        second_halves = after_first[:, N // 2 - LAST_COLUMNS :].bitcast(BF16)
-        for index, name in enumerate(("qm", "dom")):
-            new_grouped(name, 0, HALVES[1], second_halves[:, 2 * WIDTH * index : 2 * WIDTH * (index + 1)])
-        scaled_on_gpsimd(
-            second_halves.rearrange("p (c e j) -> p c j e", e=2, j=PACK), as_planar(raw[("rows", 1)], WHOLE), 1.0
-        )
-        scatter(0, 0, HALVES[0], first_dense)
-        second_sums = sums(0, 1, "shared_bank1")
-        new_grouped("q", 1, HALVES[1], grouped_buffer(WIDTH // 2, "slope"))
-        for groups in (slice(0, P // 2), slice(P // 2, P)):
-            query_half("q", 1, 1, on_scalar, groups)
-        scatter(0, 1, HALVES[0], copy_out(second_sums, HALVES[0], "first_codes"))
-        on_scalar(first_rest[:, : N // 2 - LAST_COLUMNS], first_sums[:, N // 2 : N - LAST_COLUMNS])
+        new_grouped("do", 1, HALVES[0], "grouped_a")
+        new_grouped("do", 1, HALVES[1], "grouped_d")
+        cast_queries("do", 1, 2 * P)
+        scores(1, "prob")
+        quantize("ds", 0, WHOLE)
+        for cols in HALVES:
+            quantize("do", 1, cols)
+        scales[("pw", 0)] = reused([P, WIDTH], U8, "grouped_a")
+        quantize("pw", 0, WHOLE)
+        slopes(1, "grouped_d")
+        new_grouped("qm", 0, WHOLE, "grouped_qm")
+        joint = reused([P, 2 * WIDTH * PACK], BF16, "grouped_ds")
+        for name, b, cols in (("dom", 0, HALVES[0]), ("ds", 1, WHOLE), ("dom", 0, HALVES[1])):
+            place = joint_columns(name, cols)
+            pieces.setdefault((name, b), []).append((cols, joint[:, PACK * place.start : PACK * place.stop]))
+
+        def quantize_joint(half):
+            cols = slice(WIDTH * half, WIDTH * (half + 1))
+            nc.vector.quantize_mx(
+                out=joint_codes[:, cols].bitcast(E5M2),
+                scales=joint_scales[:, cols],
+                in_=joint[:, PACK * cols.start : PACK * cols.stop],
+            )
 
         for name in ("qm", "dom"):
-            quantize(name, 0, HALVES[1])
-        after_cast = reused([P, WIDTH], U8, "rows1")
-        for index, name in enumerate(("q", "do")):
-            scales_apart[(name, 1)] = (HALVES[1], after_cast[:, HALVES[index]])
-        quantize("q", 1, HALVES[1])
-        new_operand("do", 1, "neg_pw")
-        for h in range(2):
-            query_half("do", 1, h, on_scalar)
-        quantize("do", 1, HALVES[0])
-        on_vector(first_rest[:, N // 2 - LAST_COLUMNS :], first_sums[:, N - LAST_COLUMNS :])
-        quantize("do", 1, HALVES[1])
-        scatter(0, 0, HALVES[1], first_rest)
+            group_rows(name, 0, HALVES[0], on_scalar)
+        quantize("qm", 0, HALVES[0])
+        group_ds(1, HALVES[0])
+        group_ds(1, slice(N // 2, N // 2 + DS_FILLER))
+        quantize_joint(0)
+        bank_a = sums(0, [(1, WHOLE)], "score_bank0")
+        bank_b = sums(0, [(0, HALVES[0])], "score_bank1")
+        for name in ("qm", "dom"):
+            group_rows(name, 0, HALVES[1], on_scalar)
+        group_ds(1, slice(N // 2 + DS_FILLER, N))
+        dense_a = copy_out(bank_a, WHOLE, on_scalar, dense_buffer(N, "dense_a"))
+        quantize("qm", 0, HALVES[1])
+        quantize_joint(1)
+        bank_c = sums(0, [(3, HALVES[0]), (0, HALVES[1])], "score_bank2")
+        bank_d = sums(0, [(2, WHOLE)], "score_bank3")
+        bank_e = sums(0, [(3, HALVES[1])], "slope_bank0")
 
-        scores(1)
-        after_scores = reused([P, 3 * N + N // 2], F32, "rows1")
-        third_dense = after_scores[:, :N]
-        second_rest = after_scores[:, N : N + N // 2]
-        new_grouped("qm", 1, HALVES[0], after_scores[:, N + N // 2 : 2 * N + N // 2].bitcast(BF16))
-        new_grouped("dom", 1, HALVES[0], after_scores[:, 2 * N + N // 2 :].bitcast(BF16))
-        on_scalar(second_rest, second_sums[:, HALVES[1]])
-        slopes(1, shared_banks[2:] + ["shared_bank0", "score_bank0"])
-        on_scalar(third_dense, sums(0, 2, "score_bank2")[:])
-
-        scatter(0, 1, HALVES[1], second_rest)
-        scatter(0, 2, WHOLE, third_dense)
-        group_rows("qm", 1, HALVES[0])
-        fourth_sums = sums(0, 3, "score_bank3")
-        scatter(0, 3, HALVES[0], copy_out(fourth_sums, HALVES[0], "fourth_half"))
-        planar_ds = reused([P, PACK, N], BF16, "planar_ds")
-        for pair in (slice(0, 2), slice(2, PACK)):
-            nc.gpsimd.tensor_tensor(planar_ds[:, pair, :], slope[1][:, pair, :], neg_pw[1][:, pair, :], ALU.mult)
-        new_grouped("qm", 1, HALVES[1], grouped_buffer(WIDTH // 2, "do0"))
-        scaled_on_gpsimd(as_grouped("qm", 1, HALVES[1]), planar_rows("qm", 1, HALVES[1]), 1.0)
-
-        new_operand("ds", 1, "grouped_c")
-        new_operand("pw", 1, "grouped_d")
-        new_codes("dom", 1)
-        group_pw(1)
-        quantize("pw", 1, WHOLE)
-        group_rows("dom", 1, HALVES[0])
-        quantize("dom", 1, HALVES[0])
-        new_codes("qm", 1, "neg_pw")
-        quantize("qm", 1, HALVES[0])
+        late = reused([P, 9 * WIDTH], BF16, "grouped_ds")
+        pieces[("pw", 1)] = [(WHOLE, late[:, : 4 * WIDTH])]
+        pieces[("dom", 1)] = [(HALVES[0], late[:, 5 * WIDTH : 7 * WIDTH]), (HALVES[1], late[:, WIDTH : 3 * WIDTH])]
+        pieces[("qm", 1)] = [(HALVES[0], late[:, 7 * WIDTH :]), (HALVES[1], late[:, 3 * WIDTH : 5 * WIDTH])]
+        scatter(0, 1, WHOLE, on_vector, dense_a)
+        dense_b = copy_out(bank_b, HALVES[0], on_scalar, dense_buffer(N // 2, "dense_b"))
+        for name in ("dom", "qm"):
+            group_rows(name, 1, HALVES[0], on_gpsimd)
+        group_pw(1, scaled_on_gpsimd)
+        scatter(0, 0, HALVES[0], on_scalar, dense_b)
+        dense_c = copy_out(bank_c, WHOLE, on_scalar, dense_buffer(N, "dense_c"))
+        dense_d = copy_out(bank_d, WHOLE, on_scalar, dense_buffer(N, "dense_d"))
+        scatter(0, 0, HALVES[1], on_scalar, dense_c[:, HALVES[1]])
+        scatter(0, 3, HALVES[0], on_vector, dense_c[:, HALVES[0]])
+        for name in ("dom", "qm"):
+            quantize(name, 1, HALVES[0])
         for cols in HALVES:
-            nc.scalar.copy(as_grouped("ds", 1, cols, run=4), as_planar(planar_ds, cols, run=4))
-            quantize("ds", 1, cols)
-
-        after_products = reused([P, N + N // 2], F32, "slope")
-        on_scalar(after_products[:, : N // 2], fourth_sums[:, HALVES[1]])
-        scatter(0, 3, HALVES[1], after_products[:, : N // 2])
-        scales_apart[("qm", 1)] = (HALVES[1], reused([P, WIDTH // 2], U8, "planar_ds"))
-        quantize("qm", 1, HALVES[1])
-        new_grouped("dom", 1, HALVES[1], after_products[:, N // 2 :].bitcast(BF16))
-        group_rows("dom", 1, HALVES[1])
+            quantize("pw", 1, cols)
+        for cols in HALVES:
+            scatter(0, 2, cols, on_scalar, dense_d[:, cols])
+        second_sums = [None] * PACK
+        for k in (0, 1):
+            second_sums[k] = sums(1, [(k, WHOLE)], "slope_bank%d" % (k + 1))
+        scatter(0, 3, HALVES[1], on_vector, copy_out(bank_e, HALVES[0], on_vector, late[:, :WIDTH].bitcast(F32)))
+        for name in ("dom", "qm"):
+            group_rows(name, 1, HALVES[1], on_gpsimd)
+        scatter(1, 1, HALVES[0], on_vector, copy_out(second_sums[1], HALVES[0], on_vector, dense_buffer(N // 2, "dense_b")))
+        dense0 = copy_out(second_sums[0], WHOLE, on_scalar, dense_buffer(N, "dense_a"))
+        scatter(1, 0, HALVES[0], on_scalar, dense0[:, HALVES[0]])
         quantize("dom", 1, HALVES[1])
-
-        for k in range(D // P):
-            scatter(1, k, WHOLE, copy_out(sums(1, k, shared_banks[k]), WHOLE, "dense%d" % k))
-            nc.sync.dma_start(out[P * k : P * (k + 1), :], windows[k][:])
+        for cols in BLOCKS[2:]:
+            quantize("qm", 1, cols)
+        for k, bank_name in ((3, "slope_bank3"), (2, "score_bank0")):
+            second_sums[k] = sums(1, [(k, WHOLE)], bank_name)
+        rest = late[:, 3 * WIDTH : 4 * WIDTH].bitcast(F32)
+        scatter(1, 1, HALVES[1], on_vector, copy_out(second_sums[1], HALVES[1], on_vector, rest))
+        scatter(1, 0, HALVES[1], on_scalar, dense0[:, HALVES[1]])
+        store(0)
+        store(1)
+        dense3 = copy_out(second_sums[3], WHOLE, on_scalar, dense_buffer(N, "dense_c"))
+        dense2 = copy_out(second_sums[2], WHOLE, on_scalar, dense_buffer(N, "dense_d"))
+        for cols in HALVES:
+            scatter(1, 2, cols, on_scalar, dense2[:, cols])
+        scatter(1, 3, WHOLE, on_vector, dense3)
+        store(3)
+        store(2)

@@ -34,7 +34,10 @@ POOL_LOADS = (
 )
 Q0_GROUPS_ON_VECTOR = 104
 DO0_GROUPS_ON_VECTOR = 168
+LAST_COLUMNS = 16
 DS_FILLER = 64
+SCALAR_PARTS = ((0, 384), (384, 768), (768, 1024))
+PW_ON_SCALAR = 128
 
 
 def tile_attend_gat_sig_c_kernel(tc, qT, cT, doT, rw, qm, dom, offs, out):
@@ -74,9 +77,18 @@ def tile_attend_gat_sig_c_kernel(tc, qT, cT, doT, rw, qm, dom, offs, out):
         gate = keep.tile([P, B, PACK], F32, name="gate")
         nc.sync.dma_start(gate[:], rw.rearrange("b (p t) o -> p b (t o)", t=PACK))
         load(("q", 1), qT[1], "q1")
-        for index, (name, b, src) in enumerate((("do", 1, doT), ("qm", 0, qm), ("dom", 0, dom), ("dom", 1, dom))):
-            load((name, b), src[b], "chunk%d" % index)
-        load(("qm", 1), qm[1], "q1")
+        load(("do", 1), doT[1], "chunk0")
+
+        def load_halves(b, half, buffer_name):
+            raw[("rows", b, half)] = reused([P, PACK, WIDTH], F32, buffer_name)
+            for index, src in enumerate((qm, dom)):
+                nc.sync.dma_start(
+                    raw[("rows", b, half)][:, :, HALVES[index]],
+                    src[b][:, HALVES[half]].rearrange("(p j) c -> p j c", j=PACK),
+                )
+
+        for b, half, buffer_name in ((0, 0, "chunk1"), (1, 0, "chunk2"), (0, 1, "chunk3"), (1, 1, "q1")):
+            load_halves(b, half, buffer_name)
 
         warm_up = keep.tile([P, 1], F32, name="warm_up")
         nc.scalar.activation(warm_up[:], chunks[0][:, 0, 0:1], ACT.Sigmoid)
@@ -120,21 +132,19 @@ def tile_attend_gat_sig_c_kernel(tc, qT, cT, doT, rw, qm, dom, offs, out):
         scales = {}
         for name in FORMAT:
             for b in range(B):
-                if (name, b) not in (("dom", 0), ("ds", 1)):
+                if (name, b) not in (("ds", 1), ("pw", 1)):
                     codes[(name, b)] = keep.tile([P, WIDTH], U32, name="%s%d_codes" % (name, b), align_bytes=64)
-                if (name, b) not in (("dom", 0), ("ds", 1), ("pw", 0)):
+                if (name, b) not in (("ds", 1), ("pw", 1), ("pw", 0)):
                     scales[(name, b)] = keep.tile([P, WIDTH], U8, name="%s%d_scales" % (name, b), align_bytes=64)
-        joint_codes = keep.tile([P, 2 * WIDTH], U32, name="joint_codes", align_bytes=64)
-        joint_scales = keep.tile([P, 2 * WIDTH], U8, name="joint_scales", align_bytes=64)
-
-        def joint_columns(name, cols):
-            first = cols.start + (WIDTH // 2 if name == "ds" else WIDTH * (cols.start // (WIDTH // 2)))
-            return slice(first, first + cols.stop - cols.start)
+        joint_start = {("dom", 0): 0, ("ds", 1): 256, ("dom", 1): 768, ("qm", 1): 1024, ("pw", 1): 1280}
+        joint_width = 1792
+        joint_codes = keep.tile([P, joint_width], U32, name="joint_codes", align_bytes=64)
+        joint_scales = keep.tile([P, joint_width], U8, name="joint_scales", align_bytes=64)
 
         def quantized(name, b, cols):
-            if (name, b) in (("dom", 0), ("ds", 1)):
-                place = joint_columns(name, cols)
-                return joint_codes[:, place].bitcast(E5M2), joint_scales[:, place]
+            if (name, b) in joint_start and (name in ("ds", "pw") or cols.start < WIDTH // 2):
+                place = slice(joint_start[(name, b)] + cols.start, joint_start[(name, b)] + cols.stop)
+                return joint_codes[:, place].bitcast(FORMAT[name]), joint_scales[:, place]
             return codes[(name, b)][:, cols].bitcast(FORMAT[name]), scales[(name, b)][:, cols]
 
         def new_grouped(name, b, cols, buffer_name):
@@ -211,11 +221,23 @@ def tile_attend_gat_sig_c_kernel(tc, qT, cT, doT, rw, qm, dom, offs, out):
                 as_grouped("ds", b, cols), as_planar(slope[b][:, :, cols]), as_planar(neg_pw[b][:, :, cols]), ALU.mult
             )
 
-        def group_pw(b, scaled):
-            scaled(as_grouped("pw", b, WHOLE), as_planar(neg_pw[b][:]), -1.0)
+        def scaled_on_vector(dst, src, factor):
+            nc.vector.tensor_scalar(dst, src, factor, None, ALU.mult)
+
+        def group_pw(b, cols, scaled):
+            scaled(as_grouped("pw", b, cols), as_planar(neg_pw[b][:, :, cols]), -1.0)
 
         def group_rows(name, b, cols, move):
-            move(as_grouped(name, b, cols), as_planar(raw[(name, b)][:, :, cols]))
+            half, first = divmod(cols.start, WIDTH // 2)
+            first = first + HALVES[("qm", "dom").index(name)].start
+            src = raw[("rows", b, half)][:, :, first : first + cols.stop - cols.start]
+            move(as_grouped(name, b, cols), as_planar(src))
+
+        def group_halves(b, half, move, buffer):
+            for index, name in enumerate(("qm", "dom")):
+                piece = buffer[:, 2 * WIDTH * index : 2 * WIDTH * (index + 1)]
+                pieces.setdefault((name, b), []).append((HALVES[half], piece))
+            move(buffer.rearrange("p (c e j) -> p c j e", e=2, j=PACK), as_planar(raw[("rows", b, half)][:]))
 
         def sums(b, parts, bank_name):
             bank = psum.tile([P, N], F32, name=bank_name)
@@ -234,8 +256,8 @@ def tile_attend_gat_sig_c_kernel(tc, qT, cT, doT, rw, qm, dom, offs, out):
         def dense_buffer(width, buffer_name):
             return reused([P, width], F32, buffer_name)[:]
 
-        def scatter(b, k, cols, move, dense):
-            move(windows[k][:].indirect(list_columns(N * b + cols.start, cols.stop - cols.start)), dense)
+        def scatter(k, first_slot, move, dense):
+            move(windows[k][:].indirect(list_columns(first_slot, dense.shape[1])), dense)
 
         def store(k):
             nc.sync.dma_start(out[P * k : P * (k + 1), :], windows[k][:])
@@ -280,7 +302,7 @@ def tile_attend_gat_sig_c_kernel(tc, qT, cT, doT, rw, qm, dom, offs, out):
         quantize("q", 1, WHOLE)
         group_ds(0, HALVES[1])
         new_grouped("pw", 0, WHOLE, "grouped_pw")
-        group_pw(0, scaled_on_scalar)
+        group_pw(0, WHOLE, scaled_on_scalar)
 
         new_grouped("do", 1, HALVES[0], "grouped_a")
         new_grouped("do", 1, HALVES[1], "grouped_d")
@@ -292,18 +314,18 @@ def tile_attend_gat_sig_c_kernel(tc, qT, cT, doT, rw, qm, dom, offs, out):
         scales[("pw", 0)] = reused([P, WIDTH], U8, "grouped_a")
         quantize("pw", 0, WHOLE)
         slopes(1, "grouped_d")
-        new_grouped("qm", 0, WHOLE, "grouped_qm")
-        joint = reused([P, 2 * WIDTH * PACK], BF16, "grouped_ds")
-        for name, b, cols in (("dom", 0, HALVES[0]), ("ds", 1, WHOLE), ("dom", 0, HALVES[1])):
-            place = joint_columns(name, cols)
-            pieces.setdefault((name, b), []).append((cols, joint[:, PACK * place.start : PACK * place.stop]))
+        new_grouped("qm", 0, HALVES[0], "grouped_qm")
+        joint = reused([P, joint_width * PACK], BF16, "grouped_ds")
+        for name, b in joint_start:
+            cols = WHOLE if name in ("ds", "pw") else HALVES[0]
+            first = PACK * joint_start[(name, b)]
+            pieces[(name, b)] = [(cols, joint[:, first : first + PACK * cols.stop])]
 
-        def quantize_joint(half):
-            cols = slice(WIDTH * half, WIDTH * (half + 1))
+        def quantize_joint(first, fmt):
             nc.vector.quantize_mx(
-                out=joint_codes[:, cols].bitcast(E5M2),
-                scales=joint_scales[:, cols],
-                in_=joint[:, PACK * cols.start : PACK * cols.stop],
+                out=joint_codes[:, first : first + WIDTH].bitcast(fmt),
+                scales=joint_scales[:, first : first + WIDTH],
+                in_=joint[:, PACK * first : PACK * (first + WIDTH)],
             )
 
         for name in ("qm", "dom"):
@@ -311,62 +333,67 @@ def tile_attend_gat_sig_c_kernel(tc, qT, cT, doT, rw, qm, dom, offs, out):
         quantize("qm", 0, HALVES[0])
         group_ds(1, HALVES[0])
         group_ds(1, slice(N // 2, N // 2 + DS_FILLER))
-        quantize_joint(0)
-        bank_a = sums(0, [(1, WHOLE)], "score_bank0")
-        bank_b = sums(0, [(0, HALVES[0])], "score_bank1")
-        for name in ("qm", "dom"):
-            group_rows(name, 0, HALVES[1], on_scalar)
-        group_ds(1, slice(N // 2 + DS_FILLER, N))
-        dense_a = copy_out(bank_a, WHOLE, on_scalar, dense_buffer(N, "dense_a"))
-        quantize("qm", 0, HALVES[1])
-        quantize_joint(1)
-        bank_c = sums(0, [(3, HALVES[0]), (0, HALVES[1])], "score_bank2")
-        bank_d = sums(0, [(2, WHOLE)], "score_bank3")
-        bank_e = sums(0, [(3, HALVES[1])], "slope_bank0")
-
-        late = reused([P, 9 * WIDTH], BF16, "grouped_ds")
-        pieces[("pw", 1)] = [(WHOLE, late[:, : 4 * WIDTH])]
-        pieces[("dom", 1)] = [(HALVES[0], late[:, 5 * WIDTH : 7 * WIDTH]), (HALVES[1], late[:, WIDTH : 3 * WIDTH])]
-        pieces[("qm", 1)] = [(HALVES[0], late[:, 7 * WIDTH :]), (HALVES[1], late[:, 3 * WIDTH : 5 * WIDTH])]
-        scatter(0, 1, WHOLE, on_vector, dense_a)
-        dense_b = copy_out(bank_b, HALVES[0], on_scalar, dense_buffer(N // 2, "dense_b"))
-        for name in ("dom", "qm"):
-            group_rows(name, 1, HALVES[0], on_gpsimd)
-        group_pw(1, scaled_on_gpsimd)
-        scatter(0, 0, HALVES[0], on_scalar, dense_b)
-        dense_c = copy_out(bank_c, WHOLE, on_scalar, dense_buffer(N, "dense_c"))
-        dense_d = copy_out(bank_d, WHOLE, on_scalar, dense_buffer(N, "dense_d"))
-        scatter(0, 0, HALVES[1], on_scalar, dense_c[:, HALVES[1]])
-        scatter(0, 3, HALVES[0], on_vector, dense_c[:, HALVES[0]])
-        for name in ("dom", "qm"):
-            quantize(name, 1, HALVES[0])
-        for cols in HALVES:
-            quantize("pw", 1, cols)
-        for cols in HALVES:
-            scatter(0, 2, cols, on_scalar, dense_d[:, cols])
+        quantize_joint(0, E5M2)
+        first_sums = [None] * PACK
         second_sums = [None] * PACK
         for k in (0, 1):
-            second_sums[k] = sums(1, [(k, WHOLE)], "slope_bank%d" % (k + 1))
-        scatter(0, 3, HALVES[1], on_vector, copy_out(bank_e, HALVES[0], on_vector, late[:, :WIDTH].bitcast(F32)))
+            first_sums[k] = sums(0, [(k, WHOLE)], "score_bank%d" % k)
         for name in ("dom", "qm"):
-            group_rows(name, 1, HALVES[1], on_gpsimd)
-        scatter(1, 1, HALVES[0], on_vector, copy_out(second_sums[1], HALVES[0], on_vector, dense_buffer(N // 2, "dense_b")))
-        dense0 = copy_out(second_sums[0], WHOLE, on_scalar, dense_buffer(N, "dense_a"))
-        scatter(1, 0, HALVES[0], on_scalar, dense0[:, HALVES[0]])
-        quantize("dom", 1, HALVES[1])
-        for cols in BLOCKS[2:]:
-            quantize("qm", 1, cols)
-        for k, bank_name in ((3, "slope_bank3"), (2, "score_bank0")):
-            second_sums[k] = sums(1, [(k, WHOLE)], bank_name)
-        rest = late[:, 3 * WIDTH : 4 * WIDTH].bitcast(F32)
-        scatter(1, 1, HALVES[1], on_vector, copy_out(second_sums[1], HALVES[1], on_vector, rest))
-        scatter(1, 0, HALVES[1], on_scalar, dense0[:, HALVES[1]])
+            group_rows(name, 1, HALVES[0], on_scalar)
+        group_pw(1, slice(0, PW_ON_SCALAR), scaled_on_scalar)
+        group_ds(1, slice(N // 2 + DS_FILLER, N))
+        group_pw(1, slice(PW_ON_SCALAR, N), scaled_on_vector)
+        quantize_joint(WIDTH, E5M2)
+        quantize("pw", 1, HALVES[1])
+        both = [dense_buffer(B * N, "both%d" % index) for index in range(2)]
+        copy_out(first_sums[0], WHOLE, on_scalar, both[0][:, :N])
+        dense = copy_out(first_sums[1], WHOLE, on_scalar, dense_buffer(N, "dense_a"))
+        quantize_joint(2 * WIDTH, E4M3)
+        for k in (0, 1):
+            second_sums[k] = sums(1, [(k, WHOLE)], "score_bank%d" % (k + 2))
+
+        def scatter_on_scalar(k, part):
+            first, stop = SCALAR_PARTS[part]
+            scatter(k, first, on_scalar, both[k // 2][:, first:stop])
+
+        def quantize_late_halves(b):
+            quantize("dom", b, BLOCKS[2])
+            quantize("qm", b, HALVES[1])
+            quantize("dom", b, BLOCKS[3])
+
+        bulk = N - LAST_COLUMNS
+        late = reused([P, bulk + 3 * N // 2 + 2 * N], F32, "grouped_ds")
+        scatter(1, 0, on_vector, dense)
+        group_halves(0, 1, on_gpsimd, late[:, bulk : bulk + 2 * N].bitcast(BF16))
+        scatter_on_scalar(0, 0)
+
+        held = late[:, :N]
+        copy_out(second_sums[0], WHOLE, on_scalar, both[0][:, N:])
+        copy_out(second_sums[1], slice(0, bulk), on_scalar, held[:, :bulk])
+        quantize_late_halves(0)
+        for index, k in enumerate((2, 3)):
+            first_sums[k] = sums(0, [(k, WHOLE)], "slope_bank%d" % index)
+        copy_out(second_sums[1], slice(bulk, N), on_vector, held[:, bulk:])
+        scatter(1, N, on_vector, held)
+        group_halves(1, 1, on_gpsimd, late[:, bulk + 3 * N // 2 :].bitcast(BF16))
+        for part in (1, 2):
+            scatter_on_scalar(0, part)
         store(0)
         store(1)
-        dense3 = copy_out(second_sums[3], WHOLE, on_scalar, dense_buffer(N, "dense_c"))
-        dense2 = copy_out(second_sums[2], WHOLE, on_scalar, dense_buffer(N, "dense_d"))
-        for cols in HALVES:
-            scatter(1, 2, cols, on_scalar, dense2[:, cols])
-        scatter(1, 3, WHOLE, on_vector, dense3)
-        store(3)
+
+        held = late[:, 3 * N // 2 : 3 * N // 2 + N]
+        copy_out(first_sums[2], WHOLE, on_scalar, both[1][:, :N])
+        copy_out(first_sums[3], slice(0, bulk), on_scalar, held[:, :bulk])
+        scatter_on_scalar(2, 0)
+        quantize_late_halves(1)
+        for index, k in enumerate((2, 3)):
+            second_sums[k] = sums(1, [(k, WHOLE)], "slope_bank%d" % (index + 2))
+        copy_out(first_sums[3], slice(bulk, N), on_vector, held[:, bulk:])
+        scatter(3, 0, on_vector, held)
+        copy_out(second_sums[2], WHOLE, on_scalar, both[1][:, N:])
+        dense = copy_out(second_sums[3], WHOLE, on_scalar, dense_buffer(N, "dense_a"))
+        for part in (1, 2):
+            scatter_on_scalar(2, part)
         store(2)
+        scatter(3, N, on_vector, dense)
+        store(3)

@@ -32,12 +32,13 @@ POOL_LOADS = (
     (1, T // 2, T - T // 8, T // 2 - T // 8),
     (1, T - T // 8, T, 160),
 )
-Q0_GROUPS_ON_VECTOR = 104
+Q0_GROUPS_ON_VECTOR = 168
 DO0_GROUPS_ON_VECTOR = 168
 LAST_COLUMNS = 16
 DS_FILLER = 64
 SCALAR_PARTS = ((0, 384), (384, 768), (768, 1024))
 PW_ON_SCALAR = 128
+LATE_PARTS = ((0, 256), (256, 512), (512, 768), (768, 1024))
 
 
 def tile_attend_gat_sig_c_kernel(tc, qT, cT, doT, rw, qm, dom, offs, out):
@@ -79,8 +80,12 @@ def tile_attend_gat_sig_c_kernel(tc, qT, cT, doT, rw, qm, dom, offs, out):
         load(("q", 1), qT[1], "q1")
         load(("do", 1), doT[1], "chunk0")
 
+        rows_tile = {}
+
         def load_halves(b, half, buffer_name):
-            raw[("rows", b, half)] = reused([P, PACK, WIDTH], F32, buffer_name)
+            spare = (N - LAST_COLUMNS) * half
+            rows_tile[(b, half)] = reused([P, spare + PACK * WIDTH], F32, buffer_name)
+            raw[("rows", b, half)] = rows_tile[(b, half)][:, spare:].rearrange("p (j c) -> p j c", j=PACK)
             for index, src in enumerate((qm, dom)):
                 nc.sync.dma_start(
                     raw[("rows", b, half)][:, :, HALVES[index]],
@@ -132,14 +137,20 @@ def tile_attend_gat_sig_c_kernel(tc, qT, cT, doT, rw, qm, dom, offs, out):
         scales = {}
         for name in FORMAT:
             for b in range(B):
-                if (name, b) not in (("ds", 1), ("pw", 1)):
+                if (name, b) not in (("ds", 1), ("pw", 1), ("latent", 0), ("q", 0)):
                     codes[(name, b)] = keep.tile([P, WIDTH], U32, name="%s%d_codes" % (name, b), align_bytes=64)
-                if (name, b) not in (("ds", 1), ("pw", 1), ("pw", 0)):
+                if (name, b) not in (("ds", 1), ("pw", 1), ("latent", 0), ("q", 0), ("pw", 0)):
                     scales[(name, b)] = keep.tile([P, WIDTH], U8, name="%s%d_scales" % (name, b), align_bytes=64)
         joint_start = {("dom", 0): 0, ("ds", 1): 256, ("dom", 1): 768, ("qm", 1): 1024, ("pw", 1): 1280}
         joint_width = 1792
         joint_codes = keep.tile([P, joint_width], U32, name="joint_codes", align_bytes=64)
         joint_scales = keep.tile([P, joint_width], U8, name="joint_scales", align_bytes=64)
+
+        first_codes = keep.tile([P, 2 * WIDTH], U32, name="first_codes", align_bytes=64)
+        first_scales = keep.tile([P, 2 * WIDTH], U8, name="first_scales", align_bytes=64)
+        for index, name in enumerate(("latent", "q")):
+            codes[(name, 0)] = first_codes[:, WIDTH * index : WIDTH * (index + 1)]
+            scales[(name, 0)] = first_scales[:, WIDTH * index : WIDTH * (index + 1)]
 
         def quantized(name, b, cols):
             if (name, b) in joint_start and (name in ("ds", "pw") or cols.start < WIDTH // 2):
@@ -206,8 +217,8 @@ def tile_attend_gat_sig_c_kernel(tc, qT, cT, doT, rw, qm, dom, offs, out):
         def on_gpsimd(dst, src):
             scaled_on_gpsimd(dst, src, 1.0)
 
-        def slopes(b, buffer_name):
-            gated = [scaled_on_gpsimd] * (PACK - 1) + [scaled_on_scalar]
+        def slopes(b, buffer_name, last_gate):
+            gated = [scaled_on_gpsimd] * (PACK - 1) + [last_gate]
             neg_pw[b] = reused([P, PACK, N], F32, buffer_name)
             slope[b] = reused([P, PACK, N], F32, "slope")
             for t in range(PACK):
@@ -273,16 +284,21 @@ def tile_attend_gat_sig_c_kernel(tc, qT, cT, doT, rw, qm, dom, offs, out):
                 if split < P:
                     on_scalar(dst[h][:, split:], src[:, h, split:])
 
-        new_grouped("latent", 0, WHOLE, "grouped_a")
+        first_grouped = reused([P, 2 * WIDTH * PACK], BF16, "grouped_a")
+        for index, name in enumerate(("latent", "q")):
+            pieces[(name, 0)] = [(WHOLE, first_grouped[:, index * WIDTH * PACK : (index + 1) * WIDTH * PACK])]
         group_latents(0, HALVES[0], nc.scalar.copy)
         gather(1, N, N // 2)
-        group_latents(0, HALVES[1], words_on_vector)
-        for cols in HALVES:
-            quantize("latent", 0, cols)
-        new_grouped("q", 0, WHOLE, "grouped_b")
+        group_latents(0, HALVES[1], nc.scalar.copy)
+        quantize("latent", 0, HALVES[0])
         cast_queries("q", 0, Q0_GROUPS_ON_VECTOR)
-        for cols in HALVES:
-            quantize("q", 0, cols)
+        middle = slice(WIDTH // 2, WIDTH + WIDTH // 2)
+        nc.vector.quantize_mx(
+            out=first_codes[:, middle].bitcast(E4M3),
+            scales=first_scales[:, middle],
+            in_=first_grouped[:, PACK * middle.start : PACK * middle.stop],
+        )
+        quantize("q", 0, HALVES[1])
         new_grouped("latent", 1, WHOLE, "q0")
         group_latents(1, HALVES[0], nc.scalar.copy)
         pieces[("do", 0)] = [(HALVES[0], picked_row[:, 2 * B * N - N // 2 :].bitcast(BF16))]
@@ -292,7 +308,7 @@ def tile_attend_gat_sig_c_kernel(tc, qT, cT, doT, rw, qm, dom, offs, out):
         for cols in HALVES:
             quantize("do", 0, cols)
         gather(1, N + N // 2, N // 2)
-        slopes(0, "grouped_c")
+        slopes(0, "grouped_c", scaled_on_scalar)
         group_latents(1, HALVES[1], nc.scalar.copy)
         quantize("latent", 1, WHOLE)
         new_grouped("q", 1, WHOLE, "grouped_b")
@@ -313,19 +329,22 @@ def tile_attend_gat_sig_c_kernel(tc, qT, cT, doT, rw, qm, dom, offs, out):
             quantize("do", 1, cols)
         scales[("pw", 0)] = reused([P, WIDTH], U8, "grouped_a")
         quantize("pw", 0, WHOLE)
-        slopes(1, "grouped_d")
+        slopes(1, "grouped_d", scaled_on_scalar)
         new_grouped("qm", 0, HALVES[0], "grouped_qm")
-        joint = reused([P, joint_width * PACK], BF16, "grouped_ds")
-        for name, b in joint_start:
-            cols = WHOLE if name in ("ds", "pw") else HALVES[0]
-            first = PACK * joint_start[(name, b)]
-            pieces[(name, b)] = [(cols, joint[:, first : first + PACK * cols.stop])]
+        joint = reused([P, 3 * WIDTH * PACK], BF16, "grouped_ds")
+        closing = reused([P, WIDTH // 2 * PACK], BF16, "grouped_pw")
+        half = WIDTH // 2 * PACK
+        pieces[("dom", 0)] = [(HALVES[0], joint[:, :half])]
+        pieces[("ds", 1)] = [(WHOLE, joint[:, half : 3 * half])]
+        pieces[("dom", 1)] = [(HALVES[0], joint[:, 3 * half : 4 * half])]
+        pieces[("qm", 1)] = [(HALVES[0], joint[:, 4 * half : 5 * half])]
+        pieces[("pw", 1)] = [(HALVES[0], joint[:, 5 * half :]), (HALVES[1], closing[:])]
 
-        def quantize_joint(first, fmt):
+        def quantize_joint(first, fmt, grouped):
             nc.vector.quantize_mx(
                 out=joint_codes[:, first : first + WIDTH].bitcast(fmt),
                 scales=joint_scales[:, first : first + WIDTH],
-                in_=joint[:, PACK * first : PACK * (first + WIDTH)],
+                in_=grouped,
             )
 
         for name in ("qm", "dom"):
@@ -333,7 +352,7 @@ def tile_attend_gat_sig_c_kernel(tc, qT, cT, doT, rw, qm, dom, offs, out):
         quantize("qm", 0, HALVES[0])
         group_ds(1, HALVES[0])
         group_ds(1, slice(N // 2, N // 2 + DS_FILLER))
-        quantize_joint(0, E5M2)
+        quantize_joint(0, E5M2, joint[:, : 2 * half])
         first_sums = [None] * PACK
         second_sums = [None] * PACK
         for k in (0, 1):
@@ -342,13 +361,14 @@ def tile_attend_gat_sig_c_kernel(tc, qT, cT, doT, rw, qm, dom, offs, out):
             group_rows(name, 1, HALVES[0], on_scalar)
         group_pw(1, slice(0, PW_ON_SCALAR), scaled_on_scalar)
         group_ds(1, slice(N // 2 + DS_FILLER, N))
-        group_pw(1, slice(PW_ON_SCALAR, N), scaled_on_vector)
-        quantize_joint(WIDTH, E5M2)
+        group_pw(1, slice(PW_ON_SCALAR, N // 2), scaled_on_vector)
+        group_pw(1, HALVES[1], scaled_on_vector)
+        quantize_joint(WIDTH, E5M2, joint[:, 2 * half : 4 * half])
+        quantize_joint(2 * WIDTH, E4M3, joint[:, 4 * half :])
         quantize("pw", 1, HALVES[1])
         both = [dense_buffer(B * N, "both%d" % index) for index in range(2)]
         copy_out(first_sums[0], WHOLE, on_scalar, both[0][:, :N])
         dense = copy_out(first_sums[1], WHOLE, on_scalar, dense_buffer(N, "dense_a"))
-        quantize_joint(2 * WIDTH, E4M3)
         for k in (0, 1):
             second_sums[k] = sums(1, [(k, WHOLE)], "score_bank%d" % (k + 2))
 
@@ -357,43 +377,46 @@ def tile_attend_gat_sig_c_kernel(tc, qT, cT, doT, rw, qm, dom, offs, out):
             scatter(k, first, on_scalar, both[k // 2][:, first:stop])
 
         def quantize_late_halves(b):
-            quantize("dom", b, BLOCKS[2])
-            quantize("qm", b, HALVES[1])
-            quantize("dom", b, BLOCKS[3])
+            for name in ("dom", "qm"):
+                quantize(name, b, HALVES[1])
 
         bulk = N - LAST_COLUMNS
-        late = reused([P, bulk + 3 * N // 2 + 2 * N], F32, "grouped_ds")
+        late = reused([P, 3 * N], F32, "grouped_ds")
         scatter(1, 0, on_vector, dense)
-        group_halves(0, 1, on_gpsimd, late[:, bulk : bulk + 2 * N].bitcast(BF16))
+        group_halves(0, 1, on_gpsimd, late[:, : 2 * N].bitcast(BF16))
         scatter_on_scalar(0, 0)
 
-        held = late[:, :N]
-        copy_out(second_sums[0], WHOLE, on_scalar, both[0][:, N:])
-        copy_out(second_sums[1], slice(0, bulk), on_scalar, held[:, :bulk])
+        held = rows_tile[(0, 1)][:, :N]
+        for cols in HALVES:
+            copy_out(second_sums[0], cols, on_scalar, both[0][:, N + cols.start : N + cols.stop])
+        copy_out(second_sums[1], slice(0, bulk), on_vector, held[:, :bulk])
+        copy_out(second_sums[1], slice(bulk, N), on_vector, held[:, bulk:])
         quantize_late_halves(0)
         for index, k in enumerate((2, 3)):
             first_sums[k] = sums(0, [(k, WHOLE)], "slope_bank%d" % index)
-        copy_out(second_sums[1], slice(bulk, N), on_vector, held[:, bulk:])
         scatter(1, N, on_vector, held)
-        group_halves(1, 1, on_gpsimd, late[:, bulk + 3 * N // 2 :].bitcast(BF16))
+        group_halves(1, 1, on_gpsimd, late[:, N:].bitcast(BF16))
         for part in (1, 2):
             scatter_on_scalar(0, part)
         store(0)
         store(1)
 
-        held = late[:, 3 * N // 2 : 3 * N // 2 + N]
-        copy_out(first_sums[2], WHOLE, on_scalar, both[1][:, :N])
-        copy_out(first_sums[3], slice(0, bulk), on_scalar, held[:, :bulk])
-        scatter_on_scalar(2, 0)
-        quantize_late_halves(1)
-        for index, k in enumerate((2, 3)):
-            second_sums[k] = sums(1, [(k, WHOLE)], "slope_bank%d" % (index + 2))
+        held = rows_tile[(1, 1)][:, :N]
+        for cols in HALVES:
+            copy_out(first_sums[2], cols, on_scalar, both[1][:, cols])
+        copy_out(first_sums[3], slice(0, bulk), on_vector, held[:, :bulk])
+        for first, stop in LATE_PARTS[:-2]:
+            scatter(2, first, on_scalar, both[1][:, first:stop])
         copy_out(first_sums[3], slice(bulk, N), on_vector, held[:, bulk:])
+        quantize_late_halves(1)
+        halves = [sums(1, [(2, cols)], bank_name) for cols, bank_name in zip(HALVES, ("slope_bank2", "score_bank0"))]
+        second_sums[3] = sums(1, [(3, WHOLE)], "slope_bank3")
         scatter(3, 0, on_vector, held)
-        copy_out(second_sums[2], WHOLE, on_scalar, both[1][:, N:])
-        dense = copy_out(second_sums[3], WHOLE, on_scalar, dense_buffer(N, "dense_a"))
-        for part in (1, 2):
-            scatter_on_scalar(2, part)
+        for cols, bank in zip(HALVES, halves):
+            copy_out(bank, HALVES[0], on_scalar, both[1][:, N + cols.start : N + cols.stop])
+        dense = copy_out(second_sums[3], WHOLE, on_vector, dense_buffer(N, "dense_a"))
+        for first, stop in LATE_PARTS[-2:]:
+            scatter(2, first, on_scalar, both[1][:, first:stop])
         store(2)
         scatter(3, N, on_vector, dense)
         store(3)

@@ -35,6 +35,7 @@ POOL_LOADS = (
 Q0_GROUPS_ON_VECTOR = 168
 DO0_GROUPS_ON_VECTOR = 168
 LAST_COLUMNS = 16
+COPY_RUN = 4
 DS_FILLER = 64
 SCALAR_PARTS = ((0, 384), (384, 768), (768, 1024))
 PW_ON_SCALAR = 128
@@ -166,11 +167,11 @@ def tile_attend_gat_sig_c_kernel(tc, qT, cT, doT, rw, qm, dom, offs, out):
             held, buffer = [x for x in pieces[(name, b)] if x[0].start <= cols.start and cols.stop <= x[0].stop][0]
             return buffer[:, PACK * (cols.start - held.start) : PACK * (cols.stop - held.start)]
 
-        def as_grouped(name, b, cols):
-            return grouped_columns(name, b, cols).rearrange("p (c e j) -> p c j e", e=2, j=PACK)
+        def as_grouped(name, b, cols, run):
+            return grouped_columns(name, b, cols).rearrange("p (c e j) -> p c j e", e=run, j=PACK)
 
-        def as_planar(view):
-            return view.rearrange("p j (c e) -> p c j e", e=2)
+        def as_planar(view, run):
+            return view.rearrange("p j (c e) -> p c j e", e=run)
 
         def group_latents(b, cols, move):
             src = picked[:, :, N * b + cols.start : N * b + cols.stop]
@@ -229,26 +230,30 @@ def tile_attend_gat_sig_c_kernel(tc, qT, cT, doT, rw, qm, dom, offs, out):
 
         def group_ds(b, cols):
             nc.vector.tensor_tensor(
-                as_grouped("ds", b, cols), as_planar(slope[b][:, :, cols]), as_planar(neg_pw[b][:, :, cols]), ALU.mult
+                as_grouped("ds", b, cols, 2),
+                as_planar(slope[b][:, :, cols], 2),
+                as_planar(neg_pw[b][:, :, cols], 2),
+                ALU.mult,
             )
 
         def scaled_on_vector(dst, src, factor):
             nc.vector.tensor_scalar(dst, src, factor, None, ALU.mult)
 
         def group_pw(b, cols, scaled):
-            scaled(as_grouped("pw", b, cols), as_planar(neg_pw[b][:, :, cols]), -1.0)
+            scaled(as_grouped("pw", b, cols, COPY_RUN), as_planar(neg_pw[b][:, :, cols], COPY_RUN), -1.0)
 
         def group_rows(name, b, cols, move):
             half, first = divmod(cols.start, WIDTH // 2)
             first = first + HALVES[("qm", "dom").index(name)].start
             src = raw[("rows", b, half)][:, :, first : first + cols.stop - cols.start]
-            move(as_grouped(name, b, cols), as_planar(src))
+            move(as_grouped(name, b, cols, COPY_RUN), as_planar(src, COPY_RUN))
 
         def group_halves(b, half, move, buffer):
             for index, name in enumerate(("qm", "dom")):
                 piece = buffer[:, 2 * WIDTH * index : 2 * WIDTH * (index + 1)]
                 pieces.setdefault((name, b), []).append((HALVES[half], piece))
-            move(buffer.rearrange("p (c e j) -> p c j e", e=2, j=PACK), as_planar(raw[("rows", b, half)][:]))
+            dst = buffer.rearrange("p (c e j) -> p c j e", e=COPY_RUN, j=PACK)
+            move(dst, as_planar(raw[("rows", b, half)][:], COPY_RUN))
 
         def sums(b, parts, bank_name):
             bank = psum.tile([P, N], F32, name=bank_name)

@@ -35,10 +35,10 @@ POOL_LOADS = (
 Q0_GROUPS_ON_VECTOR = 168
 DO0_GROUPS_ON_VECTOR = 168
 LAST_COLUMNS = 16
+PW0_ON_VECTOR = 192
 COPY_RUN = 4
-DS_FILLER = 64
-SCALAR_PARTS = ((0, 384), (384, 768), (768, 1024))
-PW_ON_SCALAR = 128
+SCALAR_PARTS = ((0, 256), (256, 512), (512, 768), (768, 1024))
+PW_ON_SCALAR = 64
 LATE_PARTS = ((0, 256), (256, 512), (512, 768), (768, 1024))
 
 
@@ -313,7 +313,7 @@ def tile_attend_gat_sig_c_kernel(tc, qT, cT, doT, rw, qm, dom, offs, out):
         for cols in HALVES:
             quantize("do", 0, cols)
         gather(1, N + N // 2, N // 2)
-        slopes(0, "grouped_c", scaled_on_scalar)
+        slopes(0, "grouped_c", scaled_on_gpsimd)
         group_latents(1, HALVES[1], nc.scalar.copy)
         quantize("latent", 1, WHOLE)
         new_grouped("q", 1, WHOLE, "grouped_b")
@@ -323,12 +323,13 @@ def tile_attend_gat_sig_c_kernel(tc, qT, cT, doT, rw, qm, dom, offs, out):
         quantize("q", 1, WHOLE)
         group_ds(0, HALVES[1])
         new_grouped("pw", 0, WHOLE, "grouped_pw")
-        group_pw(0, WHOLE, scaled_on_scalar)
+        group_pw(0, slice(0, N - PW0_ON_VECTOR), scaled_on_scalar)
 
         new_grouped("do", 1, HALVES[0], "grouped_a")
         new_grouped("do", 1, HALVES[1], "grouped_d")
         cast_queries("do", 1, 2 * P)
         scores(1, "prob")
+        group_pw(0, slice(N - PW0_ON_VECTOR, N), scaled_on_vector)
         quantize("ds", 0, WHOLE)
         for cols in HALVES:
             quantize("do", 1, cols)
@@ -354,10 +355,8 @@ def tile_attend_gat_sig_c_kernel(tc, qT, cT, doT, rw, qm, dom, offs, out):
 
         for name in ("qm", "dom"):
             group_rows(name, 0, HALVES[0], on_scalar)
-        quantize("qm", 0, HALVES[0])
-        group_ds(1, HALVES[0])
-        group_ds(1, slice(N // 2, N // 2 + DS_FILLER))
-        quantize_joint(0, E5M2, joint[:, : 2 * half])
+        for name in ("qm", "dom"):
+            quantize(name, 0, HALVES[0])
         first_sums = [None] * PACK
         second_sums = [None] * PACK
         for k in (0, 1):
@@ -365,7 +364,9 @@ def tile_attend_gat_sig_c_kernel(tc, qT, cT, doT, rw, qm, dom, offs, out):
         for name in ("dom", "qm"):
             group_rows(name, 1, HALVES[0], on_scalar)
         group_pw(1, slice(0, PW_ON_SCALAR), scaled_on_scalar)
-        group_ds(1, slice(N // 2 + DS_FILLER, N))
+        for cols in HALVES:
+            group_ds(1, cols)
+        quantize("ds", 1, HALVES[0])
         group_pw(1, slice(PW_ON_SCALAR, N // 2), scaled_on_vector)
         group_pw(1, HALVES[1], scaled_on_vector)
         quantize_joint(WIDTH, E5M2, joint[:, 2 * half : 4 * half])
@@ -389,7 +390,8 @@ def tile_attend_gat_sig_c_kernel(tc, qT, cT, doT, rw, qm, dom, offs, out):
         late = reused([P, 3 * N], F32, "grouped_ds")
         scatter(1, 0, on_vector, dense)
         group_halves(0, 1, on_gpsimd, late[:, : 2 * N].bitcast(BF16))
-        scatter_on_scalar(0, 0)
+        for part in (0, 1):
+            scatter_on_scalar(0, part)
 
         held = rows_tile[(0, 1)][:, :N]
         for cols in HALVES:
@@ -401,7 +403,7 @@ def tile_attend_gat_sig_c_kernel(tc, qT, cT, doT, rw, qm, dom, offs, out):
             first_sums[k] = sums(0, [(k, WHOLE)], "slope_bank%d" % index)
         scatter(1, N, on_vector, held)
         group_halves(1, 1, on_gpsimd, late[:, N:].bitcast(BF16))
-        for part in (1, 2):
+        for part in (2, 3):
             scatter_on_scalar(0, part)
         store(0)
         store(1)

@@ -19,27 +19,26 @@ ALU = mybir.AluOpType
 P = 128
 PACK = 4
 WIDTH = 512
+HALF = WIDTH // 2
 SLOTS_PER_COLUMN = 16
 
 WHOLE = slice(0, WIDTH)
-HALVES = (slice(0, WIDTH // 2), slice(WIDTH // 2, WIDTH))
+HALVES = (slice(0, HALF), slice(HALF, WIDTH))
 BLOCKS = tuple(slice(P * k, P * (k + 1)) for k in range(WIDTH // P))
 FORMAT = {"q": E4M3, "latent": E4M3, "do": E5M2, "qm": E4M3, "ds": E5M2, "dom": E5M2, "pw": E4M3}
 
 POOL_LOADS = (
-    (0, 0, T, 1376),
+    (0, 0, T // 2, 0),
+    (0, T // 2, T, 640),
     (1, 0, T // 2, 0),
-    (1, T // 2, T - T // 8, T // 2 - T // 8),
+    (1, T // 2, T - T // 8, 640),
     (1, T - T // 8, T, 160),
 )
-Q0_GROUPS_ON_VECTOR = 168
-DO0_GROUPS_ON_VECTOR = 168
+SHARED_GROUPS_ON_VECTOR = 40
+PW_COLUMNS_ON_SCALAR = 128
 LAST_COLUMNS = 16
-PW0_ON_VECTOR = 192
 COPY_RUN = 4
-SCALAR_PARTS = ((0, 256), (256, 512), (512, 768), (768, 1024))
-PW_ON_SCALAR = 64
-LATE_PARTS = ((0, 256), (256, 512), (512, 768), (768, 1024))
+PRODUCT_RUN = 2
 
 
 def tile_attend_gat_sig_c_kernel(tc, qT, cT, doT, rw, qm, dom, offs, out):
@@ -65,51 +64,53 @@ def tile_attend_gat_sig_c_kernel(tc, qT, cT, doT, rw, qm, dom, offs, out):
         for index, (u, first, stop, on_vector_tokens) in enumerate(POOL_LOADS):
             chunks.append(reused([P, 2, stop - first], F32, "chunk%d" % index))
             nc.sync.dma_start(chunks[index][:], pool_rows[u][:, :, first:stop])
-            if index == 0:
+            if (u, stop) == (0, T):
                 nc.sync.dma_start(offsets[:], offs)
 
-        raw = {}
+        queries = {}
 
-        def load(key, src, buffer_name):
-            raw[key] = reused([P, PACK, src.shape[1]], F32, buffer_name)
-            nc.sync.dma_start(raw[key][:], src.rearrange("(p j) c -> p j c", j=PACK))
+        def load_queries(name, b, src, buffer_name):
+            queries[(name, b)] = reused([P, PACK, R], F32, buffer_name)
+            nc.sync.dma_start(queries[(name, b)][:], src[b].rearrange("(p j) c -> p j c", j=PACK))
 
-        load(("q", 0), qT[0], "q0")
-        load(("do", 0), doT[0], "do0")
+        load_queries("q", 0, qT, "q0")
+        load_queries("do", 0, doT, "do0")
         gate = keep.tile([P, B, PACK], F32, name="gate")
         nc.sync.dma_start(gate[:], rw.rearrange("b (p t) o -> p b (t o)", t=PACK))
-        load(("q", 1), qT[1], "q1")
-        load(("do", 1), doT[1], "chunk0")
+        load_queries("q", 1, qT, "q1")
+        load_queries("do", 1, doT, "chunk0")
 
-        rows_tile = {}
+        rows = {}
+        in_front = {}
 
-        def load_halves(b, half, buffer_name):
+        def load_rows(b, half, buffer_name):
             spare = (N - LAST_COLUMNS) * half
-            rows_tile[(b, half)] = reused([P, spare + PACK * WIDTH], F32, buffer_name)
-            raw[("rows", b, half)] = rows_tile[(b, half)][:, spare:].rearrange("p (j c) -> p j c", j=PACK)
+            tile = reused([P, spare + PACK * WIDTH], F32, buffer_name)
+            rows[(b, half)] = tile[:, spare:].rearrange("p (j c) -> p j c", j=PACK)
+            in_front[(b, half)] = tile[:, :N]
             for index, src in enumerate((qm, dom)):
                 nc.sync.dma_start(
-                    raw[("rows", b, half)][:, :, HALVES[index]],
+                    rows[(b, half)][:, :, HALVES[index]],
                     src[b][:, HALVES[half]].rearrange("(p j) c -> p j c", j=PACK),
                 )
 
         for b, half, buffer_name in ((0, 0, "chunk1"), (1, 0, "chunk2"), (0, 1, "chunk3"), (1, 1, "q1")):
-            load_halves(b, half, buffer_name)
+            load_rows(b, half, buffer_name)
 
         warm_up = keep.tile([P, 1], F32, name="warm_up")
         nc.scalar.activation(warm_up[:], chunks[0][:, 0, 0:1], ACT.Sigmoid)
 
         pairs = [keep.tile([P, T, 2], BF16, name="pairs%d" % u) for u in range(2)]
-        picked_row = keep.tile([P, 2 * B * N + N // 2], U32, name="picked", align_bytes=64)
+        picked_row = keep.tile([P, 2 * B * N + HALF], U32, name="picked", align_bytes=64)
         picked = picked_row[:, : 2 * B * N].rearrange("p (u c) -> p u c", u=2)
 
         def pair_up(index):
             u, first, stop, split = POOL_LOADS[index]
             for move, lo, hi in ((on_vector, 0, split), (on_scalar, split, stop - first)):
                 if lo < hi:
-                    src = chunks[index][:, :, lo:hi]
-                    dst = pairs[u][:, first + lo : first + hi, :]
-                    move(dst.rearrange("p (c f) e -> p c e f", f=4), src.rearrange("p e (c f) -> p c e f", f=4))
+                    src = chunks[index][:, :, lo:hi].rearrange("p e (c f) -> p c e f", f=COPY_RUN)
+                    dst = pairs[u][:, first + lo : first + hi, :].rearrange("p (c f) e -> p c e f", f=COPY_RUN)
+                    move(dst, src)
 
         def list_columns(first_slot, count):
             return offsets[:, first_slot // SLOTS_PER_COLUMN : (first_slot + count) // SLOTS_PER_COLUMN]
@@ -120,12 +121,16 @@ def tile_attend_gat_sig_c_kernel(tc, qT, cT, doT, rw, qm, dom, offs, out):
                 picked[:, u, first_slot : first_slot + count], words.indirect(list_columns(first_slot, count))
             )
 
-        pair_up(0)
+        def pair_up_all(u):
+            for index in range(len(POOL_LOADS)):
+                if POOL_LOADS[index][0] == u:
+                    pair_up(index)
+
+        pair_up_all(0)
         gather(0, 0, B * N)
-        for index in range(1, len(POOL_LOADS)):
-            pair_up(index)
+        pair_up_all(1)
         for cols in HALVES:
-            gather(1, cols.start, N // 2)
+            gather(1, cols.start, HALF)
 
         windows = [keep.tile([P, T], F32, name="window%d" % k) for k in range(D // P)]
         for window in windows:
@@ -133,63 +138,99 @@ def tile_attend_gat_sig_c_kernel(tc, qT, cT, doT, rw, qm, dom, offs, out):
         neg_gate = keep.tile([P, B, PACK], F32, name="neg_gate")
         nc.scalar.activation(neg_gate[:], gate[:], ACT.Copy, scale=-1.0)
 
-        pieces = {}
+        grouped = {}
         codes = {}
         scales = {}
-        for name in FORMAT:
-            for b in range(B):
-                if (name, b) not in (("ds", 1), ("pw", 1), ("latent", 0), ("q", 0)):
-                    codes[(name, b)] = keep.tile([P, WIDTH], U32, name="%s%d_codes" % (name, b), align_bytes=64)
-                if (name, b) not in (("ds", 1), ("pw", 1), ("latent", 0), ("q", 0), ("pw", 0)):
-                    scales[(name, b)] = keep.tile([P, WIDTH], U8, name="%s%d_scales" % (name, b), align_bytes=64)
-        joint_start = {("dom", 0): 0, ("ds", 1): 256, ("dom", 1): 768, ("qm", 1): 1024, ("pw", 1): 1280}
-        joint_width = 1792
-        joint_codes = keep.tile([P, joint_width], U32, name="joint_codes", align_bytes=64)
-        joint_scales = keep.tile([P, joint_width], U8, name="joint_scales", align_bytes=64)
 
-        first_codes = keep.tile([P, 2 * WIDTH], U32, name="first_codes", align_bytes=64)
-        first_scales = keep.tile([P, 2 * WIDTH], U8, name="first_scales", align_bytes=64)
-        for index, name in enumerate(("latent", "q")):
-            codes[(name, 0)] = first_codes[:, WIDTH * index : WIDTH * (index + 1)]
-            scales[(name, 0)] = first_scales[:, WIDTH * index : WIDTH * (index + 1)]
+        def enter(table, parts, tile, per_column):
+            first = 0
+            for name, b, cols in parts:
+                stop = first + per_column * (cols.stop - cols.start)
+                table.setdefault((name, b), []).append((cols, tile[:, first:stop]))
+                first = stop
+
+        def look_up(table, name, b, cols, per_column):
+            held, view = [x for x in table[(name, b)] if x[0].start <= cols.start and cols.stop <= x[0].stop][0]
+            return view[:, per_column * (cols.start - held.start) : per_column * (cols.stop - held.start)]
+
+        def width_of(parts):
+            return sum(cols.stop - cols.start for name, b, cols in parts)
+
+        def new_codes(parts, tile_name):
+            tile = keep.tile([P, width_of(parts)], U32, name=tile_name + "_codes", align_bytes=64)
+            enter(codes, parts, tile, 1)
+            return tile
+
+        def new_scales(parts, tile_name):
+            tile = keep.tile([P, width_of(parts)], U8, name=tile_name + "_scales", align_bytes=64)
+            enter(scales, parts, tile, 1)
+            return tile
+
+        def new_grouped(parts, buffer_name):
+            tile = reused([P, width_of(parts) * PACK], BF16, buffer_name)
+            enter(grouped, parts, tile, PACK)
+            return tile
+
+        first_parts = [("latent", 0, WHOLE), ("q", 0, WHOLE)]
+        last_parts = [("ds", 1, WHOLE), ("dom", 1, HALVES[0]), ("qm", 1, HALVES[0]), ("pw", 1, WHOLE)]
+        first_codes, first_scales = new_codes(first_parts, "first"), new_scales(first_parts, "first")
+        last_codes, last_scales = new_codes(last_parts, "last"), new_scales(last_parts, "last")
+        for name, b, cols in [(name, 0, WHOLE) for name in ("do", "qm", "ds", "dom")] + [
+            ("latent", 1, WHOLE),
+            ("q", 1, WHOLE),
+            ("do", 1, WHOLE),
+            ("qm", 1, HALVES[1]),
+            ("dom", 1, HALVES[1]),
+        ]:
+            new_codes([(name, b, cols)], "%s%d" % (name, b))
+            new_scales([(name, b, cols)], "%s%d" % (name, b))
+        new_codes([("pw", 0, WHOLE)], "pw0")
 
         def quantized(name, b, cols):
-            if (name, b) in joint_start and (name in ("ds", "pw") or cols.start < WIDTH // 2):
-                place = slice(joint_start[(name, b)] + cols.start, joint_start[(name, b)] + cols.stop)
-                return joint_codes[:, place].bitcast(FORMAT[name]), joint_scales[:, place]
-            return codes[(name, b)][:, cols].bitcast(FORMAT[name]), scales[(name, b)][:, cols]
-
-        def new_grouped(name, b, cols, buffer_name):
-            buffer = reused([P, (cols.stop - cols.start) * PACK], BF16, buffer_name)
-            pieces.setdefault((name, b), []).append((cols, buffer))
-
-        def grouped_columns(name, b, cols):
-            held, buffer = [x for x in pieces[(name, b)] if x[0].start <= cols.start and cols.stop <= x[0].stop][0]
-            return buffer[:, PACK * (cols.start - held.start) : PACK * (cols.stop - held.start)]
-
-        def as_grouped(name, b, cols, run):
-            return grouped_columns(name, b, cols).rearrange("p (c e j) -> p c j e", e=run, j=PACK)
-
-        def as_planar(view, run):
-            return view.rearrange("p j (c e) -> p c j e", e=run)
-
-        def group_latents(b, cols, move):
-            src = picked[:, :, N * b + cols.start : N * b + cols.stop]
-            dst = grouped_columns("latent", b, cols).bitcast(U32).rearrange("p (c u) -> p c u", u=2)
-            move(dst, src.rearrange("p u c -> p c u"))
-
-        def words_on_vector(dst, src):
-            nc.vector.tensor_copy(dst.bitcast(I32), src.bitcast(I32))
+            return look_up(codes, name, b, cols, 1).bitcast(FORMAT[name]), look_up(scales, name, b, cols, 1)
 
         def quantize(name, b, cols):
             out_codes, out_scales = quantized(name, b, cols)
-            nc.vector.quantize_mx(out=out_codes, scales=out_scales, in_=grouped_columns(name, b, cols))
+            nc.vector.quantize_mx(out=out_codes, scales=out_scales, in_=look_up(grouped, name, b, cols, PACK))
 
-        def product(sums, stationary, block, moving, b, cols, start, stop):
+        def quantize_across(codes_tile, scales_tile, grouped_tile, first, fmt):
+            nc.vector.quantize_mx(
+                out=codes_tile[:, first : first + WIDTH].bitcast(fmt),
+                scales=scales_tile[:, first : first + WIDTH],
+                in_=grouped_tile[:, PACK * first : PACK * (first + WIDTH)],
+            )
+
+        def runs_of_grouped(view, run):
+            return view.rearrange("p (c e j) -> p c j e", e=run, j=PACK)
+
+        def runs_of_planar(view, run):
+            return view.rearrange("p j (c e) -> p c j e", e=run)
+
+        def group_latents(b, cols):
+            src = picked[:, :, N * b + cols.start : N * b + cols.stop]
+            dst = look_up(grouped, "latent", b, cols, PACK).bitcast(U32).rearrange("p (c u) -> p c u", u=2)
+            nc.scalar.copy(dst, src.rearrange("p u c -> p c u"))
+
+        def group_queries(name, b, h, move, groups):
+            dst = look_up(grouped, name, b, HALVES[h], PACK).rearrange("p (e m j) -> p m j e", e=2, j=PACK)
+            src = queries[(name, b)][:].rearrange("p j (m h e) -> p h m j e", h=2, e=2)
+            move(dst[:, groups], src[:, h, groups])
+
+        def group_queries_shared(name):
+            group_queries(name, 0, 0, on_vector, slice(0, P))
+            group_queries(name, 0, 1, on_vector, slice(0, SHARED_GROUPS_ON_VECTOR))
+            group_queries(name, 0, 1, on_scalar, slice(SHARED_GROUPS_ON_VECTOR, P))
+
+        def group_early_half(name, b):
+            src = rows[(b, 0)][:, :, HALVES[("qm", "dom").index(name)]]
+            dst = look_up(grouped, name, b, HALVES[0], PACK)
+            on_scalar(runs_of_grouped(dst, COPY_RUN), runs_of_planar(src, COPY_RUN))
+
+        def product(sums_view, stationary, block, moving, b, cols, start, stop):
             lhs_codes, lhs_scales = quantized(stationary, b, BLOCKS[block])
             rhs_codes, rhs_scales = quantized(moving, b, cols)
             nc.tensor.matmul_mx(
-                out=sums,
+                out=sums_view,
                 lhsT=lhs_codes,
                 lhsT_scale=lhs_scales,
                 rhs=rhs_codes,
@@ -212,15 +253,15 @@ def tile_attend_gat_sig_c_kernel(tc, qT, cT, doT, rw, qm, dom, offs, out):
         def scaled_on_scalar(dst, src, factor):
             nc.scalar.activation(dst, src, ACT.Copy, scale=factor)
 
+        def scaled_on_vector(dst, src, factor):
+            nc.vector.tensor_scalar(dst, src, factor, None, ALU.mult)
+
         def scaled_on_gpsimd(dst, src, factor):
             nc.gpsimd.tensor_scalar(dst, src, factor, 0.0, ALU.mult, ALU.add)
 
-        def on_gpsimd(dst, src):
-            scaled_on_gpsimd(dst, src, 1.0)
-
-        def slopes(b, buffer_name, last_gate):
-            gated = [scaled_on_gpsimd] * (PACK - 1) + [last_gate]
-            neg_pw[b] = reused([P, PACK, N], F32, buffer_name)
+        def slopes(b, neg_pw_buffer, last_gated):
+            gated = [scaled_on_gpsimd] * (PACK - 1) + [last_gated]
+            neg_pw[b] = reused([P, PACK, N], F32, neg_pw_buffer)
             slope[b] = reused([P, PACK, N], F32, "slope")
             for t in range(PACK):
                 bank = psum.tile([P, N], F32, name="slope_bank%d" % t)
@@ -230,47 +271,85 @@ def tile_attend_gat_sig_c_kernel(tc, qT, cT, doT, rw, qm, dom, offs, out):
 
         def group_ds(b, cols):
             nc.vector.tensor_tensor(
-                as_grouped("ds", b, cols, 2),
-                as_planar(slope[b][:, :, cols], 2),
-                as_planar(neg_pw[b][:, :, cols], 2),
+                runs_of_grouped(look_up(grouped, "ds", b, cols, PACK), PRODUCT_RUN),
+                runs_of_planar(slope[b][:, :, cols], PRODUCT_RUN),
+                runs_of_planar(neg_pw[b][:, :, cols], PRODUCT_RUN),
                 ALU.mult,
             )
 
-        def scaled_on_vector(dst, src, factor):
-            nc.vector.tensor_scalar(dst, src, factor, None, ALU.mult)
-
         def group_pw(b, cols, scaled):
-            scaled(as_grouped("pw", b, cols, COPY_RUN), as_planar(neg_pw[b][:, :, cols], COPY_RUN), -1.0)
+            dst = runs_of_grouped(look_up(grouped, "pw", b, cols, PACK), COPY_RUN)
+            scaled(dst, runs_of_planar(neg_pw[b][:, :, cols], COPY_RUN), -1.0)
 
-        def group_rows(name, b, cols, move):
-            half, first = divmod(cols.start, WIDTH // 2)
-            first = first + HALVES[("qm", "dom").index(name)].start
-            src = raw[("rows", b, half)][:, :, first : first + cols.stop - cols.start]
-            move(as_grouped(name, b, cols, COPY_RUN), as_planar(src, COPY_RUN))
-
-        def group_halves(b, half, move, buffer):
-            for index, name in enumerate(("qm", "dom")):
-                piece = buffer[:, 2 * WIDTH * index : 2 * WIDTH * (index + 1)]
-                pieces.setdefault((name, b), []).append((HALVES[half], piece))
-            dst = buffer.rearrange("p (c e j) -> p c j e", e=COPY_RUN, j=PACK)
-            move(dst, as_planar(raw[("rows", b, half)][:], COPY_RUN))
-
-        def sums(b, parts, bank_name):
+        def sums(b, k, cols, bank_name):
             bank = psum.tile([P, N], F32, name=bank_name)
-            first = 0
-            for k, cols in parts:
-                stop = first + cols.stop - cols.start
-                product(bank[:, first:stop], "qm", k, "ds", b, cols, True, False)
-                product(bank[:, first:stop], "dom", k, "pw", b, cols, False, True)
-                first = stop
-            return bank
+            view = bank[:, : cols.stop - cols.start]
+            product(view, "qm", k, "ds", b, cols, True, False)
+            product(view, "dom", k, "pw", b, cols, False, True)
+            return view
 
-        def copy_out(bank, cols, move, dense):
-            move(dense, bank[:, cols])
-            return dense
+        first_grouped = new_grouped(first_parts, "first_grouped")
+        group_latents(0, HALVES[0])
+        gather(1, N, HALF)
+        group_latents(0, HALVES[1])
+        quantize("latent", 0, HALVES[0])
+        group_queries_shared("q")
+        quantize_across(first_codes, first_scales, first_grouped, HALF, E4M3)
+        quantize("q", 0, HALVES[1])
+        new_grouped([("latent", 1, WHOLE)], "q0")
+        group_latents(1, HALVES[0])
+        enter(grouped, [("do", 0, HALVES[0])], picked_row[:, 2 * B * N - HALF :].bitcast(BF16), PACK)
+        new_grouped([("do", 0, HALVES[1])], "do0_grouped")
+        group_queries_shared("do")
+        scores(0, "do0")
+        for cols in HALVES:
+            quantize("do", 0, cols)
+        gather(1, N + HALF, HALF)
+        slopes(0, "do0_grouped", scaled_on_gpsimd)
+        group_latents(1, HALVES[1])
+        quantize("latent", 1, WHOLE)
+        new_grouped([("q", 1, WHOLE)], "q1_grouped")
+        for h in range(2):
+            group_queries("q", 1, h, on_scalar, slice(0, P))
+        new_grouped([("ds", 0, WHOLE)], "ds0_grouped")
+        group_ds(0, HALVES[0])
+        quantize("q", 1, WHOLE)
+        group_ds(0, HALVES[1])
+        new_grouped([("pw", 0, WHOLE)], "pw0_grouped")
+        group_pw(0, WHOLE, scaled_on_scalar)
 
-        def dense_buffer(width, buffer_name):
-            return reused([P, width], F32, buffer_name)[:]
+        new_grouped([("do", 1, HALVES[0])], "first_grouped")
+        new_grouped([("do", 1, HALVES[1])], "do1_grouped")
+        for h in range(2):
+            group_queries("do", 1, h, on_vector, slice(0, P))
+        scores(1, "prob1")
+        quantize("ds", 0, WHOLE)
+        for cols in HALVES:
+            quantize("do", 1, cols)
+        enter(scales, [("pw", 0, WHOLE)], reused([P, WIDTH], U8, "first_grouped"), 1)
+        quantize("pw", 0, WHOLE)
+        slopes(1, "do1_grouped", scaled_on_scalar)
+
+        new_grouped([("qm", 0, HALVES[0])], "qm0_grouped")
+        last_tile = new_grouped([("dom", 0, HALVES[0])] + last_parts[:-1] + [("pw", 1, HALVES[0])], "ds0_grouped")
+        last_grouped = last_tile[:, PACK * HALF :]
+        new_grouped([("pw", 1, HALVES[1])], "pw0_grouped")
+        for name in ("qm", "dom"):
+            group_early_half(name, 0)
+        for name in ("qm", "dom"):
+            quantize(name, 0, HALVES[0])
+        first_sums = [sums(0, k, WHOLE, "score_bank%d" % k) for k in range(2)]
+        for name in ("dom", "qm"):
+            group_early_half(name, 1)
+        group_pw(1, slice(0, PW_COLUMNS_ON_SCALAR), scaled_on_scalar)
+        for cols in HALVES:
+            group_ds(1, cols)
+        quantize("ds", 1, HALVES[0])
+        group_pw(1, slice(PW_COLUMNS_ON_SCALAR, HALF), scaled_on_vector)
+        group_pw(1, HALVES[1], scaled_on_vector)
+        quantize_across(last_codes, last_scales, last_grouped, HALF, E5M2)
+        quantize_across(last_codes, last_scales, last_grouped, HALF + WIDTH, E4M3)
+        quantize("pw", 1, HALVES[1])
 
         def scatter(k, first_slot, move, dense):
             move(windows[k][:].indirect(list_columns(first_slot, dense.shape[1])), dense)
@@ -278,152 +357,62 @@ def tile_attend_gat_sig_c_kernel(tc, qT, cT, doT, rw, qm, dom, offs, out):
         def store(k):
             nc.sync.dma_start(out[P * k : P * (k + 1), :], windows[k][:])
 
-        def cast_queries(name, b, on_vector_groups):
-            src = raw[(name, b)][:].rearrange("p j (m h e) -> p h m j e", h=2, e=2)
-            dst = [grouped_columns(name, b, cols).rearrange("p (e m j) -> p m j e", e=2, j=PACK) for cols in HALVES]
-            first, second = min(on_vector_groups, P), max(on_vector_groups - P, 0)
-            for h, split in enumerate((first, second)):
-                if split > 0:
-                    on_vector(dst[h][:, :split], src[:, h, :split])
-            for h, split in enumerate((first, second)):
-                if split < P:
-                    on_scalar(dst[h][:, split:], src[:, h, split:])
+        for_scalar = {k: reused([P, B * N], F32, "for_scalar%d" % k) for k in (0, 2)}
 
-        first_grouped = reused([P, 2 * WIDTH * PACK], BF16, "grouped_a")
-        for index, name in enumerate(("latent", "q")):
-            pieces[(name, 0)] = [(WHOLE, first_grouped[:, index * WIDTH * PACK : (index + 1) * WIDTH * PACK])]
-        group_latents(0, HALVES[0], nc.scalar.copy)
-        gather(1, N, N // 2)
-        group_latents(0, HALVES[1], nc.scalar.copy)
-        quantize("latent", 0, HALVES[0])
-        cast_queries("q", 0, Q0_GROUPS_ON_VECTOR)
-        middle = slice(WIDTH // 2, WIDTH + WIDTH // 2)
-        nc.vector.quantize_mx(
-            out=first_codes[:, middle].bitcast(E4M3),
-            scales=first_scales[:, middle],
-            in_=first_grouped[:, PACK * middle.start : PACK * middle.stop],
-        )
-        quantize("q", 0, HALVES[1])
-        new_grouped("latent", 1, WHOLE, "q0")
-        group_latents(1, HALVES[0], nc.scalar.copy)
-        pieces[("do", 0)] = [(HALVES[0], picked_row[:, 2 * B * N - N // 2 :].bitcast(BF16))]
-        new_grouped("do", 0, HALVES[1], "grouped_c")
-        cast_queries("do", 0, DO0_GROUPS_ON_VECTOR)
-        scores(0, "do0")
-        for cols in HALVES:
-            quantize("do", 0, cols)
-        gather(1, N + N // 2, N // 2)
-        slopes(0, "grouped_c", scaled_on_gpsimd)
-        group_latents(1, HALVES[1], nc.scalar.copy)
-        quantize("latent", 1, WHOLE)
-        new_grouped("q", 1, WHOLE, "grouped_b")
-        cast_queries("q", 1, 0)
-        new_grouped("ds", 0, WHOLE, "grouped_ds")
-        group_ds(0, HALVES[0])
-        quantize("q", 1, WHOLE)
-        group_ds(0, HALVES[1])
-        new_grouped("pw", 0, WHOLE, "grouped_pw")
-        group_pw(0, slice(0, N - PW0_ON_VECTOR), scaled_on_scalar)
+        def copy_halves_on_scalar(b, k, views):
+            for cols, view in zip(HALVES, views):
+                on_scalar(for_scalar[k][:, N * b + cols.start : N * b + cols.stop], view)
 
-        new_grouped("do", 1, HALVES[0], "grouped_a")
-        new_grouped("do", 1, HALVES[1], "grouped_d")
-        cast_queries("do", 1, 2 * P)
-        scores(1, "prob")
-        group_pw(0, slice(N - PW0_ON_VECTOR, N), scaled_on_vector)
-        quantize("ds", 0, WHOLE)
-        for cols in HALVES:
-            quantize("do", 1, cols)
-        scales[("pw", 0)] = reused([P, WIDTH], U8, "grouped_a")
-        quantize("pw", 0, WHOLE)
-        slopes(1, "grouped_d", scaled_on_scalar)
-        new_grouped("qm", 0, HALVES[0], "grouped_qm")
-        joint = reused([P, 3 * WIDTH * PACK], BF16, "grouped_ds")
-        closing = reused([P, WIDTH // 2 * PACK], BF16, "grouped_pw")
-        half = WIDTH // 2 * PACK
-        pieces[("dom", 0)] = [(HALVES[0], joint[:, :half])]
-        pieces[("ds", 1)] = [(WHOLE, joint[:, half : 3 * half])]
-        pieces[("dom", 1)] = [(HALVES[0], joint[:, 3 * half : 4 * half])]
-        pieces[("qm", 1)] = [(HALVES[0], joint[:, 4 * half : 5 * half])]
-        pieces[("pw", 1)] = [(HALVES[0], joint[:, 5 * half :]), (HALVES[1], closing[:])]
+        def scatter_on_scalar(b, k):
+            for cols in HALVES:
+                scatter(k, N * b + cols.start, on_scalar, for_scalar[k][:, N * b + cols.start : N * b + cols.stop])
 
-        def quantize_joint(first, fmt, grouped):
-            nc.vector.quantize_mx(
-                out=joint_codes[:, first : first + WIDTH].bitcast(fmt),
-                scales=joint_scales[:, first : first + WIDTH],
-                in_=grouped,
-            )
+        def halves_of(view):
+            return [view[:, cols] for cols in HALVES]
 
-        for name in ("qm", "dom"):
-            group_rows(name, 0, HALVES[0], on_scalar)
-        for name in ("qm", "dom"):
-            quantize(name, 0, HALVES[0])
-        first_sums = [None] * PACK
-        second_sums = [None] * PACK
-        for k in (0, 1):
-            first_sums[k] = sums(0, [(k, WHOLE)], "score_bank%d" % k)
-        for name in ("dom", "qm"):
-            group_rows(name, 1, HALVES[0], on_scalar)
-        group_pw(1, slice(0, PW_ON_SCALAR), scaled_on_scalar)
-        for cols in HALVES:
-            group_ds(1, cols)
-        quantize("ds", 1, HALVES[0])
-        group_pw(1, slice(PW_ON_SCALAR, N // 2), scaled_on_vector)
-        group_pw(1, HALVES[1], scaled_on_vector)
-        quantize_joint(WIDTH, E5M2, joint[:, 2 * half : 4 * half])
-        quantize_joint(2 * WIDTH, E4M3, joint[:, 4 * half :])
-        quantize("pw", 1, HALVES[1])
-        both = [dense_buffer(B * N, "both%d" % index) for index in range(2)]
-        copy_out(first_sums[0], WHOLE, on_scalar, both[0][:, :N])
-        dense = copy_out(first_sums[1], WHOLE, on_scalar, dense_buffer(N, "dense_a"))
-        for k in (0, 1):
-            second_sums[k] = sums(1, [(k, WHOLE)], "score_bank%d" % (k + 2))
-
-        def scatter_on_scalar(k, part):
-            first, stop = SCALAR_PARTS[part]
-            scatter(k, first, on_scalar, both[k // 2][:, first:stop])
+        def group_late_halves(b, view):
+            enter(grouped, [(name, b, HALVES[1]) for name in ("qm", "dom")], view, PACK)
+            scaled_on_gpsimd(runs_of_grouped(view, COPY_RUN), runs_of_planar(rows[(b, 1)], COPY_RUN), 1.0)
 
         def quantize_late_halves(b):
             for name in ("dom", "qm"):
                 quantize(name, b, HALVES[1])
 
-        bulk = N - LAST_COLUMNS
-        late = reused([P, 3 * N], F32, "grouped_ds")
-        scatter(1, 0, on_vector, dense)
-        group_halves(0, 1, on_gpsimd, late[:, : 2 * N].bitcast(BF16))
-        for part in (0, 1):
-            scatter_on_scalar(0, part)
+        most, rest = slice(0, N - LAST_COLUMNS), slice(N - LAST_COLUMNS, N)
 
-        held = rows_tile[(0, 1)][:, :N]
-        for cols in HALVES:
-            copy_out(second_sums[0], cols, on_scalar, both[0][:, N + cols.start : N + cols.stop])
-        copy_out(second_sums[1], slice(0, bulk), on_vector, held[:, :bulk])
-        copy_out(second_sums[1], slice(bulk, N), on_vector, held[:, bulk:])
+        on_scalar(for_scalar[0][:, :N], first_sums[0])
+        for_vector = reused([P, N], F32, "for_vector")
+        on_scalar(for_vector[:], first_sums[1])
+        second_sums = [sums(1, k, WHOLE, "score_bank%d" % (k + 2)) for k in range(2)]
+
+        late_grouped = reused([P, 3 * HALF * PACK], BF16, "ds0_grouped")
+        scatter(1, 0, on_vector, for_vector[:])
+        group_late_halves(0, late_grouped[:, : 2 * HALF * PACK])
+        scatter_on_scalar(0, 0)
+
+        copy_halves_on_scalar(1, 0, halves_of(second_sums[0]))
+        for cols in (most, rest):
+            on_vector(in_front[(0, 1)][:, cols], second_sums[1][:, cols])
         quantize_late_halves(0)
-        for index, k in enumerate((2, 3)):
-            first_sums[k] = sums(0, [(k, WHOLE)], "slope_bank%d" % index)
-        scatter(1, N, on_vector, held)
-        group_halves(1, 1, on_gpsimd, late[:, N:].bitcast(BF16))
-        for part in (2, 3):
-            scatter_on_scalar(0, part)
+        first_sums = first_sums + [sums(0, k, WHOLE, "slope_bank%d" % (k - 2)) for k in (2, 3)]
+        scatter(1, N, on_vector, in_front[(0, 1)])
+        group_late_halves(1, late_grouped[:, HALF * PACK :])
+        scatter_on_scalar(1, 0)
         store(0)
         store(1)
 
-        held = rows_tile[(1, 1)][:, :N]
-        for cols in HALVES:
-            copy_out(first_sums[2], cols, on_scalar, both[1][:, cols])
-        copy_out(first_sums[3], slice(0, bulk), on_vector, held[:, :bulk])
-        for first, stop in LATE_PARTS[:-2]:
-            scatter(2, first, on_scalar, both[1][:, first:stop])
-        copy_out(first_sums[3], slice(bulk, N), on_vector, held[:, bulk:])
+        copy_halves_on_scalar(0, 2, halves_of(first_sums[2]))
+        on_vector(in_front[(1, 1)][:, most], first_sums[3][:, most])
+        scatter_on_scalar(0, 2)
+        on_vector(in_front[(1, 1)][:, rest], first_sums[3][:, rest])
         quantize_late_halves(1)
-        halves = [sums(1, [(2, cols)], bank_name) for cols, bank_name in zip(HALVES, ("slope_bank2", "score_bank0"))]
-        second_sums[3] = sums(1, [(3, WHOLE)], "slope_bank3")
-        scatter(3, 0, on_vector, held)
-        for cols, bank in zip(HALVES, halves):
-            copy_out(bank, HALVES[0], on_scalar, both[1][:, N + cols.start : N + cols.stop])
-        dense = copy_out(second_sums[3], WHOLE, on_vector, dense_buffer(N, "dense_a"))
-        for first, stop in LATE_PARTS[-2:]:
-            scatter(2, first, on_scalar, both[1][:, first:stop])
+        last_halves = [sums(1, 2, cols, name) for cols, name in zip(HALVES, ("slope_bank2", "score_bank0"))]
+        last_sums = sums(1, 3, WHOLE, "slope_bank3")
+        scatter(3, 0, on_vector, in_front[(1, 1)])
+        copy_halves_on_scalar(1, 2, last_halves)
+        for_vector = reused([P, N], F32, "for_vector")
+        on_vector(for_vector[:], last_sums)
+        scatter_on_scalar(1, 2)
         store(2)
-        scatter(3, N, on_vector, dense)
+        scatter(3, N, on_vector, for_vector[:])
         store(3)

@@ -35,10 +35,9 @@ POOL_LOADS = (
     (1, T - T // 8, T, 160),
 )
 SHARED_GROUPS_ON_VECTOR = 40
-PW_COLUMNS_ON_SCALAR = 128
+PW_COLUMNS_ON_SCALAR = (416, 96)
 LAST_COLUMNS = 16
-COPY_RUN = 4
-PRODUCT_RUN = 2
+RUN = 4
 
 
 def tile_attend_gat_sig_c_kernel(tc, qT, cT, doT, rw, qm, dom, offs, out):
@@ -108,8 +107,8 @@ def tile_attend_gat_sig_c_kernel(tc, qT, cT, doT, rw, qm, dom, offs, out):
             u, first, stop, split = POOL_LOADS[index]
             for move, lo, hi in ((on_vector, 0, split), (on_scalar, split, stop - first)):
                 if lo < hi:
-                    src = chunks[index][:, :, lo:hi].rearrange("p e (c f) -> p c e f", f=COPY_RUN)
-                    dst = pairs[u][:, first + lo : first + hi, :].rearrange("p (c f) e -> p c e f", f=COPY_RUN)
+                    src = chunks[index][:, :, lo:hi].rearrange("p e (c f) -> p c e f", f=RUN)
+                    dst = pairs[u][:, first + lo : first + hi, :].rearrange("p (c f) e -> p c e f", f=RUN)
                     move(dst, src)
 
         def list_columns(first_slot, count):
@@ -200,11 +199,11 @@ def tile_attend_gat_sig_c_kernel(tc, qT, cT, doT, rw, qm, dom, offs, out):
                 in_=grouped_tile[:, PACK * first : PACK * (first + WIDTH)],
             )
 
-        def runs_of_grouped(view, run):
-            return view.rearrange("p (c e j) -> p c j e", e=run, j=PACK)
+        def runs_of_grouped(view):
+            return view.rearrange("p (c e j) -> p c j e", e=RUN, j=PACK)
 
-        def runs_of_planar(view, run):
-            return view.rearrange("p j (c e) -> p c j e", e=run)
+        def runs_of_planar(view):
+            return view.rearrange("p j (c e) -> p c j e", e=RUN)
 
         def group_latents(b, cols):
             src = picked[:, :, N * b + cols.start : N * b + cols.stop]
@@ -224,7 +223,7 @@ def tile_attend_gat_sig_c_kernel(tc, qT, cT, doT, rw, qm, dom, offs, out):
         def group_early_half(name, b):
             src = rows[(b, 0)][:, :, HALVES[("qm", "dom").index(name)]]
             dst = look_up(grouped, name, b, HALVES[0], PACK)
-            on_scalar(runs_of_grouped(dst, COPY_RUN), runs_of_planar(src, COPY_RUN))
+            on_scalar(runs_of_grouped(dst), runs_of_planar(src))
 
         def product(sums_view, stationary, block, moving, b, cols, start, stop):
             lhs_codes, lhs_scales = quantized(stationary, b, BLOCKS[block])
@@ -271,15 +270,15 @@ def tile_attend_gat_sig_c_kernel(tc, qT, cT, doT, rw, qm, dom, offs, out):
 
         def group_ds(b, cols):
             nc.vector.tensor_tensor(
-                runs_of_grouped(look_up(grouped, "ds", b, cols, PACK), PRODUCT_RUN),
-                runs_of_planar(slope[b][:, :, cols], PRODUCT_RUN),
-                runs_of_planar(neg_pw[b][:, :, cols], PRODUCT_RUN),
+                runs_of_grouped(look_up(grouped, "ds", b, cols, PACK)),
+                runs_of_planar(slope[b][:, :, cols]),
+                runs_of_planar(neg_pw[b][:, :, cols]),
                 ALU.mult,
             )
 
         def group_pw(b, cols, scaled):
-            dst = runs_of_grouped(look_up(grouped, "pw", b, cols, PACK), COPY_RUN)
-            scaled(dst, runs_of_planar(neg_pw[b][:, :, cols], COPY_RUN), -1.0)
+            dst = runs_of_grouped(look_up(grouped, "pw", b, cols, PACK))
+            scaled(dst, runs_of_planar(neg_pw[b][:, :, cols]), -1.0)
 
         def sums(b, k, cols, bank_name):
             bank = psum.tile([P, N], F32, name=bank_name)
@@ -316,13 +315,14 @@ def tile_attend_gat_sig_c_kernel(tc, qT, cT, doT, rw, qm, dom, offs, out):
         quantize("q", 1, WHOLE)
         group_ds(0, HALVES[1])
         new_grouped([("pw", 0, WHOLE)], "pw0_grouped")
-        group_pw(0, WHOLE, scaled_on_scalar)
+        group_pw(0, slice(0, PW_COLUMNS_ON_SCALAR[0]), scaled_on_scalar)
 
         new_grouped([("do", 1, HALVES[0])], "first_grouped")
         new_grouped([("do", 1, HALVES[1])], "do1_grouped")
         for h in range(2):
             group_queries("do", 1, h, on_vector, slice(0, P))
         scores(1, "prob1")
+        group_pw(0, slice(PW_COLUMNS_ON_SCALAR[0], N), scaled_on_vector)
         quantize("ds", 0, WHOLE)
         for cols in HALVES:
             quantize("do", 1, cols)
@@ -341,11 +341,11 @@ def tile_attend_gat_sig_c_kernel(tc, qT, cT, doT, rw, qm, dom, offs, out):
         first_sums = [sums(0, k, WHOLE, "score_bank%d" % k) for k in range(2)]
         for name in ("dom", "qm"):
             group_early_half(name, 1)
-        group_pw(1, slice(0, PW_COLUMNS_ON_SCALAR), scaled_on_scalar)
+        group_pw(1, slice(0, PW_COLUMNS_ON_SCALAR[1]), scaled_on_scalar)
         for cols in HALVES:
             group_ds(1, cols)
         quantize("ds", 1, HALVES[0])
-        group_pw(1, slice(PW_COLUMNS_ON_SCALAR, HALF), scaled_on_vector)
+        group_pw(1, slice(PW_COLUMNS_ON_SCALAR[1], HALF), scaled_on_vector)
         group_pw(1, HALVES[1], scaled_on_vector)
         quantize_across(last_codes, last_scales, last_grouped, HALF, E5M2)
         quantize_across(last_codes, last_scales, last_grouped, HALF + WIDTH, E4M3)
@@ -372,7 +372,7 @@ def tile_attend_gat_sig_c_kernel(tc, qT, cT, doT, rw, qm, dom, offs, out):
 
         def group_late_halves(b, view):
             enter(grouped, [(name, b, HALVES[1]) for name in ("qm", "dom")], view, PACK)
-            scaled_on_gpsimd(runs_of_grouped(view, COPY_RUN), runs_of_planar(rows[(b, 1)], COPY_RUN), 1.0)
+            scaled_on_gpsimd(runs_of_grouped(view), runs_of_planar(rows[(b, 1)]), 1.0)
 
         def quantize_late_halves(b):
             for name in ("dom", "qm"):

@@ -27,15 +27,7 @@ HALVES = (slice(0, HALF), slice(HALF, WIDTH))
 BLOCKS = tuple(slice(P * k, P * (k + 1)) for k in range(WIDTH // P))
 FORMAT = {"q": E4M3, "latent": E4M3, "do": E5M2, "qm": E4M3, "ds": E5M2, "dom": E5M2, "pw": E4M3}
 
-POOL_LOADS = (
-    (0, 0, T // 2, 0),
-    (0, T // 2, T, 640),
-    (1, 0, T // 2, 0),
-    (1, T // 2, T - T // 8, 640),
-    (1, T - T // 8, T, 160),
-)
 SHARED_GROUPS_ON_VECTOR = 40
-PW_COLUMNS_ON_SCALAR = (416, 96)
 LAST_COLUMNS = 16
 RUN = 4
 
@@ -56,134 +48,98 @@ def tile_attend_gat_sig_c_kernel(tc, qT, cT, doT, rw, qm, dom, offs, out):
 
         on_vector = nc.vector.tensor_copy
 
-        offsets = keep.tile([P, B * N // SLOTS_PER_COLUMN], U16, name="offsets")
+        def on_gpsimd(dst, src):
+            nc.gpsimd.tensor_scalar(dst, src, 1.0, 0.0, ALU.mult, ALU.add)
 
-        pool_rows = cT.rearrange("(p u e) c -> u p e c", u=2, e=2)
-        chunks = []
-        for index, (u, first, stop, on_vector_tokens) in enumerate(POOL_LOADS):
-            chunks.append(reused([P, 2, stop - first], F32, "chunk%d" % index))
-            nc.sync.dma_start(chunks[index][:], pool_rows[u][:, :, first:stop])
-            if (u, stop) == (0, T):
-                nc.sync.dma_start(offsets[:], offs)
+        source = {"q": qT, "do": doT, "qm": qm, "dom": dom}
+        planar = {}
 
-        queries = {}
+        def load(name, b, cols, view):
+            planar.setdefault((name, b), []).append((cols, view))
+            nc.sync.dma_start(view, source[name][b][:, cols].rearrange("(p j) c -> p j c", j=PACK))
 
-        def load_queries(name, b, src, buffer_name):
-            queries[(name, b)] = reused([P, PACK, R], F32, buffer_name)
-            nc.sync.dma_start(queries[(name, b)][:], src[b].rearrange("(p j) c -> p j c", j=PACK))
+        def load_alone(name, b, cols, buffer_name):
+            load(name, b, cols, reused([P, PACK, cols.stop - cols.start], F32, buffer_name)[:])
 
-        load_queries("q", 0, qT, "q0")
-        load_queries("do", 0, doT, "do0")
-        gate = keep.tile([P, B, PACK], F32, name="gate")
-        nc.sync.dma_start(gate[:], rw.rearrange("b (p t) o -> p b (t o)", t=PACK))
-        load_queries("q", 1, qT, "q1")
-        load_queries("do", 1, doT, "chunk0")
-
-        rows = {}
+        late = {}
         in_front = {}
 
-        def load_rows(b, half, buffer_name):
-            spare = (N - LAST_COLUMNS) * half
-            tile = reused([P, spare + PACK * WIDTH], F32, buffer_name)
-            rows[(b, half)] = tile[:, spare:].rearrange("p (j c) -> p j c", j=PACK)
-            in_front[(b, half)] = tile[:, :N]
-            for index, src in enumerate((qm, dom)):
-                nc.sync.dma_start(
-                    rows[(b, half)][:, :, HALVES[index]],
-                    src[b][:, HALVES[half]].rearrange("(p j) c -> p j c", j=PACK),
-                )
+        def load_late(b, k, buffer_name):
+            spare = HALF - LAST_COLUMNS
+            tile = reused([P, spare + PACK * 2 * P], F32, buffer_name)
+            late[(b, k)] = tile[:, spare:].rearrange("p (j c) -> p j c", j=PACK)
+            in_front[(b, k)] = tile[:, :HALF]
+            for index, name in enumerate(("qm", "dom")):
+                load(name, b, BLOCKS[k], late[(b, k)][:, :, BLOCKS[index]])
 
-        for b, half, buffer_name in ((0, 0, "chunk1"), (1, 0, "chunk2"), (0, 1, "chunk3"), (1, 1, "q1")):
-            load_rows(b, half, buffer_name)
+        load_alone("q", 0, WHOLE, "q0")
+        offsets = keep.tile([P, B * N // SLOTS_PER_COLUMN], U16, name="offsets")
+        nc.sync.dma_start(offsets[:], offs)
+        planes = [reused([P, T], F32, "plane%d" % j) for j in range(PACK)]
+        for j in range(PACK):
+            nc.sync.dma_start(planes[j][:], cT.rearrange("(p j) c -> j p c", j=PACK)[j])
+        load_alone("do", 0, WHOLE, "do0")
+        gate = keep.tile([P, B, PACK], F32, name="gate")
+        nc.sync.dma_start(gate[:], rw.rearrange("b (p t) o -> p b (t o)", t=PACK))
+        load_alone("qm", 0, slice(0, 3 * P), "qm0")
+        load_alone("dom", 0, slice(0, 3 * P), "dom0")
+        load_alone("q", 1, WHOLE, "q1")
+        load_alone("do", 1, WHOLE, "do1")
+        load_alone("qm", 1, HALVES[0], "q0")
+        load_alone("dom", 1, HALVES[0], "plane0")
+        LATE = ((0, 3), (1, 2), (1, 3))
+        for index, (b, k) in enumerate(LATE):
+            load_late(b, k, "plane%d" % (index + 1))
 
-        warm_up = keep.tile([P, 1], F32, name="warm_up")
-        nc.scalar.activation(warm_up[:], chunks[0][:, 0, 0:1], ACT.Sigmoid)
-
-        pairs = [keep.tile([P, T, 2], BF16, name="pairs%d" % u) for u in range(2)]
-        picked_row = keep.tile([P, 2 * B * N + HALF], U32, name="picked", align_bytes=64)
-        picked = picked_row[:, : 2 * B * N].rearrange("p (u c) -> p u c", u=2)
-
-        def pair_up(index):
-            u, first, stop, split = POOL_LOADS[index]
-            for move, lo, hi in ((on_vector, 0, split), (on_scalar, split, stop - first)):
-                if lo < hi:
-                    src = chunks[index][:, :, lo:hi].rearrange("p e (c f) -> p c e f", f=RUN)
-                    dst = pairs[u][:, first + lo : first + hi, :].rearrange("p (c f) e -> p c e f", f=RUN)
-                    move(dst, src)
-
-        def list_columns(first_slot, count):
-            return offsets[:, first_slot // SLOTS_PER_COLUMN : (first_slot + count) // SLOTS_PER_COLUMN]
-
-        def gather(u, first_slot, count):
-            words = pairs[u][:].rearrange("p c e -> p (c e)").bitcast(U32)
-            nc.vector.tensor_copy(
-                picked[:, u, first_slot : first_slot + count], words.indirect(list_columns(first_slot, count))
-            )
-
-        def pair_up_all(u):
-            for index in range(len(POOL_LOADS)):
-                if POOL_LOADS[index][0] == u:
-                    pair_up(index)
-
-        pair_up_all(0)
-        gather(0, 0, B * N)
-        pair_up_all(1)
-        for cols in HALVES:
-            gather(1, cols.start, HALF)
+        warm_up = keep.tile([P, 2], F32, name="warm_up")
+        nc.vector.memset(warm_up[:, 0:1], 0.0)
+        nc.scalar.activation(warm_up[:, 1:2], warm_up[:, 0:1], ACT.Sigmoid)
 
         windows = [keep.tile([P, T], F32, name="window%d" % k) for k in range(D // P)]
         for window in windows:
             nc.vector.memset(window[:].bitcast(I32), 0)
-        neg_gate = keep.tile([P, B, PACK], F32, name="neg_gate")
-        nc.scalar.activation(neg_gate[:], gate[:], ACT.Copy, scale=-1.0)
 
         grouped = {}
         codes = {}
         scales = {}
 
-        def enter(table, parts, tile, per_column):
+        def enter(table, parts, view, per_column):
             first = 0
             for name, b, cols in parts:
                 stop = first + per_column * (cols.stop - cols.start)
-                table.setdefault((name, b), []).append((cols, tile[:, first:stop]))
+                table.setdefault((name, b), []).append((cols, view[:, first:stop]))
                 first = stop
 
+        def holder(table, name, b, cols):
+            return [x for x in table[(name, b)] if x[0].start <= cols.start and cols.stop <= x[0].stop][0]
+
         def look_up(table, name, b, cols, per_column):
-            held, view = [x for x in table[(name, b)] if x[0].start <= cols.start and cols.stop <= x[0].stop][0]
+            held, view = holder(table, name, b, cols)
             return view[:, per_column * (cols.start - held.start) : per_column * (cols.stop - held.start)]
+
+        def planar_view(name, b, cols):
+            held, view = holder(planar, name, b, cols)
+            return view[:, :, cols.start - held.start : cols.stop - held.start]
 
         def width_of(parts):
             return sum(cols.stop - cols.start for name, b, cols in parts)
 
-        def new_codes(parts, tile_name):
-            tile = keep.tile([P, width_of(parts)], U32, name=tile_name + "_codes", align_bytes=64)
-            enter(codes, parts, tile, 1)
-            return tile
+        together = {}
 
-        def new_scales(parts, tile_name):
-            tile = keep.tile([P, width_of(parts)], U8, name=tile_name + "_scales", align_bytes=64)
-            enter(scales, parts, tile, 1)
-            return tile
+        def new_codes(parts, codes_buffer, scales_buffer):
+            tiles = (reused([P, width_of(parts)], U32, codes_buffer), reused([P, width_of(parts)], U8, scales_buffer))
+            enter(codes, parts, tiles[0], 1)
+            enter(scales, parts, tiles[1], 1)
+            together[parts[0][0], parts[0][1], parts[0][2].start] = tiles
+
+        def own_codes(parts):
+            tag = "%s%d_%d" % (parts[0][0], parts[0][1], parts[0][2].start)
+            new_codes(parts, tag + "_codes", tag + "_scales")
 
         def new_grouped(parts, buffer_name):
             tile = reused([P, width_of(parts) * PACK], BF16, buffer_name)
             enter(grouped, parts, tile, PACK)
             return tile
-
-        first_parts = [("latent", 0, WHOLE), ("q", 0, WHOLE)]
-        last_parts = [("ds", 1, WHOLE), ("dom", 1, HALVES[0]), ("qm", 1, HALVES[0]), ("pw", 1, WHOLE)]
-        first_codes, first_scales = new_codes(first_parts, "first"), new_scales(first_parts, "first")
-        last_codes, last_scales = new_codes(last_parts, "last"), new_scales(last_parts, "last")
-        for name, b, cols in [(name, 0, WHOLE) for name in ("do", "qm", "ds", "dom")] + [
-            ("latent", 1, WHOLE),
-            ("q", 1, WHOLE),
-            ("do", 1, WHOLE),
-            ("qm", 1, HALVES[1]),
-            ("dom", 1, HALVES[1]),
-        ]:
-            new_codes([(name, b, cols)], "%s%d" % (name, b))
-            new_scales([(name, b, cols)], "%s%d" % (name, b))
-        new_codes([("pw", 0, WHOLE)], "pw0")
 
         def quantized(name, b, cols):
             return look_up(codes, name, b, cols, 1).bitcast(FORMAT[name]), look_up(scales, name, b, cols, 1)
@@ -192,12 +148,20 @@ def tile_attend_gat_sig_c_kernel(tc, qT, cT, doT, rw, qm, dom, offs, out):
             out_codes, out_scales = quantized(name, b, cols)
             nc.vector.quantize_mx(out=out_codes, scales=out_scales, in_=look_up(grouped, name, b, cols, PACK))
 
-        def quantize_across(codes_tile, scales_tile, grouped_tile, first, fmt):
+        def quantize_together(parts, grouped_view):
+            name, b, cols = parts[0]
+            codes_tile, scales_tile = together[name, b, cols.start]
+            width = width_of(parts)
             nc.vector.quantize_mx(
-                out=codes_tile[:, first : first + WIDTH].bitcast(fmt),
-                scales=scales_tile[:, first : first + WIDTH],
-                in_=grouped_tile[:, PACK * first : PACK * (first + WIDTH)],
+                out=codes_tile[:, :width].bitcast(FORMAT[name]), scales=scales_tile[:, :width], in_=grouped_view
             )
+
+        def list_columns(first_slot, count):
+            return offsets[:, first_slot // SLOTS_PER_COLUMN : (first_slot + count) // SLOTS_PER_COLUMN]
+
+        def gather(j, b, cols, move):
+            dst = look_up(grouped, "latent", b, cols, PACK).rearrange("p (c j) -> p j c", j=PACK)[:, j, :]
+            move(dst, planes[j][:].indirect(list_columns(N * b + cols.start, cols.stop - cols.start)))
 
         def runs_of_grouped(view):
             return view.rearrange("p (c e j) -> p c j e", e=RUN, j=PACK)
@@ -205,25 +169,13 @@ def tile_attend_gat_sig_c_kernel(tc, qT, cT, doT, rw, qm, dom, offs, out):
         def runs_of_planar(view):
             return view.rearrange("p j (c e) -> p c j e", e=RUN)
 
-        def group_latents(b, cols):
-            src = picked[:, :, N * b + cols.start : N * b + cols.stop]
-            dst = look_up(grouped, "latent", b, cols, PACK).bitcast(U32).rearrange("p (c u) -> p c u", u=2)
-            nc.scalar.copy(dst, src.rearrange("p u c -> p c u"))
+        def group_queries(name, b, cols, move, groups):
+            dst = look_up(grouped, name, b, cols, PACK).rearrange("p (t m j) -> p m j t", m=P, j=PACK)
+            src = planar_view(name, b, WHOLE).rearrange("p j (m t) -> p m j t", t=PACK)
+            move(dst[:, groups], src[:, groups, :, cols.start // P : cols.stop // P])
 
-        def group_queries(name, b, h, move, groups):
-            dst = look_up(grouped, name, b, HALVES[h], PACK).rearrange("p (e m j) -> p m j e", e=2, j=PACK)
-            src = queries[(name, b)][:].rearrange("p j (m h e) -> p h m j e", h=2, e=2)
-            move(dst[:, groups], src[:, h, groups])
-
-        def group_queries_shared(name):
-            group_queries(name, 0, 0, on_vector, slice(0, P))
-            group_queries(name, 0, 1, on_vector, slice(0, SHARED_GROUPS_ON_VECTOR))
-            group_queries(name, 0, 1, on_scalar, slice(SHARED_GROUPS_ON_VECTOR, P))
-
-        def group_early_half(name, b):
-            src = rows[(b, 0)][:, :, HALVES[("qm", "dom").index(name)]]
-            dst = look_up(grouped, name, b, HALVES[0], PACK)
-            on_scalar(runs_of_grouped(dst), runs_of_planar(src))
+        def group_rows(name, b, cols, move):
+            move(runs_of_grouped(look_up(grouped, name, b, cols, PACK)), runs_of_planar(planar_view(name, b, cols)))
 
         def product(sums_view, stationary, block, moving, b, cols, start, stop):
             lhs_codes, lhs_scales = quantized(stationary, b, BLOCKS[block])
@@ -238,35 +190,38 @@ def tile_attend_gat_sig_c_kernel(tc, qT, cT, doT, rw, qm, dom, offs, out):
                 stop=stop,
             )
 
-        prob = {}
-        neg_pw = {}
-        slope = {}
+        def bank(number):
+            return psum.tile([P, N], F32, name="bank%d" % number)
 
-        def scores(b, buffer_name):
+        prob = {}
+        slope = {}
+        neg_pw = {}
+
+        def held_in(b, parts, buffer_name):
+            row = reused([P, PACK * N], F32, buffer_name)
+            neg_pw[b] = row[:].rearrange("p (t c) -> p t c", t=PACK)
+            words = width_of(parts) * PACK // 2
+            first = (5 * N - words) // 2
+            view = row[:, first : first + words].bitcast(BF16)
+            enter(grouped, parts, view, PACK)
+            return view
+
+        def first_product(name, b, t, number):
+            tile = bank(number)
+            product(tile[:], name, t, "latent", b, WHOLE, True, True)
+            return tile
+
+        def sigmoids(b, banks, buffer_name):
             prob[b] = reused([P, PACK, N], F32, buffer_name)
             for t in range(PACK):
-                bank = psum.tile([P, N], F32, name="score_bank%d" % t)
-                product(bank[:], "q", t, "latent", b, WHOLE, True, True)
-                nc.scalar.activation(prob[b][:, t, :], bank[:], ACT.Sigmoid)
+                nc.scalar.activation(prob[b][:, t, :], banks[t][:], ACT.Sigmoid)
 
-        def scaled_on_scalar(dst, src, factor):
-            nc.scalar.activation(dst, src, ACT.Copy, scale=factor)
-
-        def scaled_on_vector(dst, src, factor):
-            nc.vector.tensor_scalar(dst, src, factor, None, ALU.mult)
-
-        def scaled_on_gpsimd(dst, src, factor):
-            nc.gpsimd.tensor_scalar(dst, src, factor, 0.0, ALU.mult, ALU.add)
-
-        def slopes(b, neg_pw_buffer, last_gated):
-            gated = [scaled_on_gpsimd] * (PACK - 1) + [last_gated]
-            neg_pw[b] = reused([P, PACK, N], F32, neg_pw_buffer)
+        def slopes(b, banks):
             slope[b] = reused([P, PACK, N], F32, "slope")
             for t in range(PACK):
-                bank = psum.tile([P, N], F32, name="slope_bank%d" % t)
-                product(bank[:], "do", t, "latent", b, WHOLE, True, True)
-                gated[t](neg_pw[b][:, t, :], prob[b][:, t, :], neg_gate[:, b, t : t + 1])
-                nc.vector.scalar_tensor_tensor(slope[b][:, t, :], prob[b][:, t, :], 1.0, bank[:], ALU.subtract, ALU.mult)
+                engine = nc.gpsimd if t else nc.vector
+                engine.tensor_scalar(neg_pw[b][:, t, :], prob[b][:, t, :], gate[:, b, t : t + 1], -1.0, ALU.mult, ALU.mult)
+                nc.vector.scalar_tensor_tensor(slope[b][:, t, :], prob[b][:, t, :], 1.0, banks[t][:], ALU.subtract, ALU.mult)
 
         def group_ds(b, cols):
             nc.vector.tensor_tensor(
@@ -276,143 +231,175 @@ def tile_attend_gat_sig_c_kernel(tc, qT, cT, doT, rw, qm, dom, offs, out):
                 ALU.mult,
             )
 
-        def group_pw(b, cols, scaled):
+        def group_pw(b, cols, on_engine):
             dst = runs_of_grouped(look_up(grouped, "pw", b, cols, PACK))
-            scaled(dst, runs_of_planar(neg_pw[b][:, :, cols]), -1.0)
+            src = runs_of_planar(neg_pw[b][:, :, cols])
+            if on_engine == "scalar":
+                nc.scalar.activation(dst, src, ACT.Copy, scale=-1.0)
+            else:
+                nc.vector.tensor_scalar(dst, src, -1.0, None, ALU.mult)
 
-        def sums(b, k, cols, bank_name):
-            bank = psum.tile([P, N], F32, name=bank_name)
-            view = bank[:, : cols.stop - cols.start]
+        def sums(b, k, cols, number):
+            view = bank(number)[:, : cols.stop - cols.start]
             product(view, "qm", k, "ds", b, cols, True, False)
             product(view, "dom", k, "pw", b, cols, False, True)
             return view
 
-        first_grouped = new_grouped(first_parts, "first_grouped")
-        group_latents(0, HALVES[0])
-        gather(1, N, HALF)
-        group_latents(0, HALVES[1])
-        quantize("latent", 0, HALVES[0])
-        group_queries_shared("q")
-        quantize_across(first_codes, first_scales, first_grouped, HALF, E4M3)
-        quantize("q", 0, HALVES[1])
-        new_grouped([("latent", 1, WHOLE)], "q0")
-        group_latents(1, HALVES[0])
-        enter(grouped, [("do", 0, HALVES[0])], picked_row[:, 2 * B * N - HALF :].bitcast(BF16), PACK)
-        new_grouped([("do", 0, HALVES[1])], "do0_grouped")
-        group_queries_shared("do")
-        scores(0, "do0")
-        for cols in HALVES:
-            quantize("do", 0, cols)
-        gather(1, N + HALF, HALF)
-        slopes(0, "do0_grouped", scaled_on_gpsimd)
-        group_latents(1, HALVES[1])
-        quantize("latent", 1, WHOLE)
-        new_grouped([("q", 1, WHOLE)], "q1_grouped")
-        for h in range(2):
-            group_queries("q", 1, h, on_scalar, slice(0, P))
-        new_grouped([("ds", 0, WHOLE)], "ds0_grouped")
-        group_ds(0, HALVES[0])
-        quantize("q", 1, WHOLE)
-        group_ds(0, HALVES[1])
-        new_grouped([("pw", 0, WHOLE)], "pw0_grouped")
-        group_pw(0, slice(0, PW_COLUMNS_ON_SCALAR[0]), scaled_on_scalar)
+        def copied(view, move, buffer_name):
+            dense = reused([P, view.shape[1]], F32, buffer_name)
+            move(dense[:], view)
+            return dense[:]
 
-        new_grouped([("do", 1, HALVES[0])], "first_grouped")
-        new_grouped([("do", 1, HALVES[1])], "do1_grouped")
-        for h in range(2):
-            group_queries("do", 1, h, on_vector, slice(0, P))
-        scores(1, "prob1")
-        group_pw(0, slice(PW_COLUMNS_ON_SCALAR[0], N), scaled_on_vector)
-        quantize("ds", 0, WHOLE)
-        for cols in HALVES:
-            quantize("do", 1, cols)
-        enter(scales, [("pw", 0, WHOLE)], reused([P, WIDTH], U8, "first_grouped"), 1)
-        quantize("pw", 0, WHOLE)
-        slopes(1, "do1_grouped", scaled_on_scalar)
-
-        new_grouped([("qm", 0, HALVES[0])], "qm0_grouped")
-        last_tile = new_grouped([("dom", 0, HALVES[0])] + last_parts[:-1] + [("pw", 1, HALVES[0])], "ds0_grouped")
-        last_grouped = last_tile[:, PACK * HALF :]
-        new_grouped([("pw", 1, HALVES[1])], "pw0_grouped")
-        for name in ("qm", "dom"):
-            group_early_half(name, 0)
-        for name in ("qm", "dom"):
-            quantize(name, 0, HALVES[0])
-        first_sums = [sums(0, k, WHOLE, "score_bank%d" % k) for k in range(2)]
-        for name in ("dom", "qm"):
-            group_early_half(name, 1)
-        group_pw(1, slice(0, PW_COLUMNS_ON_SCALAR[1]), scaled_on_scalar)
-        for cols in HALVES:
-            group_ds(1, cols)
-        quantize("ds", 1, HALVES[0])
-        group_pw(1, slice(PW_COLUMNS_ON_SCALAR[1], HALF), scaled_on_vector)
-        group_pw(1, HALVES[1], scaled_on_vector)
-        quantize_across(last_codes, last_scales, last_grouped, HALF, E5M2)
-        quantize_across(last_codes, last_scales, last_grouped, HALF + WIDTH, E4M3)
-        quantize("pw", 1, HALVES[1])
-
-        def scatter(k, first_slot, move, dense):
-            move(windows[k][:].indirect(list_columns(first_slot, dense.shape[1])), dense)
+        def scatter(b, k, cols, move, dense):
+            move(windows[k][:].indirect(list_columns(N * b + cols.start, cols.stop - cols.start)), dense)
 
         def store(k):
             nc.sync.dma_start(out[P * k : P * (k + 1), :], windows[k][:])
 
-        for_scalar = {k: reused([P, B * N], F32, "for_scalar%d" % k) for k in (0, 2)}
+        ones = keep.tile([P, 1], F32, name="ones")
+        nc.vector.memset(ones[:], 1.0)
 
-        def copy_halves_on_scalar(b, k, views):
-            for cols, view in zip(HALVES, views):
-                on_scalar(for_scalar[k][:, N * b + cols.start : N * b + cols.stop], view)
+        def whole_on_scalar(dst, src):
+            nc.scalar.activation(dst, src, ACT.Copy, scale=ones[:])
 
-        def scatter_on_scalar(b, k):
-            for cols in HALVES:
-                scatter(k, N * b + cols.start, on_scalar, for_scalar[k][:, N * b + cols.start : N * b + cols.stop])
+        H0, H1 = HALVES
+        ALL_GROUPS = slice(0, P)
 
-        def halves_of(view):
-            return [view[:, cols] for cols in HALVES]
+        new_grouped([("q", 0, WHOLE)], "q0_grouped")
+        new_codes([("q", 0, WHOLE)], "q0_codes", "q0_scales")
+        group_queries("q", 0, WHOLE, on_scalar, ALL_GROUPS)
+        quantize("q", 0, WHOLE)
+        new_grouped([("latent", 0, WHOLE)], "latent0_grouped")
+        held_in(0, [("latent", 1, WHOLE)], "neg_pw0")
+        for j in range(PACK):
+            for b in range(B):
+                gather(j, b, H0, on_vector)
+                gather(j, b, H1, on_scalar)
+        own_codes([("latent", 0, WHOLE)])
+        quantize("latent", 0, WHOLE)
 
-        def group_late_halves(b, view):
-            enter(grouped, [(name, b, HALVES[1]) for name in ("qm", "dom")], view, PACK)
-            scaled_on_gpsimd(runs_of_grouped(view), runs_of_planar(rows[(b, 1)]), 1.0)
+        for h in range(2):
+            new_grouped([("do", 0, HALVES[h])], "do0_grouped%d" % h)
+        own_codes([("do", 0, WHOLE)])
+        group_queries("do", 0, H0, on_vector, ALL_GROUPS)
+        group_queries("do", 0, H1, on_vector, slice(0, SHARED_GROUPS_ON_VECTOR))
+        group_queries("do", 0, H1, on_scalar, slice(SHARED_GROUPS_ON_VECTOR, P))
+        for cols in HALVES:
+            quantize("do", 0, cols)
+        new_codes([("latent", 1, WHOLE)], "latent1_codes", "do0_grouped0")
+        quantize("latent", 1, WHOLE)
+        score_banks = [first_product("q", 0, t, t) for t in range(PACK - 1)]
+        slope_banks = [first_product("do", 0, 0, PACK)]
+        score_banks.append(first_product("q", 0, PACK - 1, PACK - 1))
+        slope_banks = slope_banks + [first_product("do", 0, t, PACK + t) for t in range(1, PACK)]
+        sigmoids(0, score_banks, "do0")
+        slopes(0, slope_banks)
 
-        def quantize_late_halves(b):
-            for name in ("dom", "qm"):
-                quantize(name, b, HALVES[1])
+        new_grouped([("qm", 0, H0)], "q0_codes")
+        own_codes([("qm", 0, H0)])
+        with_ds = [("dom", 0, H0), ("ds", 0, H0)]
+        with_ds_grouped = new_grouped(with_ds, "q0_grouped")
+        own_codes([with_ds[0], ("ds", 0, WHOLE)])
+        new_grouped([("pw", 0, WHOLE)], "latent0_grouped")
+        own_codes([("pw", 0, WHOLE)])
+        new_grouped([("ds", 0, H1)], "ds_second_half")
+        group_rows("qm", 0, H0, on_scalar)
+        group_rows("dom", 0, H0, on_scalar)
+        group_pw(0, H1, "scalar")
+        new_grouped([("q", 1, WHOLE)], "do0")
+        own_codes([("q", 1, WHOLE)])
+        group_queries("q", 1, WHOLE, on_scalar, ALL_GROUPS)
+        quantize("qm", 0, H0)
+        group_ds(0, H0)
+        group_pw(0, H0, "vector")
+        quantize_together(with_ds, with_ds_grouped[:])
+        quantize("pw", 0, H0)
+        views = [sums(0, k, H0, k) for k in range(2)]
+        dense = [copied(views[k], on_scalar, "dense%d" % k) for k in range(2)]
+        for k in range(2):
+            scatter(0, k, H0, on_scalar, dense[k])
 
-        most, rest = slice(0, N - LAST_COLUMNS), slice(N - LAST_COLUMNS, N)
+        group_ds(0, H1)
+        new_grouped([("do", 1, WHOLE)], "q0_grouped")
+        new_codes([("do", 1, WHOLE)], "do1_codes", "do1_scales")
+        group_queries("do", 1, WHOLE, on_vector, ALL_GROUPS)
+        quantize("q", 1, WHOLE)
+        quantize("do", 1, WHOLE)
+        quantize("ds", 0, H1)
+        quantize("pw", 0, H1)
+        score_banks = [first_product("q", 1, t, (t + 2) % PACK) for t in range(PACK)]
+        slope_banks = [first_product("do", 1, t, PACK + t) for t in range(PACK)]
+        sigmoids(1, score_banks, "prob1")
+        views = [sums(0, k, H1, 2 + k) for k in range(2)]
+        dense = [copied(views[k], on_scalar, "dense%d" % k) for k in range(2)]
+        for k in range(2):
+            scatter(0, k, H1, on_scalar, dense[k])
 
-        on_scalar(for_scalar[0][:, :N], first_sums[0])
-        for_vector = reused([P, N], F32, "for_vector")
-        on_scalar(for_vector[:], first_sums[1])
-        second_sums = [sums(1, k, WHOLE, "score_bank%d" % (k + 2)) for k in range(2)]
+        with_qm = [("qm", 0, BLOCKS[2]), ("qm", 1, H0)]
+        with_qm_grouped = held_in(1, with_qm, "do0")
+        own_codes(with_qm)
+        new_grouped([("dom", 0, BLOCKS[2]), ("dom", 1, H0)], "q0_grouped")
+        own_codes([("dom", 0, BLOCKS[2])])
+        group_rows("dom", 0, BLOCKS[2], on_vector)
+        group_rows("qm", 0, BLOCKS[2], on_vector)
+        group_rows("qm", 1, H0, on_vector)
+        group_rows("dom", 1, H0, on_vector)
+        quantize("dom", 0, BLOCKS[2])
+        quantize_together(with_qm, with_qm_grouped)
+        slopes(1, slope_banks)
 
-        late_grouped = reused([P, 3 * HALF * PACK], BF16, "ds0_grouped")
-        scatter(1, 0, on_vector, for_vector[:])
-        group_late_halves(0, late_grouped[:, : 2 * HALF * PACK])
-        scatter_on_scalar(0, 0)
+        new_codes([("dom", 1, H0)], "dom1_codes", "do1_scales")
+        new_grouped([("ds", 1, H0)], "do0_grouped1")
+        new_grouped([("ds", 1, H1)], "ds_second_half")
+        own_codes([("ds", 1, WHOLE)])
+        new_grouped([("pw", 1, WHOLE)], "latent0_grouped")
+        own_codes([("pw", 1, WHOLE)])
+        dense = copied(sums(0, 2, WHOLE, 0), on_scalar, "prob1")
+        group_pw(1, H1, "scalar")
+        scatter(0, 2, WHOLE, whole_on_scalar, dense)
+        quantize("dom", 1, H0)
+        group_ds(1, H0)
+        group_pw(1, H0, "vector")
+        quantize("ds", 1, H0)
+        quantize("pw", 1, H0)
+        view = sums(1, 0, H0, 2)
+        group_ds(1, H1)
+        for_vector = copied(view, on_vector, "for_vector")
+        quantize("ds", 1, H1)
+        quantize("pw", 1, H1)
+        view = sums(1, 0, H1, 3)
+        scatter(1, 1, WHOLE, whole_on_scalar, copied(sums(1, 1, WHOLE, 1), on_scalar, "dense0"))
 
-        copy_halves_on_scalar(1, 0, halves_of(second_sums[0]))
-        for cols in (most, rest):
-            on_vector(in_front[(0, 1)][:, cols], second_sums[1][:, cols])
-        quantize_late_halves(0)
-        first_sums = first_sums + [sums(0, k, WHOLE, "slope_bank%d" % (k - 2)) for k in (2, 3)]
-        scatter(1, N, on_vector, in_front[(0, 1)])
-        group_late_halves(1, late_grouped[:, HALF * PACK :])
-        scatter_on_scalar(1, 0)
+        late_grouped = reused([P, (len(LATE) + 1) * P * PACK], BF16, "ds_second_half")
+        most, rest = slice(0, HALF - LAST_COLUMNS), slice(HALF - LAST_COLUMNS, HALF)
+
+        def late_step(index, next_view):
+            b, k = LATE[index]
+            parts = [(name, b, BLOCKS[k]) for name in ("qm", "dom")]
+            first = P * PACK * (len(LATE) - 1 - index)
+            view = late_grouped[:, first : first + 2 * P * PACK]
+            enter(grouped, parts, view, PACK)
+            on_gpsimd(runs_of_grouped(view), runs_of_planar(late[(b, k)]))
+            for cols in (most, rest):
+                on_vector(in_front[(b, k)][:, cols], next_view[:, cols])
+            for part in parts:
+                own_codes([part])
+                quantize(*part)
+            return in_front[(b, k)]
+
+        scatter(1, 0, H0, on_vector, for_vector)
+        dense = late_step(0, view)
+        views = [sums(0, 3, HALVES[h], 6 + h) for h in range(2)]
+        scatter(1, 0, H1, on_vector, dense)
         store(0)
         store(1)
-
-        copy_halves_on_scalar(0, 2, halves_of(first_sums[2]))
-        on_vector(in_front[(1, 1)][:, most], first_sums[3][:, most])
-        scatter_on_scalar(0, 2)
-        on_vector(in_front[(1, 1)][:, rest], first_sums[3][:, rest])
-        quantize_late_halves(1)
-        last_halves = [sums(1, 2, cols, name) for cols, name in zip(HALVES, ("slope_bank2", "score_bank0"))]
-        last_sums = sums(1, 3, WHOLE, "slope_bank3")
-        scatter(3, 0, on_vector, in_front[(1, 1)])
-        copy_halves_on_scalar(1, 2, last_halves)
-        for_vector = reused([P, N], F32, "for_vector")
-        on_vector(for_vector[:], last_sums)
-        scatter_on_scalar(1, 2)
+        dense = late_step(1, views[0])
+        scalar_view = sums(1, 2, WHOLE, 4)
+        scatter(0, 3, H0, on_vector, dense)
+        dense = late_step(2, views[1])
+        last_view = sums(1, 3, WHOLE, 5)
+        scatter(0, 3, H1, on_vector, dense)
+        scatter(1, 2, WHOLE, whole_on_scalar, copied(scalar_view, on_scalar, "dense1"))
         store(2)
-        scatter(3, N, on_vector, for_vector[:])
+        scatter(1, 3, WHOLE, on_vector, copied(last_view, on_vector, "for_vector"))
         store(3)

@@ -28,6 +28,8 @@ BLOCKS = tuple(slice(P * k, P * (k + 1)) for k in range(WIDTH // P))
 FORMAT = {"q": E4M3, "latent": E4M3, "do": E5M2, "qm": E4M3, "ds": E5M2, "dom": E5M2, "pw": E4M3}
 
 SHARED_GROUPS_ON_VECTOR = 40
+SLOTS_ON_VECTOR = 256
+PW_ON_SCALAR = 192
 LAST_COLUMNS = 16
 RUN = 4
 
@@ -72,12 +74,13 @@ def tile_attend_gat_sig_c_kernel(tc, qT, cT, doT, rw, qm, dom, offs, out):
             for index, name in enumerate(("qm", "dom")):
                 load(name, b, BLOCKS[k], late[(b, k)][:, :, BLOCKS[index]])
 
-        load_alone("q", 0, WHOLE, "q0")
         offsets = keep.tile([P, B * N // SLOTS_PER_COLUMN], U16, name="offsets")
-        nc.sync.dma_start(offsets[:], offs)
         planes = [reused([P, T], F32, "plane%d" % j) for j in range(PACK)]
         for j in range(PACK):
             nc.sync.dma_start(planes[j][:], cT.rearrange("(p j) c -> j p c", j=PACK)[j])
+            if j == 0:
+                nc.sync.dma_start(offsets[:], offs)
+        load_alone("q", 0, WHOLE, "q0")
         load_alone("do", 0, WHOLE, "do0")
         gate = keep.tile([P, B, PACK], F32, name="gate")
         nc.sync.dma_start(gate[:], rw.rearrange("b (p t) o -> p b (t o)", t=PACK))
@@ -85,11 +88,11 @@ def tile_attend_gat_sig_c_kernel(tc, qT, cT, doT, rw, qm, dom, offs, out):
         load_alone("dom", 0, slice(0, 3 * P), "dom0")
         load_alone("q", 1, WHOLE, "q1")
         load_alone("do", 1, WHOLE, "do1")
-        load_alone("qm", 1, HALVES[0], "q0")
-        load_alone("dom", 1, HALVES[0], "plane0")
+        load_alone("qm", 1, HALVES[0], "plane0")
+        load_alone("dom", 1, HALVES[0], "plane1")
         LATE = ((0, 3), (1, 2), (1, 3))
         for index, (b, k) in enumerate(LATE):
-            load_late(b, k, "plane%d" % (index + 1))
+            load_late(b, k, ("plane2", "plane3", "q0")[index])
 
         warm_up = keep.tile([P, 2], F32, name="warm_up")
         nc.vector.memset(warm_up[:, 0:1], 0.0)
@@ -265,18 +268,21 @@ def tile_attend_gat_sig_c_kernel(tc, qT, cT, doT, rw, qm, dom, offs, out):
         H0, H1 = HALVES
         ALL_GROUPS = slice(0, P)
 
-        new_grouped([("q", 0, WHOLE)], "q0_grouped")
-        new_codes([("q", 0, WHOLE)], "q0_codes", "q0_scales")
-        group_queries("q", 0, WHOLE, on_scalar, ALL_GROUPS)
-        quantize("q", 0, WHOLE)
         new_grouped([("latent", 0, WHOLE)], "latent0_grouped")
         held_in(0, [("latent", 1, WHOLE)], "neg_pw0")
         for j in range(PACK):
             for b in range(B):
-                gather(j, b, H0, on_vector)
-                gather(j, b, H1, on_scalar)
+                gather(j, b, slice(0, SLOTS_ON_VECTOR), on_vector)
+                gather(j, b, slice(SLOTS_ON_VECTOR, N), on_scalar)
         own_codes([("latent", 0, WHOLE)])
         quantize("latent", 0, WHOLE)
+        new_grouped([("q", 0, WHOLE)], "q0_grouped")
+        new_codes([("q", 0, WHOLE)], "q0_codes", "q0_scales")
+        group_queries("q", 0, H0, on_vector, ALL_GROUPS)
+        group_queries("q", 0, H1, on_scalar, ALL_GROUPS)
+        for cols in HALVES:
+            quantize("q", 0, cols)
+        score_banks = [first_product("q", 0, t, t) for t in range(PACK)]
 
         for h in range(2):
             new_grouped([("do", 0, HALVES[h])], "do0_grouped%d" % h)
@@ -288,10 +294,7 @@ def tile_attend_gat_sig_c_kernel(tc, qT, cT, doT, rw, qm, dom, offs, out):
             quantize("do", 0, cols)
         new_codes([("latent", 1, WHOLE)], "latent1_codes", "do0_grouped0")
         quantize("latent", 1, WHOLE)
-        score_banks = [first_product("q", 0, t, t) for t in range(PACK - 1)]
-        slope_banks = [first_product("do", 0, 0, PACK)]
-        score_banks.append(first_product("q", 0, PACK - 1, PACK - 1))
-        slope_banks = slope_banks + [first_product("do", 0, t, PACK + t) for t in range(1, PACK)]
+        slope_banks = [first_product("do", 0, t, PACK + t) for t in range(PACK)]
         sigmoids(0, score_banks, "do0")
         slopes(0, slope_banks)
 
@@ -308,7 +311,8 @@ def tile_attend_gat_sig_c_kernel(tc, qT, cT, doT, rw, qm, dom, offs, out):
         group_pw(0, H1, "scalar")
         new_grouped([("q", 1, WHOLE)], "do0")
         own_codes([("q", 1, WHOLE)])
-        group_queries("q", 1, WHOLE, on_scalar, ALL_GROUPS)
+        for cols in HALVES:
+            group_queries("q", 1, cols, on_scalar, ALL_GROUPS)
         quantize("qm", 0, H0)
         group_ds(0, H0)
         group_pw(0, H0, "vector")
@@ -322,7 +326,8 @@ def tile_attend_gat_sig_c_kernel(tc, qT, cT, doT, rw, qm, dom, offs, out):
         group_ds(0, H1)
         new_grouped([("do", 1, WHOLE)], "q0_grouped")
         new_codes([("do", 1, WHOLE)], "do1_codes", "do1_scales")
-        group_queries("do", 1, WHOLE, on_vector, ALL_GROUPS)
+        for cols in HALVES:
+            group_queries("do", 1, cols, on_vector, ALL_GROUPS)
         quantize("q", 1, WHOLE)
         quantize("do", 1, WHOLE)
         quantize("ds", 0, H1)
@@ -355,7 +360,7 @@ def tile_attend_gat_sig_c_kernel(tc, qT, cT, doT, rw, qm, dom, offs, out):
         new_grouped([("pw", 1, WHOLE)], "latent0_grouped")
         own_codes([("pw", 1, WHOLE)])
         dense = copied(sums(0, 2, WHOLE, 0), on_scalar, "prob1")
-        group_pw(1, H1, "scalar")
+        group_pw(1, slice(N - PW_ON_SCALAR, N), "scalar")
         scatter(0, 2, WHOLE, whole_on_scalar, dense)
         quantize("dom", 1, H0)
         group_ds(1, H0)
@@ -364,6 +369,7 @@ def tile_attend_gat_sig_c_kernel(tc, qT, cT, doT, rw, qm, dom, offs, out):
         quantize("pw", 1, H0)
         view = sums(1, 0, H0, 2)
         group_ds(1, H1)
+        group_pw(1, slice(HALF, N - PW_ON_SCALAR), "vector")
         for_vector = copied(view, on_vector, "for_vector")
         quantize("ds", 1, H1)
         quantize("pw", 1, H1)

@@ -29,7 +29,7 @@ FORMAT = {"q": E4M3, "latent": E4M3, "do": E5M2, "qm": E4M3, "ds": E5M2, "dom": 
 
 SHARED_GROUPS_ON_VECTOR = 40
 SLOTS_ON_VECTOR = 256
-PW_ON_SCALAR = 192
+PW_ON_SCALAR = 96
 LAST_COLUMNS = 16
 RUN = 4
 
@@ -259,11 +259,12 @@ def tile_attend_gat_sig_c_kernel(tc, qT, cT, doT, rw, qm, dom, offs, out):
         def store(k):
             nc.sync.dma_start(out[P * k : P * (k + 1), :], windows[k][:])
 
-        ones = keep.tile([P, 1], F32, name="ones")
-        nc.vector.memset(ones[:], 1.0)
+        def scatter_halves(b, k, dense):
+            for cols, part in zip(HALVES, dense):
+                scatter(b, k, cols, on_scalar, part)
 
-        def whole_on_scalar(dst, src):
-            nc.scalar.activation(dst, src, ACT.Copy, scale=ones[:])
+        def copied_halves(view):
+            return [copied(view[:, HALVES[h]], on_scalar, "dense%d" % h) for h in range(2)]
 
         H0, H1 = HALVES
         ALL_GROUPS = slice(0, P)
@@ -361,7 +362,7 @@ def tile_attend_gat_sig_c_kernel(tc, qT, cT, doT, rw, qm, dom, offs, out):
         own_codes([("pw", 1, WHOLE)])
         dense = copied(sums(0, 2, WHOLE, 0), on_scalar, "prob1")
         group_pw(1, slice(N - PW_ON_SCALAR, N), "scalar")
-        scatter(0, 2, WHOLE, whole_on_scalar, dense)
+        scatter_halves(0, 2, [dense[:, cols] for cols in HALVES])
         quantize("dom", 1, H0)
         group_ds(1, H0)
         group_pw(1, H0, "vector")
@@ -374,7 +375,7 @@ def tile_attend_gat_sig_c_kernel(tc, qT, cT, doT, rw, qm, dom, offs, out):
         quantize("ds", 1, H1)
         quantize("pw", 1, H1)
         view = sums(1, 0, H1, 3)
-        scatter(1, 1, WHOLE, whole_on_scalar, copied(sums(1, 1, WHOLE, 1), on_scalar, "dense0"))
+        scatter_halves(1, 1, copied_halves(sums(1, 1, WHOLE, 1)))
 
         late_grouped = reused([P, (len(LATE) + 1) * P * PACK], BF16, "ds_second_half")
         most, rest = slice(0, HALF - LAST_COLUMNS), slice(HALF - LAST_COLUMNS, HALF)
@@ -405,7 +406,7 @@ def tile_attend_gat_sig_c_kernel(tc, qT, cT, doT, rw, qm, dom, offs, out):
         dense = late_step(2, views[1])
         last_view = sums(1, 3, WHOLE, 5)
         scatter(0, 3, H1, on_vector, dense)
-        scatter(1, 2, WHOLE, whole_on_scalar, copied(scalar_view, on_scalar, "dense1"))
+        scatter_halves(1, 2, copied_halves(scalar_view))
         store(2)
         scatter(1, 3, WHOLE, on_vector, copied(last_view, on_vector, "for_vector"))
         store(3)

from contextlib import ExitStack

import concourse.mybir as mybir

B, N, T, D, R = 2, 512, 2048, 512, 512
FLOPS = 4 * 2 * B * N * D * R

F32 = mybir.dt.float32
BF16 = mybir.dt.bfloat16
I32 = mybir.dt.int32
U32 = mybir.dt.uint32
U16 = mybir.dt.uint16
U8 = mybir.dt.uint8
E4M3 = mybir.dt.float8_e4m3fn_x4
E5M2 = mybir.dt.float8_e5m2_x4
ACT = mybir.ActivationFunctionType
ALU = mybir.AluOpType

P = 128
PACK = 4
WIDTH = 512
HALF = WIDTH // 2
SLOTS_PER_COLUMN = 16

WHOLE = slice(0, WIDTH)
HALVES = (slice(0, HALF), slice(HALF, WIDTH))
BLOCKS = tuple(slice(P * k, P * (k + 1)) for k in range(WIDTH // P))
FORMAT = {"q": E4M3, "latent": E4M3, "do": E5M2, "qm": E4M3, "ds": E5M2, "dom": E5M2, "pw": E4M3}

SHARED_GROUPS_ON_VECTOR = 40
SLOTS_ON_VECTOR = 256
PW_ON_SCALAR = 96
LAST_COLUMNS = 16
RUN = 4


def tile_attend_gat_sig_c_kernel(tc, qT, cT, doT, rw, qm, dom, offs, out):
    nc = tc.nc

    with ExitStack() as ctx:
        keep = ctx.enter_context(tc.tile_pool(name="keep", bufs=1))
        reuse = ctx.enter_context(tc.tile_pool(name="reuse", bufs=1))
        psum = ctx.enter_context(tc.psum_pool(name="psum", bufs=1))

        def reused(shape, dtype, buffer_name):
            return reuse.tile(shape, dtype, name=buffer_name, align_bytes=64)

        def on_scalar(dst, src):
            nc.scalar.activation(dst, src, ACT.Copy)

        on_vector = nc.vector.tensor_copy

        def on_gpsimd(dst, src):
            nc.gpsimd.tensor_scalar(dst, src, 1.0, 0.0, ALU.mult, ALU.add)

        source = {"q": qT, "do": doT, "qm": qm, "dom": dom}
        planar = {}

        def load(name, b, cols, view):
            planar.setdefault((name, b), []).append((cols, view))
            nc.sync.dma_start(view, source[name][b][:, cols].rearrange("(p j) c -> p j c", j=PACK))

        def load_alone(name, b, cols, buffer_name):
            load(name, b, cols, reused([P, PACK, cols.stop - cols.start], F32, buffer_name)[:])

        late = {}
        in_front = {}

        def load_late(b, k, buffer_name):
            spare = HALF - LAST_COLUMNS
            tile = reused([P, spare + PACK * 2 * P], F32, buffer_name)
            late[(b, k)] = tile[:, spare:].rearrange("p (j c) -> p j c", j=PACK)
            in_front[(b, k)] = tile[:, :HALF]
            for index, name in enumerate(("qm", "dom")):
                load(name, b, BLOCKS[k], late[(b, k)][:, :, BLOCKS[index]])

        offsets = keep.tile([P, B * N // SLOTS_PER_COLUMN], U16, name="offsets")
        planes = [reused([P, T], F32, "plane%d" % j) for j in range(PACK)]
        for j in range(PACK):
            nc.sync.dma_start(planes[j][:], cT.rearrange("(p j) c -> j p c", j=PACK)[j])
            if j == 0:
                nc.sync.dma_start(offsets[:], offs)
        load_alone("q", 0, WHOLE, "q0")
        load_alone("do", 0, WHOLE, "do0")
        gate = keep.tile([P, B, PACK], F32, name="gate")
        nc.sync.dma_start(gate[:], rw.rearrange("b (p t) o -> p b (t o)", t=PACK))
        load_alone("qm", 0, slice(0, 3 * P), "qm0")
        load_alone("dom", 0, slice(0, 3 * P), "dom0")
        load_alone("q", 1, WHOLE, "q1")
        load_alone("do", 1, WHOLE, "do1")
        load_alone("qm", 1, HALVES[0], "plane0")
        load_alone("dom", 1, HALVES[0], "plane1")
        LATE = ((0, 3), (1, 2), (1, 3))
        for index, (b, k) in enumerate(LATE):
            load_late(b, k, ("plane2", "plane3", "q0")[index])

        warm_up = keep.tile([P, 2], F32, name="warm_up")
        nc.vector.memset(warm_up[:, 0:1], 0.0)
        nc.scalar.activation(warm_up[:, 1:2], warm_up[:, 0:1], ACT.Sigmoid)

        windows = [keep.tile([P, T], F32, name="window%d" % k) for k in range(D // P)]
        for window in windows:
            nc.vector.memset(window[:].bitcast(I32), 0)

        grouped = {}
        codes = {}
        scales = {}

        def enter(table, parts, view, per_column):
            first = 0
            for name, b, cols in parts:
                stop = first + per_column * (cols.stop - cols.start)
                table.setdefault((name, b), []).append((cols, view[:, first:stop]))
                first = stop

        def holder(table, name, b, cols):
            return [x for x in table[(name, b)] if x[0].start <= cols.start and cols.stop <= x[0].stop][0]

        def look_up(table, name, b, cols, per_column):
            held, view = holder(table, name, b, cols)
            return view[:, per_column * (cols.start - held.start) : per_column * (cols.stop - held.start)]

        def planar_view(name, b, cols):
            held, view = holder(planar, name, b, cols)
            return view[:, :, cols.start - held.start : cols.stop - held.start]

        def width_of(parts):
            return sum(cols.stop - cols.start for name, b, cols in parts)

        together = {}

        def new_codes(parts, codes_buffer, scales_buffer):
            tiles = (reused([P, width_of(parts)], U32, codes_buffer), reused([P, width_of(parts)], U8, scales_buffer))
            enter(codes, parts, tiles[0], 1)
            enter(scales, parts, tiles[1], 1)
            together[parts[0][0], parts[0][1], parts[0][2].start] = tiles

        def own_codes(parts):
            tag = "%s%d_%d" % (parts[0][0], parts[0][1], parts[0][2].start)
            new_codes(parts, tag + "_codes", tag + "_scales")

        def new_grouped(parts, buffer_name):
            tile = reused([P, width_of(parts) * PACK], BF16, buffer_name)
            enter(grouped, parts, tile, PACK)
            return tile

        def quantized(name, b, cols):
            return look_up(codes, name, b, cols, 1).bitcast(FORMAT[name]), look_up(scales, name, b, cols, 1)

        def quantize(name, b, cols):
            out_codes, out_scales = quantized(name, b, cols)
            nc.vector.quantize_mx(out=out_codes, scales=out_scales, in_=look_up(grouped, name, b, cols, PACK))

        def quantize_together(parts, grouped_view):
            name, b, cols = parts[0]
            codes_tile, scales_tile = together[name, b, cols.start]
            width = width_of(parts)
            nc.vector.quantize_mx(
                out=codes_tile[:, :width].bitcast(FORMAT[name]), scales=scales_tile[:, :width], in_=grouped_view
            )

        def list_columns(first_slot, count):
            return offsets[:, first_slot // SLOTS_PER_COLUMN : (first_slot + count) // SLOTS_PER_COLUMN]

        def gather(j, b, cols, move):
            dst = look_up(grouped, "latent", b, cols, PACK).rearrange("p (c j) -> p j c", j=PACK)[:, j, :]
            move(dst, planes[j][:].indirect(list_columns(N * b + cols.start, cols.stop - cols.start)))

        def runs_of_grouped(view):
            return view.rearrange("p (c e j) -> p c j e", e=RUN, j=PACK)

        def runs_of_planar(view):
            return view.rearrange("p j (c e) -> p c j e", e=RUN)

        def group_queries(name, b, cols, move, groups):
            dst = look_up(grouped, name, b, cols, PACK).rearrange("p (t m j) -> p m j t", m=P, j=PACK)
            src = planar_view(name, b, WHOLE).rearrange("p j (m t) -> p m j t", t=PACK)
            move(dst[:, groups], src[:, groups, :, cols.start // P : cols.stop // P])

        def group_rows(name, b, cols, move):
            move(runs_of_grouped(look_up(grouped, name, b, cols, PACK)), runs_of_planar(planar_view(name, b, cols)))

        def product(sums_view, stationary, block, moving, b, cols, start, stop):
            lhs_codes, lhs_scales = quantized(stationary, b, BLOCKS[block])
            rhs_codes, rhs_scales = quantized(moving, b, cols)
            nc.tensor.matmul_mx(
                out=sums_view,
                lhsT=lhs_codes,
                lhsT_scale=lhs_scales,
                rhs=rhs_codes,
                rhs_scale=rhs_scales,
                start=start,
                stop=stop,
            )

        def bank(number):
            return psum.tile([P, N], F32, name="bank%d" % number)

        prob = {}
        slope = {}
        neg_pw = {}

        def held_in(b, parts, buffer_name):
            row = reused([P, PACK * N], F32, buffer_name)
            neg_pw[b] = row[:].rearrange("p (t c) -> p t c", t=PACK)
            words = width_of(parts) * PACK // 2
            first = (5 * N - words) // 2
            view = row[:, first : first + words].bitcast(BF16)
            enter(grouped, parts, view, PACK)
            return view

        def first_product(name, b, t, number):
            tile = bank(number)
            product(tile[:], name, t, "latent", b, WHOLE, True, True)
            return tile

        def sigmoids(b, banks, buffer_name):
            prob[b] = reused([P, PACK, N], F32, buffer_name)
            for t in range(PACK):
                nc.scalar.activation(prob[b][:, t, :], banks[t][:], ACT.Sigmoid)

        def slopes(b, banks):
            slope[b] = reused([P, PACK, N], F32, "slope")
            for t in range(PACK):
                engine = nc.gpsimd if t else nc.vector
                engine.tensor_scalar(neg_pw[b][:, t, :], prob[b][:, t, :], gate[:, b, t : t + 1], -1.0, ALU.mult, ALU.mult)
                nc.vector.scalar_tensor_tensor(slope[b][:, t, :], prob[b][:, t, :], 1.0, banks[t][:], ALU.subtract, ALU.mult)

        def group_ds(b, cols):
            nc.vector.tensor_tensor(
                runs_of_grouped(look_up(grouped, "ds", b, cols, PACK)),
                runs_of_planar(slope[b][:, :, cols]),
                runs_of_planar(neg_pw[b][:, :, cols]),
                ALU.mult,
            )

        def group_pw(b, cols, on_engine):
            dst = runs_of_grouped(look_up(grouped, "pw", b, cols, PACK))
            src = runs_of_planar(neg_pw[b][:, :, cols])
            if on_engine == "scalar":
                nc.scalar.activation(dst, src, ACT.Copy, scale=-1.0)
            else:
                nc.vector.tensor_scalar(dst, src, -1.0, None, ALU.mult)

        def sums(b, k, cols, number):
            view = bank(number)[:, : cols.stop - cols.start]
            product(view, "qm", k, "ds", b, cols, True, False)
            product(view, "dom", k, "pw", b, cols, False, True)
            return view

        def copied(view, move, buffer_name):
            dense = reused([P, view.shape[1]], F32, buffer_name)
            move(dense[:], view)
            return dense[:]

        def scatter(b, k, cols, move, dense):
            move(windows[k][:].indirect(list_columns(N * b + cols.start, cols.stop - cols.start)), dense)

        def store(k):
            nc.sync.dma_start(out[P * k : P * (k + 1), :], windows[k][:])

        def scatter_halves(b, k, dense):
            for cols, part in zip(HALVES, dense):
                scatter(b, k, cols, on_scalar, part)

        def copied_halves(view):
            return [copied(view[:, HALVES[h]], on_scalar, "dense%d" % h) for h in range(2)]

        H0, H1 = HALVES
        ALL_GROUPS = slice(0, P)

        new_grouped([("latent", 0, WHOLE)], "latent0_grouped")
        held_in(0, [("latent", 1, WHOLE)], "neg_pw0")
        for j in range(PACK):
            for b in range(B):
                gather(j, b, slice(0, SLOTS_ON_VECTOR), on_vector)
                gather(j, b, slice(SLOTS_ON_VECTOR, N), on_scalar)
        own_codes([("latent", 0, WHOLE)])
        quantize("latent", 0, WHOLE)
        new_grouped([("q", 0, WHOLE)], "q0_grouped")
        new_codes([("q", 0, WHOLE)], "q0_codes", "q0_scales")
        group_queries("q", 0, H0, on_vector, ALL_GROUPS)
        group_queries("q", 0, H1, on_scalar, ALL_GROUPS)
        for cols in HALVES:
            quantize("q", 0, cols)
        score_banks = [first_product("q", 0, t, t) for t in range(PACK)]

        for h in range(2):
            new_grouped([("do", 0, HALVES[h])], "do0_grouped%d" % h)
        own_codes([("do", 0, WHOLE)])
        group_queries("do", 0, H0, on_vector, ALL_GROUPS)
        group_queries("do", 0, H1, on_vector, slice(0, SHARED_GROUPS_ON_VECTOR))
        group_queries("do", 0, H1, on_scalar, slice(SHARED_GROUPS_ON_VECTOR, P))
        for cols in HALVES:
            quantize("do", 0, cols)
        new_codes([("latent", 1, WHOLE)], "latent1_codes", "do0_grouped0")
        quantize("latent", 1, WHOLE)
        slope_banks = [first_product("do", 0, t, PACK + t) for t in range(PACK)]
        sigmoids(0, score_banks, "do0")
        slopes(0, slope_banks)

        new_grouped([("qm", 0, H0)], "q0_codes")
        own_codes([("qm", 0, H0)])
        with_ds = [("dom", 0, H0), ("ds", 0, H0)]
        with_ds_grouped = new_grouped(with_ds, "q0_grouped")
        own_codes([with_ds[0], ("ds", 0, WHOLE)])
        new_grouped([("pw", 0, WHOLE)], "latent0_grouped")
        own_codes([("pw", 0, WHOLE)])
        new_grouped([("ds", 0, H1)], "ds_second_half")
        group_rows("qm", 0, H0, on_scalar)
        group_rows("dom", 0, H0, on_scalar)
        group_pw(0, H1, "scalar")
        new_grouped([("q", 1, WHOLE)], "do0")
        own_codes([("q", 1, WHOLE)])
        for cols in HALVES:
            group_queries("q", 1, cols, on_scalar, ALL_GROUPS)
        quantize("qm", 0, H0)
        group_ds(0, H0)
        group_pw(0, H0, "vector")
        quantize_together(with_ds, with_ds_grouped[:])
        quantize("pw", 0, H0)
        views = [sums(0, k, H0, k) for k in range(2)]
        dense = [copied(views[k], on_scalar, "dense%d" % k) for k in range(2)]
        for k in range(2):
            scatter(0, k, H0, on_scalar, dense[k])

        group_ds(0, H1)
        new_grouped([("do", 1, WHOLE)], "q0_grouped")
        new_codes([("do", 1, WHOLE)], "do1_codes", "do1_scales")
        for cols in HALVES:
            group_queries("do", 1, cols, on_vector, ALL_GROUPS)
        quantize("q", 1, WHOLE)
        quantize("do", 1, WHOLE)
        quantize("ds", 0, H1)
        quantize("pw", 0, H1)
        score_banks = [first_product("q", 1, t, (t + 2) % PACK) for t in range(PACK)]
        slope_banks = [first_product("do", 1, t, PACK + t) for t in range(PACK)]
        sigmoids(1, score_banks, "prob1")
        views = [sums(0, k, H1, 2 + k) for k in range(2)]
        dense = [copied(views[k], on_scalar, "dense%d" % k) for k in range(2)]
        for k in range(2):
            scatter(0, k, H1, on_scalar, dense[k])

        with_qm = [("qm", 0, BLOCKS[2]), ("qm", 1, H0)]
        with_qm_grouped = held_in(1, with_qm, "do0")
        own_codes(with_qm)
        new_grouped([("dom", 0, BLOCKS[2]), ("dom", 1, H0)], "q0_grouped")
        own_codes([("dom", 0, BLOCKS[2])])
        group_rows("dom", 0, BLOCKS[2], on_vector)
        group_rows("qm", 0, BLOCKS[2], on_vector)
        group_rows("qm", 1, H0, on_vector)
        group_rows("dom", 1, H0, on_vector)
        quantize("dom", 0, BLOCKS[2])
        quantize_together(with_qm, with_qm_grouped)
        slopes(1, slope_banks)

        new_codes([("dom", 1, H0)], "dom1_codes", "do1_scales")
        new_grouped([("ds", 1, H0)], "do0_grouped1")
        new_grouped([("ds", 1, H1)], "ds_second_half")
        own_codes([("ds", 1, WHOLE)])
        new_grouped([("pw", 1, WHOLE)], "latent0_grouped")
        own_codes([("pw", 1, WHOLE)])
        dense = copied(sums(0, 2, WHOLE, 0), on_scalar, "prob1")
        group_pw(1, slice(N - PW_ON_SCALAR, N), "scalar")
        scatter_halves(0, 2, [dense[:, cols] for cols in HALVES])
        quantize("dom", 1, H0)
        group_ds(1, H0)
        group_pw(1, H0, "vector")
        quantize("ds", 1, H0)
        quantize("pw", 1, H0)
        view = sums(1, 0, H0, 2)
        group_ds(1, H1)
        group_pw(1, slice(HALF, N - PW_ON_SCALAR), "vector")
        for_vector = copied(view, on_vector, "for_vector")
        quantize("ds", 1, H1)
        quantize("pw", 1, H1)
        view = sums(1, 0, H1, 3)
        scatter_halves(1, 1, copied_halves(sums(1, 1, WHOLE, 1)))

        late_grouped = reused([P, (len(LATE) + 1) * P * PACK], BF16, "ds_second_half")
        most, rest = slice(0, HALF - LAST_COLUMNS), slice(HALF - LAST_COLUMNS, HALF)

        def late_step(index, next_view):
            b, k = LATE[index]
            parts = [(name, b, BLOCKS[k]) for name in ("qm", "dom")]
            first = P * PACK * (len(LATE) - 1 - index)
            view = late_grouped[:, first : first + 2 * P * PACK]
            enter(grouped, parts, view, PACK)
            on_gpsimd(runs_of_grouped(view), runs_of_planar(late[(b, k)]))
            for cols in (most, rest):
                on_vector(in_front[(b, k)][:, cols], next_view[:, cols])
            for part in parts:
                own_codes([part])
                quantize(*part)
            return in_front[(b, k)]

        scatter(1, 0, H0, on_vector, for_vector)
        dense = late_step(0, view)
        views = [sums(0, 3, HALVES[h], 6 + h) for h in range(2)]
        scatter(1, 0, H1, on_vector, dense)
        store(0)
        store(1)
        dense = late_step(1, views[0])
        scalar_view = sums(1, 2, WHOLE, 4)
        scatter(0, 3, H0, on_vector, dense)
        dense = late_step(2, views[1])
        last_view = sums(1, 3, WHOLE, 5)
        scatter(0, 3, H1, on_vector, dense)
        scatter_halves(1, 2, copied_halves(scalar_view))
        store(2)
        scatter(1, 3, WHOLE, on_vector, copied(last_view, on_vector, "for_vector"))
        store(3)
